import numpy as np, ml_dtypes
CORES = [66,74,82,90,194,202,210,218]
N = 8
BF = ml_dtypes.bfloat16
def gentries(a):
    return np.ascontiguousarray(a.reshape(8, 16, -1).transpose(0, 2, 1)).reshape(8, -1)
def gtable(e):
    e = np.asarray(e); return np.ascontiguousarray(e.reshape(8, -1, 16).transpose(0, 2, 1)).reshape(128, -1).astype(np.int32)
E, V, XB, K0, RO = 2048, 1024, 7, 3, 3
MASKS = [4, 1, 2]
C, TOP, OFF = 2 ** K0, 2 ** XB - 1, 64 * 2 ** XB
def cut(rng, n, m):
    return np.repeat(np.arange(len(n)), n)[:m][rng.permutation(m)]
def ring(rng, cid):
    o = np.lexsort((rng.random(E), cid)); c = cid[o]
    st = np.flatnonzero(np.concatenate([np.array([True]), c[1:] != c[:-1]])); n = np.diff(np.append(st, E))
    nx = np.arange(1, E + 1); nx[np.append(st[1:], E) - 1] = st
    s, l, p = np.empty(E, np.int64), np.empty(E, np.int64), np.empty(E, np.int64)
    s[o] = o[nx]; l[o] = np.repeat(np.minimum.reduceat(o, st), n); p[o] = np.arange(E) - np.repeat(st, n)
    return s, l, p
def rings(rng, cid):
    s, l, p = np.empty(cid.shape, np.int64), np.empty(cid.shape, np.int64), np.empty(cid.shape, np.int64)
    for q in range(N):
        for g in range(8): s[q, g], l[q, g], p[q, g] = ring(rng, cid[q, g])
    return s, l, p
def deal(rng):
    return np.stack([np.stack([cut(rng, np.append(C, rng.integers(1, C + 1, E)), E) for g in range(8)]) for q in range(N)])
def levels(rng, l):
    w = rng.random((N, 8, 16, 1)); lev = np.take_along_axis(rng.random((N, 8, 16, E)), l[:, :, None, :], 3)
    return np.minimum((2 ** XB * (w * lev + (1 - w) * rng.random((N, 8, 16, E)))).astype(np.int64), TOP)
def chains(rng):
    n = 5 * V // 16; o = np.sort(np.append(0, 1 + rng.permutation(V - 1))[:3 * n].reshape(n, 3), axis=1); d = 2 * o + rng.integers(0, 2, (n, 3)); c = np.arange(E)
    c[d[:, 0]] = d[:, 1]; c[d[:, 0] ^ 1] = d[:, 2]
    return c
def graded(rng):
    o = rng.permutation(V); n = V // 8; c = np.arange(E); x = np.zeros((16, E), np.int64)
    a, b, d = o[:n], o[n:2 * n], o[2 * n:3 * n]; c[2 * a] = 2 * d; c[2 * a + 1] = 2 * b; c[2 * b + 1] = 2 * d + 1
    y = rng.integers(2 ** (XB - 1) + 1, TOP, (16, n)); up = rng.integers(0, 2, (16, n)); up[0] = 1
    x[:, 2 * d] = y + up; x[:, 2 * b + 1] = y; x[:, 2 * a + 1] = TOP
    a, b = o[3 * n::2], o[3 * n + 1::2]; c[2 * a + 1] = 2 * b
    y = rng.integers(2 ** (XB - 1) + 1, TOP, (16, len(a))); up = rng.integers(0, 2, y.shape); up[0] = 1
    x[:, 2 * a] = y; x[:, 2 * b + 1] = y + up
    return c, x
def pack(x, s, l):
    return {"x0": np.ascontiguousarray(x.reshape(N, 128, E)).astype(np.float32).astype(BF), "su": np.stack([gtable(a) for a in s]), "lab": l.astype(np.int32)}
def setup_inputs(rng):
    s, l, p = rings(rng, deal(rng))
    return pack(levels(rng, l), s, l)
def setup_inputs_full(rng):
    cid = np.empty((N, 8, E), np.int64); n = E // C
    for q in range(N):
        for g in range(8):
            if g & 1: cid[q, g] = cut(rng, np.full(n, C), E); continue
            c = np.full(E, -1, np.int64); top = V - 1
            for t in range(RO):
                w = 2 ** (t + 1); k = np.arange(n // w); flip = rng.integers(0, 2, len(k)); e = 2 * (top - k)
                c[e + flip] = w * k + rng.integers(0, w // 2, len(k)); c[e + 1 - flip] = w * k + w // 2 + rng.integers(0, w // 2, len(k)); top -= n // w
            free = np.repeat(np.arange(n), C - np.bincount(c[c >= 0], minlength=n))
            c[c < 0] = rng.permutation(free); cid[q, g] = c
    s, l, p = rings(rng, cid); x = levels(rng, l); x[:, ::2] = rng.integers(1, TOP + 1, (1, 4, 1, 1))
    return pack(x, s, l)
def setup_inputs_ties(rng):
    cid = deal(rng)
    cid[0, 0] = cut(rng, np.full(E // C, C), E)
    cid[0, 1, 0::2] = 2 * cut(rng, rng.integers(1, C + 1, V), V); cid[0, 1, 1::2] = 2 * cut(rng, rng.integers(1, C + 1, V), V) + 1
    cid[0, 1, 0] = E; cid[0, 1, 1] = E + 1
    for q in range(N): cid[q, 4] = chains(rng)
    cid[0, 6], lev = graded(rng)
    s, l, p = rings(rng, cid)
    for a in (s, l, p): a[:, [0, 1, 6]] = a[0:1, [0, 1, 6]].copy()
    x = TOP * rng.integers(0, 2, (N, 8, 16, E))
    x[:, 0] = TOP * (p[:, 0, None, :] & 1); x[:, 1] = TOP * (1 - (np.arange(E) & 1))
    x[:, 2:4] = rng.integers(0, 2, (N, 2, 16, E)); x[:, 4:6] = rng.integers(0, TOP + 1, (N, 2, 1, 1)); x[:, 6] = lev
    return pack(x, s, l)
def setup_inputs_ends(rng):
    cid = deal(rng); e = np.arange(E)
    shut = rng.permutation(np.concatenate([np.array([0, 7]), 1 + rng.permutation(6)])[:N]); z = int(rng.choice(np.flatnonzero(shut < 7)))
    for q in range(N):
        k = rng.permutation(8); i = int(np.flatnonzero(k == 3)[0]); k[i] = k[shut[q]]; k[shut[q]] = 3
        if q == z: k = np.where(k == 3, 3, 0); k[7] = 7
        for g in range(8):
            if k[g] == 0: cid[q, g] = e
            if k[g] in (1, 2, 3, 6): cid[q, g] = np.repeat(cut(rng, rng.integers(1, C // 2 + 1, V), V), 2)
            if k[g] == 1: cid[q, g, 0] = E; cid[q, g, 1] = E + 1
            if k[g] == 2: cid[q, g, E - 2] = E; cid[q, g, E - 1] = E + 1
            if k[g] == 4: cid[q, g] = cut(rng, np.full(E // C, C), E)
            if k[g] == 5: cid[q, g] = ((e + 1) >> 1) & (V - 1)
            if k[g] == 6: cid[q, g, V:] = E + cut(rng, rng.integers(1, C + 1, V), V)
    s, l, p = rings(rng, cid)
    return pack(levels(rng, l), s, l)
def setup_inputs_spread(rng):
    cid = np.stack([np.stack([cut(rng, np.minimum(np.exp2((K0 + 1) * rng.random(E)).astype(np.int64), C), E) for g in range(8)]) for q in range(N)])
    s, l, p = rings(rng, cid)
    x = np.exp2((XB + 1) * rng.random((N, 8, 1, E))) * rng.random((N, 8, 16, E)) * (rng.random((N, 8, 1, E)) > 0.0625)
    return pack(np.minimum(x.astype(np.int64), TOP), s, l)
def check_inputs(d):
    bad = []; x = np.asarray(d["x0"]).astype(np.float32)
    if not np.all((x >= 0) & (x <= TOP) & (x == np.floor(x))): bad.append("range of x0")
    if np.min(d["su"]) < 0 or np.max(d["su"]) >= E: return bad + ["range of su"]
    s = np.stack([gentries(a) for a in d["su"]]).astype(np.int64); e = np.broadcast_to(np.arange(E), s.shape)
    if not np.array_equal(np.sort(s, axis=2), e): bad.append("su is no permutation")
    cur, low, back = e, e, np.zeros(s.shape, bool)
    for t in range(C):
        cur = np.take_along_axis(s, cur, 2); low = np.minimum(low, cur); back = back | (cur == e)
    if not np.all(back): bad.append("a circuit of su is too long")
    if not np.array_equal(low, np.asarray(d["lab"])): bad.append("lab is not the lowest edge of the circuit")
    return bad
def reference(x0, su, lab):
    x = x0.astype(np.float32).astype(np.int64).reshape(N, 8, 16, E)
    s = np.stack([gentries(a) for a in su]).astype(np.int64); l = lab.astype(np.int64); v = np.arange(V)
    for t in range(RO):
        K = K0 + t; gain = np.zeros((N, 8, V), np.int64)
        for y in (x, x[np.arange(N) ^ MASKS[t]]):
            o = np.take_along_axis(y, s[:, :, None, :], 3)
            i0, i1, o0, o1 = y[..., 0::2], y[..., 1::2], o[..., 0::2], o[..., 1::2]
            gain = gain + np.add.reduce(np.abs(i0 - o0) + np.abs(i1 - o1) - np.abs(i0 - o1) - np.abs(i1 - o0), axis=2)
        l0, l1 = l[..., 0::2], l[..., 1::2]
        key = np.where(l0 != l1, V * (gain + OFF) + v, 0)
        b, a, j = np.repeat(key, 2, axis=2), x, s
        for k in range(K):
            a = a + np.take_along_axis(a, j[:, :, None, :], 3)
            b = np.maximum(b, np.take_along_axis(b, j, 2))
            j = np.take_along_axis(j, j, 2)
        merge = (key > 0) & (b[..., 0::2] == key) & (b[..., 1::2] == key)
        s0, s1 = s[..., 0::2], s[..., 1::2]
        s = np.stack([np.where(merge, s1, s0), np.where(merge, s0, s1)], axis=3).reshape(N, 8, E)
        low = np.where(merge, np.minimum(l0, l1), E)
        l = np.where(b > 0, np.minimum(l, np.take_along_axis(low, b & (V - 1), 2)), l)
        x = a >> K
    return {"ysu": s.astype(np.float32), "ylab": l.astype(np.float32), "yx": x.reshape(N, 128, E).astype(np.float32).astype(BF)}

@@ -1,0 +1,537 @@
+from concourse.mybir import AluOpType, ActivationFunctionType
+
+F, B16, I32, U16 = "float32", "bfloat16", "int32", "uint16"
+SCRATCH = {}
+for _names, _shape, _dt in [
+        ("xa xb xc pa pb pc xq xo xd jt j0 j1 lg ob sel", [128, 2048], B16), ("a0 a1 b0 b1 kw ac bc", [128, 2048], F), ("lw", [128, 1040], B16),
+        ("mv ab", [128, 4096], B16), ("vc", [128, 1024], B16), ("big idb idn rp rn vw lh", [128, 128], B16), ("sui labi", [128, 128], I32),
+        ("suf one idf nat lv", [128, 128], F), ("io1", [128, 144], F), ("io5 neg vcon cv nd mc mm", [128, 64], F), ("kc", [128, 8], I32),
+        ("col selb", [128, 16], F), ("prm", [128, 512], F), ("zz", [128, 144], B16), ("rd", [128, 192], F), ("selh", [128, 8], B16),
+        ("ti", [128, 1024], I32), ("tf", [128, 1024], F), ("sb", [128, 3, 2, 64], F), ("sd st", [128, 3, 64], F),
+        ("hl", [128, 2, 2, 64], B16), ("hd ht", [128, 2, 64], B16), ("lnat ll", [128, 128], U16), ("lu0 lu1 lu2", [128, 384], U16),
+        ("jl", [128, 512], U16), ("eq", [128, 64], B16), ("tp tm osu olb ol0", [128, 256], F)]:
+    for _n in _names.split():
+        SCRATCH[_n] = ("sbuf", _shape, _dt)
+for _n, _c in [("pk0", 512), ("pk1", 512), ("pda", 1024), ("pdb", 1024), ("pj", 512), ("pt", 512)]:
+    SCRATCH[_n] = ("psum", [128, _c], F)
+SEMAPHORES = ["nv", "ns", "nt", "ng", "sent", "arr0", "arr1", "arr2"] + ["d%d" % k for k in range(90)]
+
+MASKS = [4, 1, 2]
+GR = 1.56
+CY = 0.83e-3
+PC = 0.42e-3
+PSUM = ("pk0", "pk1", "pda", "pdb", "pj", "pt")
+OPT = {"u": ["svss", "ssss", "svss"]}
+CODE = ("0806000U07010302040;090:0<0V0T10190B12131411180W16171:1;1<052227211=1?1V1>1@1A1B1C1N2823241H1D1E1I1F1G1K1M1J1L1O3<2;3:2A2<3=3>3?3F"
+        "2?1U2=3@253A2>262@3G2B292:3I383H1S3J0>0D0?0=0A0M0F0J0C0H0G3;2C2D2F2E2N2G2J2H2I2P2K2O2T3D393E3B3K3M3C0@0E0L1T3L1W1P2Q152U3Q3N0P0I3R"
+        "0N0R0O3O2L2M2R2S2V2W30313335323436374W3T3V463U3W4247434041484<494450511Q53523P3S54554:454;4=575856594>1R5:5;5=5>5<5?5@5A5H5B5G5C5I"
+        "5D5J5K5L5T4@4B4K4A4L4C4G4?4D4H4M4N4Q4E4F4I4J4U5F5E604R614O4P4S4T4V5O5V5U6266636:5W670K645Q5N5P65686=6;6<6>5R5S696D6@6A6?7U6B6G6E6F"
+        "6H6C7S6I6J6K6L7V7T7W806O6P0Q816N836S6Q82840S7476787:5M6R706T6U716V6W857572737787888689796M8:208;8=8<8>8?8@8L8B8A8G8C8H8D8I8J8K8U8W"
+        "8E8F7<7=7>7H7G7?7@7C7;7I7D7J7M7A917N7B7K7E7F7Q7L928M7O7P7R8N8V93978P948O8S8Q9;9095968R99:79>9<9=9?9E8T:9:89@:;9F9G9H9O9I:::=9:98:<"
+        "9C:?:>9J:A9R:@9A9P9Q9S:C:B:D9T:G:H:E:F9D9B9K9L9M9U9N:I:J:K:L9V:N:M:S;3:O:T:P:V:Q:U;0:W;1;4;6;5:R;7;8;;;9;<;:;=;H;>9W:4:1:0;2:2:5;K"
+        ";?;F;D;B;@;A;C;G;E:6:3;I;J;L;M;N;U;Q;S;R;T;V;P;O")
+ORDER = [(ord(CODE[i]) - 48) * 40 + ord(CODE[i + 1]) - 48 for i in range(0, len(CODE), 2)]
+
+
+def build(g, core, T, topo, rank):
+    A, AF = AluOpType, ActivationFunctionType
+    ops = []
+    tag = ["I"]
+
+    def add(eng, fn, r, w, t, kind="c", lat=0.0):
+        ops.append({"e": eng, "f": fn, "r": list(r), "w": list(w), "t": t, "k": kind, "lat": lat, "g": tag[0]})
+
+    def vt(n, c=1.0):
+        return 0.05 + max(64, n * c) * CY
+
+    def ts(out, in0, s1, s2, o0, o1, r, w, n, c=1.0):
+        if o1 is None:
+            add("v", lambda: g.vector.tensor_scalar(out, in0, s1, None, o0), r, w, vt(n, c))
+        else:
+            add("v", lambda: g.vector.tensor_scalar(out, in0, s1, s2, o0, o1), r, w, vt(n, c))
+
+    def tt(out, in0, in1, o, r, w, n, c=2.0):
+        add("v", lambda: g.vector.tensor_tensor(out, in0, in1, o), r, w, vt(n, c))
+
+    def cp(out, in_, r, w, n, c=1.0):
+        add("v", lambda: g.vector.tensor_copy(out, in_), r, w, vt(n, c))
+
+    def ms(out, val, w, n, c=1.0):
+        add("v", lambda: g.vector.memset(out, val), [], w, vt(n, c))
+
+    def act(out, in_, fn, r, w, n, c=1.0, bias=0.0, scale=1.0):
+        add("s", lambda: g.scalar.activation(out, in_, fn, bias=bias, scale=scale), r, w, 0.065 + max(64, n * c) * CY)
+
+    def mms(lst, r, w, cyc):
+        def fn():
+            for a in lst:
+                ins = g.tensor.matmul(*a)
+            return ins
+        add("p", fn, r, w, 0.05 + cyc * PC)
+
+    def dma(q, out, in_, r, w, lat=2.0):
+        add(q, lambda: (g.sync if q == "y" else g.scalar).dma_start(out, in_), r, w, 0.06, "d", lat)
+
+    def iota(out, pat, base, cm, w, n, flt=True, r=()):
+        if flt:
+            add("g", lambda: g.iota(out, pat, base, cm, allow_small_or_imprecise_dtypes=True), r, w, 0.13 + 2 * n * CY)
+        else:
+            add("g", lambda: g.iota(out, pat, base, cm), r, w, 0.13 + 2 * n * CY)
+
+    def fill(out, val, w, n, r=()):
+        iota(out, [[0, n]], val, 0, w, n, True, r)
+
+    def pick(out, in_, pat, base, cm, r, w, n):
+        add("g", lambda: g.affine_select(out, in_, pat, A.is_equal, 0.0, base, cm), r, w, 0.17 + 2 * n * CY)
+
+    def send(t, src, dst, h, r):
+        peer = T.cores[rank ^ MASKS[t]]
+        rid, pid = topo.addr(peer, core)
+        m = topo.mask(core, peer)
+        add("g", lambda: g.remote_dma(dst[:, H(h)], src[:, H(h)], T.sem["arr%d" % t], T.sem.sent, pid, rid, m), r, [("snd", t, h)], 0.3, "r", 6.0)
+        ops[-1]["n"] = len(topo.engines(core, peer))
+        ops[-1]["nb"] = len(topo.engines(peer, core))
+
+    def H(h):
+        return slice(1024 * h, 1024 * h + 1024)
+
+    def hk(name):
+        return [(name, 0), (name, 1)]
+
+    col = T.col
+    C15, CN15, CZ, CW, CE2, CHL, CB0, CB1 = [col[:, k:k + 1] for k in range(8)]
+    X = [T.xa, T.xb, T.xc]
+    XP = [T.pa, T.pb, T.pc]
+    LU = [T.lu0, T.lu1, T.lu2]
+    PK = [T.pk0, T.pk1]
+    AB = [T.a0, T.a1]
+
+    dma("y", T.sui[:], T.su[:], [], ["sui"])
+    dma("s", T.xa[:, H(1)], T.x0[:, H(1)], [], [("x0", 1)], 2.8)
+    dma("y", T.xa[:, H(0)], T.x0[:, H(0)], [], [("x0", 0)], 2.8)
+    for h in range(2):
+        dma("y", T.xd[:, H(h)], T.x0[:, H(h)], [], [("xd", h)], 2.8)
+    dma("s", T.labi[:], T.lab[:], [], ["labi"])
+    iota(T.kc[:, 0:1], [[1, 1]], 0, 1, ["kc0"], 1, False)
+    iota(T.io1[:], [[1, 144]], 0, -1, ["io1"], 144)
+    ms(T.one[:], 1.0, ["one"], 128)
+    for k in range(4):
+        pick(T.prm[:, 128 * k:128 * k + 128], T.one[:], [[16, 8], [1000, 2], [2, 8]], k // 2 - 1000 * (k % 2), -1, ["one"], [("prm", k)], 128)
+    send(0, T.xa, T.pa, 0, [("x0", 0)])
+    send(0, T.xa, T.pa, 1, [("x0", 1)])
+    iota(T.vc[0:32, :], [[1, 32], [0, 32]], 0, 0, ["vc0"], 1024)
+    iota(T.vc[32:64, :], [[0, 32], [1, 32]], 0, 0, ["vc1"], 1024)
+    fill(T.sel[:], 0, ["sel"], 2048)
+    ms(T.big[:], -float(2 ** 25), ["big"], 128, 0.5)
+    pick(T.sel[:, 0:2048:16], T.big[:], [[-1, 16], [-16, 8]], 0, 1, ["big"], ["sel"], 128)
+    fill(T.vw[0:64, :], 0, ["vw"], 128)
+    fill(T.vw[0:1, 0:128:16], 32, ["vw0"], 8, ["vw"])
+    fill(T.vw[0:1, 8:128:16], -64, ["vw1"], 8, ["vw"])
+    fill(T.vw[32:33, 0:128:16], 1, ["vw2"], 8, ["vw"])
+    fill(T.vw[32:33, 8:128:16], -2, ["vw3"], 8, ["vw"])
+    fill(T.bc[:], 0, hk("bc"), 2048)
+    pick(T.selb[:], T.one[:, 0:16], [[8, 2], [16, 8]], 0, -1, ["one"], ["selb"], 16)
+    pick(T.idf[:], T.one[:], [[1, 128]], 0, -1, ["one"], ["idf"], 128)
+    pick(T.rd[:, 64:192], T.one[:], [[1, 128]], 0, -1, ["one"], ["rd1"], 128)
+    fill(T.neg[:], -1, ["neg"], 64)
+    pick(T.rd[0:64, 0:64], T.one[0:64, 0:64], [[1, 64]], 0, -1, ["one"], ["rd0"], 64)
+    pick(T.rd[64:128, 0:64], T.neg[64:128, :], [[1, 64]], 0, -1, ["neg"], ["rd2"], 64)
+    iota(T.io5[:], [[16, 64]], 0, 0, ["io5"], 64)
+    fill(T.lw[:], 0, ["lw0", "lw1", "lw2"], 1040)
+    fill(T.lg[0:8, 0:1040], 32, hk("lg"), 1040)
+    dma("y", T.lw[2:128:16, :], T.lg[0:8, 0:1040], hk("lg"), ["lw2"])
+    ms(T.jt[:], 0.0, ["jt0", "jt1"], 2048, 0.5)
+    ts(T.kc[:, 4:5], T.kc[:, 0:1], 15, None, A.bitwise_and, None, ["kc0"], ["kc4"], 1)
+    cp(C15, T.kc[:, 4:5], ["kc4"], ["c15"], 1)
+    ts(T.idb[:], T.io1[:, 0:128], 0.0, None, A.is_equal, None, ["io1", "jt0"], ["idb"], 128)
+    ts(T.idn[:], T.io1[:, 0:128], 0.0, -1.0, A.is_equal, A.mult, ["io1"], ["idn"], 128)
+    act(CN15, C15, AF.Copy, ["c15"], ["cn15"], 1, scale=-1.0)
+    act(CZ, C15, AF.Copy, ["c15"], ["cz"], 1, scale=-1.0, bias=15.0)
+    act(CW, C15, AF.Copy, ["c15"], ["cw"], 1, scale=-63.0, bias=64.0)
+    act(CB0, C15, AF.Copy, ["c15"], ["cb0"], 1, scale=-(2 ** 23 - 2048) / 8, bias=float(2 ** 23))
+    act(CB1, C15, AF.Copy, ["c15"], ["cb1"], 1, scale=-(2 ** 23 - 2047) / 8, bias=float(2 ** 23))
+    ts(T.rp[:], T.io1[:, 0:128], CN15, 2048.0, A.is_equal, A.mult, ["io1", "cn15"], ["rp"], 128)
+    act(T.rn[:], T.rp[:], AF.Copy, ["rp"], ["rn"], 128, scale=-1.0)
+    ts(T.zz[:], T.io1[:], CZ, CW, A.is_equal, A.mult, ["io1", "cz", "cw"], ["zz"], 144)
+
+    cp(T.suf[:], T.sui[:], ["sui"], ["suf"], 128)
+    for h in range(2):
+        mms([(T.pj[:, 64 * h:64 * h + 64], T.prm[:, 128 * (2 * h + b):128 * (2 * h + b) + 128], T.suf[:, b:128:2], b == 0, b == 1) for b in range(2)],
+            ["suf", ("prm", 2 * h), ("prm", 2 * h + 1)], ["pj"], 512)
+    ti, tf = T.ti, T.tf
+
+    def I(k, n=128):
+        return ti[:, 128 * k:128 * k + n]
+
+    def Fq(k, n=128):
+        return tf[:, 128 * k:128 * k + n]
+
+    cp(T.lnat[:], T.pj[:, 0:128], ["pj"], ["lnat"], 128)
+    cp(I(0), T.pj[:, 0:128], ["pj"], ["i0"], 128)
+    act(T.nat[:], T.pj[:, 0:128], AF.Copy, ["pj"], ["nat"], 128)
+    ts(I(1), I(0), 1, None, A.bitwise_and, None, ["i0"], ["i1"], 128)
+    ts(I(2), I(0), 1, None, A.arith_shift_right, None, ["i0"], ["i2"], 128)
+    ts(I(4), I(0), 1, 63, A.arith_shift_right, A.bitwise_and, ["i0"], ["i4"], 128)
+    ts(Fq(0), I(1), 1024.0, None, A.mult, None, ["i1"], ["f0"], 128)
+    cp(T.hl[:, 1], I(4), ["i4"], ["hl1"], 128)
+    tt(I(3), Fq(0), I(2), A.add, ["f0", "i2"], ["i3"], 128)
+    ts(I(5), I(3), 6, None, A.arith_shift_right, None, ["i3"], ["i5"], 128)
+    cp(T.hl[:, 0], I(5), ["i5"], ["hl0"], 128)
+
+    def rows_of_su():
+        dma("y", T.jt[0:128:16, :], T.hl[:, 0], ["hl0"], ["jt0"])
+        dma("y", T.jt[1:128:16, :], T.hl[:, 1], ["hl1"], ["jt1"])
+
+    rows_of_su()
+    ts(I(6), I(3), 15, None, A.bitwise_and, None, ["i3"], ["i6"], 128)
+    ts(I(7), I(3), 4, None, A.arith_shift_right, None, ["i3"], ["i7"], 128)
+    ts(Fq(1), I(6), 128.0, None, A.mult, None, ["i6"], ["f1"], 128)
+    tt(T.sb[:, 1], Fq(1), I(7), A.add, ["f1", "i7"], ["sb1"], 128)
+    cp(T.sb[:, 0], I(3), ["i3"], ["sb0"], 128)
+    cp(T.sb[:, 2], I(2), ["i2"], ["sb2"], 128)
+    cp(T.lu0[:], T.sb[:], ["sb0", "sb1", "sb2"], ["lu0"], 384)
+    tt(T.eq[:], T.labi[:, 0:128:2], T.labi[:, 1:128:2], A.is_equal, ["labi"], ["eq"], 64)
+    ts(T.vcon[:], T.io5[:], C15, None, A.add, None, ["io5", "c15"], ["vcon"], 64)
+    ts(T.cv[:], T.vcon[:], 0.0, None, A.is_equal, None, ["vcon"], ["cv"], 64)
+    tt(T.sd[:], T.sb[:, :, 1, :], T.sb[:, :, 0, :], A.subtract, ["sb0", "sb1", "sb2"], ["sd"], 192)
+    tt(T.hd[:], T.hl[:, :, 1, :], T.hl[:, :, 0, :], A.subtract, ["hl0", "hl1"], ["hd"], 128)
+    tt(T.nd[:], T.nat[:, 64:128], T.nat[:, 0:64], A.subtract, ["nat"], ["nd"], 64)
+    ts(CE2, C15, 2.0, 2.0, A.is_equal, A.mult, ["c15"], ["ce2"], 1)
+    ts(CHL, CW, -1.0, CE2, A.mult, A.add, ["cw", "ce2"], ["chl"], 1)
+    ts(T.selh[:], T.io1[:, 0:128:16], CN15, CHL, A.is_equal, A.mult, ["io1", "cn15", "chl"], ["selh"], 8)
+
+    ring = {"v": 0, "s": 0}
+    started = [False, False]
+
+    def own(x, t, h, a, n):
+        return x[:, 2 * a + h:2 * (a + n):2] if t == 0 else x[:, 1024 * h + a:1024 * h + a + n]
+
+    def reduce_into(b, w, src, r):
+        mms([(PK[b][:], w[:], src, not started[b], False)], r + ["rp", "rn"], ["pk%d" % b], 512)
+        started[b] = True
+
+    def gain_unit(t, s, b, eng):
+        tag[0] = "U%d%s%d" % (t, s, b)
+        x = X[t] if s == "o" else XP[t]
+        lst, lk = (T.lnat, "lnat") if t == 0 else (T.lu0, "lu0")
+        off = [lst[:, 64 * h + 32 * b:64 * h + 32 * b + 32] for h in range(2)]
+        xk = hk("x%d" % t) if s == "o" else [("xp", t)]
+        q = ring[eng]
+        ring[eng] = 1 - q
+        if eng == "v":
+            for n, (hi, ho) in enumerate([(0, 0), (0, 1), (1, 1), (1, 0)]):
+                m = T.mv[:, 2048 * q + 512 * n:2048 * q + 512 * n + 512]
+                tt(m, x[:, 0:2048].indirect(off[ho]), own(T.xd, t, hi, 512 * b, 512), A.max, xk + hk("xd") + [lk], [("mv", q, n)], 512, GR)
+                reduce_into(b, T.rp if hi == ho else T.rn, m, [("mv", q, n)])
+            return
+        for ho in range(2):
+            o = T.ob[:, 1024 * q + 512 * ho:1024 * q + 512 * ho + 512]
+            act(o, x[:, 0:2048].indirect(off[ho]), AF.Copy, xk + [lk], [("ob", q, ho)], 512, GR)
+        for ho in range(2):
+            o = T.ob[:, 1024 * q + 512 * ho:1024 * q + 512 * ho + 512]
+            pd, pn = (T.pda, "pda") if ho == 0 else (T.pdb, "pdb")
+            lst2 = []
+            for hi in range(2):
+                d = pd[:, 512 * hi:512 * hi + 512]
+                lst2 += [(d, T.idb[:], own(x, t, hi, 512 * b, 512), True, False), (d, T.idn[:], o, False, True)]
+            mms(lst2, xk + [("ob", q, ho), "idb", "idn"], [pn], 2048)
+            a0 = 2048 * q + 1024 * ho
+            act(T.ab[:, a0:a0 + 1024], pd[:], AF.Abs, [pn], [("ab", q, ho)], 1024, scale=0.5)
+            for hi in range(2):
+                reduce_into(b, T.rp if hi == ho else T.rn, T.ab[:, a0 + 512 * hi:a0 + 512 * hi + 512], [("ab", q, ho)])
+
+    def gains(t):
+        for n, (s, b) in enumerate([("o", 0), ("o", 1), ("p", 0), ("p", 1)]):
+            if n == 2:
+                add("a", None, [("snd", t, 0), ("snd", t, 1)], [("xp", t)], 0.0, "a")
+                ops[-1]["sem"] = "arr%d" % t
+            gain_unit(t, s, b, OPT["u"][t][n])
+        for b in range(2):
+            mms([(PK[b][:], T.vw[0:64, :], T.vc[0:64, 512 * b:512 * b + 512], False, False)],
+                ["vw", "vw0", "vw1", "vw2", "vw3", "vc0", "vc1"], ["pk%d" % b], 512)
+
+    def key(t):
+        tag[0] = "K%d" % t
+        for b in range(2):
+            if t == 0:
+                lst = [(PK[b][:, 64 * a:64 * a + 64], T.sel[:, 128 * (8 * b + a):128 * (8 * b + a) + 128], T.eq[:], False, a == 7) for a in range(8)]
+            else:
+                lst = [(PK[b][:, i:512:16], T.sel[:, 128 * i:128 * i + 128], T.eq[:, 32 * b:32 * b + 32], False, i == 15) for i in range(16)]
+            mms(lst, ["sel", "eq"], ["pk%d" % b], 64 * len(lst))
+            started[b] = False
+        act(T.kw[:, 0:512], T.pk0[:], AF.Identity, ["pk0", "cb0"], [("kw", 0)], 512, bias=CB0)
+        ts(T.kw[:, 512:1024], T.pk1[:], CB0, None, A.add, None, ["pk1", "cb0"], [("kw", 1)], 512)
+        act(T.kw[:, 1536:2048], T.pk1[:], AF.Identity, ["pk1", "cb1"], [("kw", 3)], 512, bias=CB1)
+        ts(T.kw[:, 1024:1536], T.pk0[:], CB1, None, A.add, None, ["pk0", "cb1"], [("kw", 2)], 512)
+        for h in range(2 if t == 2 else 0):
+            rows(T.kw[0:128:8, H(h)], [("kw", 2 * h), ("kw", 2 * h + 1)], h)
+
+    def rows(src, r, h):
+        dma("y", T.bc[0:128:8, H(h)], src, r, [("bc", h)])
+
+    def jlist(k, h):
+        return T.jl[:, 128 * (k - 1) + 64 * h:128 * (k - 1) + 64 * h + 64]
+
+    def jstep(t, k):
+        tag[0] = "J%d%d" % (t, k)
+        out, on = ([T.j0, T.j1][k % 2], "j%d" % (k % 2))
+        for h in range(2):
+            if k == 1:
+                act(out[:, H(h)], T.jt[:, 0:2048].indirect(LU[t][:, 128 + 64 * h:192 + 64 * h]), AF.Copy, ["jt0", "jt1", "lu%d" % t], [(on, h)], 1024, GR)
+            else:
+                win = [T.j0, T.j1][(k - 1) % 2]
+                act(out[:, H(h)], win[:, 0:2048].indirect(jlist(k - 1, h)), AF.Copy, hk("j%d" % ((k - 1) % 2)) + [("jl", k - 1, h)], [(on, h)], 1024, GR)
+            mms([(T.pj[:, 64 * h:64 * h + 64], T.zz[:, 15 - i:143 - i], out[:, 1024 * h + i:1024 * h + 1024:16], i == 0, i == 15) for i in range(16)],
+                [(on, h), "zz"], ["pj"], 1024)
+            cp(jlist(k, h), T.pj[:, 64 * h:64 * h + 64], ["pj"], [("jl", k, h)], 64)
+
+    def astep(t, k):
+        tag[0] = "A%d%d" % (t, k)
+        out, on = (AB[k % 2], "a%d" % (k % 2))
+        win, wk = (AB[(k - 1) % 2], hk("a%d" % ((k - 1) % 2)))
+        for h in range(2):
+            if k == 1:
+                off, lk = (T.lnat[:, 64 * h:64 * h + 64], "lnat") if t == 0 else (LU[t][:, 64 * h:64 * h + 64], "lu%d" % t)
+                tt(out[:, H(h)], X[t][:, 0:2048].indirect(off), own(T.xd, t, h, 0, 1024), A.add, hk("x%d" % t) + hk("xd") + [lk], [(on, h)], 1024, GR)
+            else:
+                tt(out[:, H(h)], win[:, 0:2048].indirect(jlist(k - 1, h)), T.ac[:, H(h)], A.add, wk + [("ac", h), ("jl", k - 1, h)], [(on, h)], 1024, GR)
+            if k < 3 + t:
+                pick(T.ac[:, H(h)], out[:, H(h)], [[0, 1024]], 0, 0, [(on, h)], [("ac", h)], 1024)
+
+    def quant(t):
+        tag[0] = "Q%d" % t
+        K = 3 + t
+        src = AB[K % 2]
+        bias = (129.0 if t == 0 else 0.0) - 0.5 + 2.0 ** (-K - 1)
+        dst = X[t + 1] if t < 2 else T.xq
+        for h in range(2):
+            act(dst[:, H(h)], src[:, H(h)], AF.Copy, [("a%d" % (K % 2), h)], [("x%d" % (t + 1), h)], 1024, bias=bias, scale=2.0 ** -K)
+            if t < 2:
+                send(t + 1, dst, XP[t + 1], h, [("x%d" % (t + 1), h)])
+                dma("y", T.xd[:, H(h)], dst[:, H(h)], [("x%d" % (t + 1), h)], [("xd", h)], 2.6)
+
+    def to_columns(src, r, nb):
+        mms([(T.pt[:, i:16 * nb:16], src[:, i:2048:16], T.selb[:, 0:nb], True, True) for i in range(16)], r + ["selb"], ["pt"], 4096)
+
+    def bstep(t, k):
+        tag[0] = "B%d%d" % (t, k)
+        K = 3 + t
+        out, on = ([T.b0, T.b1][k % 2], "b%d" % (k % 2))
+        win, wn = ([T.b0, T.b1][(k - 1) % 2], "b%d" % ((k - 1) % 2))
+        nb = 16 if t == 2 else 8
+        kk = [("kw", q) for q in range(4)]
+        for h in range(2):
+            if k == 1 and t < 2:
+                tt(out[:, H(h)], T.kw[:, 0:1024].indirect(LU[t][:, 256 + 64 * h:320 + 64 * h]), T.kw[:, H(1)], A.max, kk + ["lu%d" % t], [(on, h)], 1024, GR)
+            elif k == 1:
+                tt(out[:, H(h)], T.kw[:, 0:2048].indirect(LU[t][:, 64 * h:64 * h + 64]), T.bc[:, H(h)], A.max, kk + [("bc", h), "lu%d" % t], [(on, h)], 1024, GR)
+            elif k < K:
+                tt(out[:, H(h)], win[:, 0:2048].indirect(jlist(k - 1, h)), T.bc[:, H(h)], A.max, hk(wn) + [("bc", h), ("jl", k - 1, h)], [(on, h)], 1024, GR)
+            else:
+                act(out[:, H(h)], win[:, 0:2048].indirect(jlist(k - 1, h)), AF.Copy, hk(wn) + [("jl", k - 1, h)], [(on, h)], 1024, GR)
+            if k < K - 1:
+                rows(out[0:128:8, H(h)], [(on, h)], h)
+        if k == K - 1:
+            to_columns(out, hk(on), nb)
+            act(T.tp[:, 0:16 * nb], T.pt[:, 0:16 * nb], AF.Copy, ["pt"], ["tp"], 16 * nb)
+        if k == K:
+            to_columns(out, hk(on), nb)
+            tt(T.tm[:, 0:16 * nb], T.pt[:, 0:16 * nb], T.tp[:, 0:16 * nb], A.max, ["pt", "tp"], ["tm"], 16 * nb, 1.0)
+
+    def merge(t):
+        tag[0] = "M%d" % t
+        n = 128 if t < 2 else 192
+        mms([(T.pj[:, 0:n], T.tm[:, 0:128], T.rd[:, 0:n], True, True)], ["tm", "rd0", "rd1", "rd2"], ["pj"], 4 * n)
+        if t == 2:
+            mms([(T.pk1[:, 0:128], T.tm[:, 128:256], T.idf[:], True, True)], ["tm", "idf"], ["pk1"], 512)
+        ts(T.eq[:], T.pj[:, 0:64], 0.0, None, A.is_equal, None, ["pj"], ["eq"], 64)
+        tt(I(0, 64), T.pj[:, 64:128], T.cv[:], A.max, ["pj", "cv"], ["i0"], 64, 1.0)
+        ts(I(1, 64), I(0, 64), 1023, None, A.bitwise_and, None, ["i0"], ["i1"], 64)
+        tt(Fq(0, 64), I(1, 64), T.vcon[:], A.is_equal, ["i1", "vcon"], ["f0"], 64)
+        tt(T.mm[:], Fq(0, 64), T.eq[:], A.mult, ["f0", "eq"], ["mm"], 64)
+        if t < 2:
+            nr = 3 - t
+            for q in range(2):
+                tt(T.ht[:, q], T.hd[:, q], T.mm[:], A.mult, ["hd", "mm"], [("ht", q)], 64)
+            tt(T.hl[:, :, 0, :], T.hl[:, :, 0, :], T.ht[:], A.add, hk("ht"), ["hl0", "hl1"], 128)
+            tt(T.hl[:, :, 1, :], T.hl[:, :, 1, :], T.ht[:], A.subtract, hk("ht"), ["hl0", "hl1"], 128)
+            rows_of_su()
+            for q in range(nr):
+                tt(T.st[:, q], T.sd[:, q], T.mm[:], A.mult, ["sd", "mm"], [("st", q)], 64)
+            sk = [("st", q) for q in range(nr)]
+            tt(T.sb[:, 0:nr, 0, :], T.sb[:, 0:nr, 0, :], T.st[:, 0:nr], A.add, sk, ["sb0"], 64 * nr)
+            tt(T.sb[:, 0:nr, 1, :], T.sb[:, 0:nr, 1, :], T.st[:, 0:nr], A.subtract, sk, ["sb1"], 64 * nr)
+            cp(LU[t + 1][:, 0:128 * nr], T.sb[:, 0:nr], ["sb0", "sb1", "sb2"], ["lu%d" % (t + 1)], 128 * nr)
+        if t == 0:
+            act(T.mc[:], T.mm[:], AF.Copy, ["mm"], ["mc"], 64)
+        else:
+            tt(T.mc[:], T.mc[:], T.mm[:], A.max, ["mm"], ["mc"], 64)
+
+    def turn_out(ps, pn, src, r):
+        mms([(ps[0:64, h:256:2], src[:, 64 * h:64 * h + 64], T.idf[:], True, True) for h in range(2)], r + ["idf"], [pn], 1024)
+
+    def store8(y, src, r, name):
+        for q in range(8):
+            dma("y" if q % 2 == 0 else "s", y[q], src[0:64, 32 * q:32 * q + 32], r, [(name, q)])
+
+    def finish():
+        tag[0] = "F"
+        cp(T.lv[:], T.pk1[:, 0:128], ["pk1"], ["lv"], 128)
+        tt(I(2, 64), T.lv[:, 0:64], T.lv[:, 64:128], A.max, ["lv"], ["i2"], 64)
+        ts(I(3, 64), I(2, 64), 6, None, A.arith_shift_right, None, ["i2"], ["i3"], 64)
+        ts(I(4, 64), I(2, 64), 63, None, A.bitwise_and, None, ["i2"], ["i4"], 64)
+        tt(T.lh[:, 0:64], I(3, 64), T.mm[:], A.mult, ["i3", "mm"], ["lh0"], 64)
+        tt(T.lh[:, 64:128], I(4, 64), T.mm[:], A.mult, ["i4", "mm"], ["lh1"], 64)
+        dma("y", T.lw[0:128:16, 0:1024], T.lh[:, 0:64], ["lh0"], ["lw0"])
+        dma("s", T.lw[1:128:16, 0:1024], T.lh[:, 64:128], ["lh1"], ["lw1"])
+        ts(I(5), T.pj[:, 64:192], 0.0, None, A.max, None, ["pj"], ["i5"], 128)
+        ts(I(6), I(5), 15, None, A.bitwise_and, None, ["i5"], ["i6"], 128)
+        ts(I(7), I(5), 4, 63, A.arith_shift_right, A.bitwise_and, ["i5"], ["i7"], 128)
+        ts(Fq(1), I(5), 0.0, 1024.0, A.is_equal, A.mult, ["i5"], ["f1"], 128)
+        ts(Fq(2), I(6), 64.0, None, A.mult, None, ["i6"], ["f2"], 128)
+        tt(Fq(3), Fq(1), I(7), A.add, ["f1", "i7"], ["f3"], 128)
+        tt(Fq(4), Fq(2), Fq(3), A.add, ["f2", "f3"], ["f4"], 128)
+        cp(T.ll[:], Fq(4), ["f4"], ["ll"], 128)
+        tt(Fq(5, 64), T.nd[:], T.mc[:], A.mult, ["nd", "mc"], ["f5"], 64)
+        tt(T.nat[:, 0:64], T.nat[:, 0:64], Fq(5, 64), A.add, ["f5"], ["nat"], 64)
+        tt(T.nat[:, 64:128], T.nat[:, 64:128], Fq(5, 64), A.subtract, ["f5"], ["nat1"], 64)
+        turn_out(T.pk0, "pk0", T.nat, ["nat", "nat1"])
+        act(T.osu[0:64, :], T.pk0[0:64, 0:256], AF.Copy, ["pk0"], ["osu"], 256)
+        store8(T.ysu, T.osu, ["osu"], "ysu")
+        turn_out(T.pk1, "pk1", T.lv, ["lv"])
+        act(T.ol0[0:64, :], T.pk1[0:64, 0:256], AF.Copy, ["pk1"], ["ol0"], 256, bias=2048.0, scale=-1.0)
+        lk = ["lw0", "lw1", "lw2", "ll"]
+        cp(T.lg[:, H(0)], T.lw[:, 0:1040].indirect(T.ll[:, 0:64]), lk, [("lg", 0)], 1024, GR)
+        act(T.lg[:, H(1)], T.lw[:, 0:1040].indirect(T.ll[:, 64:128]), AF.Copy, lk, [("lg", 1)], 1024, GR)
+        for h in range(2):
+            mms([(T.pt[0:64, 2 * i + h:256:32], T.lg[:, 1024 * h + i:1024 * h + 1024:16], T.selh[:], True, True) for i in range(16)],
+                [("lg", h), "selh"], ["pt"], 1024)
+        tt(T.olb[0:64, :], T.pt[0:64, 0:256], T.ol0[0:64, :], A.min, ["pt", "ol0"], ["olb"], 256, 1.0)
+        store8(T.ylab, T.olb, ["olb"], "ylab")
+
+    def out_x():
+        tag[0] = "X"
+        for c in range(2):
+            for h in range(2):
+                act(T.xo[:, 1024 * c + h:1024 * c + 1024:2], T.xq[:, 1024 * h + 512 * c:1024 * h + 512 * c + 512], AF.Copy,
+                    [("x3", h)], [("xo", c, h)], 512, bias=-129.0)
+            dma("y", T.yx[:, H(c)], T.xo[:, H(c)], [("xo", c, 0), ("xo", c, 1)], [("yx", c)], 2.8)
+
+    gains(0)
+    for t in range(3):
+        K = 3 + t
+        key(t)
+        astep(t, 1)
+        for k in range(1, K):
+            jstep(t, k)
+            astep(t, k + 1)
+        quant(t)
+        if t < 2:
+            gains(t + 1)
+        else:
+            out_x()
+        for k in range(1, K + 1):
+            bstep(t, k)
+        merge(t)
+    finish()
+    return ops
+
+
+def plan_deps(ops):
+    last_w, readers, bank = {}, {}, {}
+    for i, o in enumerate(ops):
+        d = set()
+        for k in set(o["r"] + o["w"]):
+            if k in PSUM:
+                e, cur, before = bank.get(k, (None, [], []))
+                if e == o["e"] and e != "p":
+                    d.update(before)
+                    bank[k] = (e, cur + [i], before)
+                else:
+                    d.update(cur)
+                    bank[k] = (o["e"], [i], cur)
+                continue
+            if k in last_w:
+                d.add(last_w[k])
+            if k in o["w"]:
+                d.update(readers.get(k, []))
+        d.discard(i)
+        o["d"] = d
+        for k in o["r"]:
+            if k not in PSUM:
+                readers.setdefault(k, []).append(i)
+        for k in o["w"]:
+            if k not in PSUM:
+                last_w[k] = i
+                readers[k] = []
+    return ops
+
+
+def rank_program(g, core, T, topo):
+    rank = T.rank_of(core)
+    if rank is None:
+        return
+    ops = plan_deps(build(g, core, T, topo, rank))
+    order = ORDER
+    Q = {"v": g.vector, "s": g.scalar, "p": g.tensor, "g": g, "y": g.sync}
+    CS = {"v": "nv", "s": "ns", "p": "nt", "g": "ng"}
+    pos = {i: n for n, i in enumerate(order)}
+    pool = [i for i in order if ops[i]["e"] == "g" and ops[i]["k"] == "c"]
+    for a, b in zip(pool, pool[1:]):
+        ops[b]["d"].add(a)
+
+    def needs(i, j):
+        a, b = ops[i], ops[j]
+        return not (b["k"] == "r" or (a["e"] == "p" and b["e"] == "p"))
+
+    want, seen = {}, {}
+    for i in order:
+        o = ops[i]
+        if o["k"] == "a":
+            continue
+        best, w = {}, []
+        for j in sorted(o["d"]):
+            if not needs(i, j):
+                continue
+            b = ops[j]
+            if b["k"] == "c":
+                if b["e"] not in best or pos[j] > pos[best[b["e"]]]:
+                    best[b["e"]] = j
+            elif (o["e"], j) not in seen:
+                seen[(o["e"], j)] = True
+                w.append(j)
+        for e, j in best.items():
+            if pos[j] > seen.get((o["e"], e), -1):
+                seen[(o["e"], e)] = pos[j]
+                w.append(j)
+        want[i] = w
+    waited = set(j for w in want.values() for j in w)
+    count = {e: 0 for e in CS}
+    nd = 0
+    for i in order:
+        o = ops[i]
+        if o["k"] == "c" and i in waited:
+            count[o["e"]] += 1
+            o["sv"] = (CS[o["e"]], count[o["e"]])
+        elif o["k"] == "d":
+            o["sv"] = ("d%d" % nd, 16)
+            nd += 1
+        elif o["k"] == "a":
+            o["sv"] = (o["sem"], sum(ops[j]["nb"] for j in o["d"]))
+    sent = 0
+    for i in order:
+        o = ops[i]
+        if o["k"] == "a":
+            continue
+        q = Q[o["e"]]
+        for j in want[i]:
+            q.wait_ge(T.sem[ops[j]["sv"][0]], ops[j]["sv"][1])
+        ins = o["f"]()
+        if o["k"] == "r":
+            sent += o["n"]
+        elif "sv" in o:
+            ins.then_inc(T.sem[o["sv"][0]], 16 if o["k"] == "d" else 1)
+    g.wait_ge(T.sem.sent, sent)
+    for i in order:
+        if ops[i]["k"] == "d" and i not in waited:
+            g.sync.wait_ge(T.sem[ops[i]["sv"][0]], 16)

@@ -1,164 +1,126 @@
 from concourse.mybir import AluOpType, ActivationFunctionType
 
-F, B16, I32, U16 = "float32", "bfloat16", "int32", "uint16"
+F, B16, I32, U16, H16 = "float32", "bfloat16", "int32", "uint16", "float16"
 SCRATCH = {}
 for _names, _shape, _dt in [
-        ("xa xb xc pa pb pc xq xo xd jt j0 j1 lg ob sel", [128, 2048], B16), ("a0 a1 b0 b1 kw ac bc", [128, 2048], F), ("lw", [128, 1040], B16),
-        ("mv ab", [128, 4096], B16), ("vc", [128, 1024], B16), ("big idb idn rp rn vw lh", [128, 128], B16), ("sui labi", [128, 128], I32),
-        ("suf one idf nat lv", [128, 128], F), ("io1", [128, 144], F), ("io5 neg vcon cv nd mc mm", [128, 64], F), ("kc", [128, 8], I32),
-        ("col selb", [128, 16], F), ("prm", [128, 512], F), ("zz", [128, 144], B16), ("rd", [128, 192], F), ("selh", [128, 8], B16),
-        ("ti", [128, 1024], I32), ("tf", [128, 1024], F), ("sb", [128, 3, 2, 64], F), ("sd st", [128, 3, 64], F),
-        ("hl", [128, 2, 2, 64], B16), ("hd ht", [128, 2, 64], B16), ("lnat ll", [128, 128], U16), ("lu0 lu1 lu2", [128, 384], U16),
-        ("jl", [128, 512], U16), ("eq", [128, 64], B16), ("tp tm osu olb ol0", [128, 256], F)]:
+        ("xa xb xc g1 gp gk w1 w2 xq", [128, 2048], B16), ("mo mp", [128, 4096], B16),
+        ("jt ib kw bc b0 b1 w3 w4 gf yl", [128, 2048], F), ("lw", [128, 1032], F),
+        ("sel", [128, 128, 16], B16), ("til", [128, 128, 8], H16), ("vc", [128, 1024], B16),
+        ("idb ids0 ids1 ids2 rp rn vw", [128, 128], B16), ("idh", [128, 128], H16), ("sui labi", [128, 128], I32),
+        ("suf one idf nat io1 st2", [128, 128], F), ("st2b", [128, 128], B16), ("kc", [128, 8], I32), ("col", [128, 16], F),
+        ("selb", [128, 24], F), ("gs", [128, 16], B16), ("prm", [128, 512], F),
+        ("ti", [128, 512], I32), ("tf", [128, 512], F), ("sb", [128, 2, 2, 64], F), ("sd st", [128, 2, 64], F),
+        ("nd mc", [128, 64], F), ("lraw lp0 lp1 lp2 ll", [128, 128], U16), ("lu0 lu1 lu2", [128, 256], U16),
+        ("jl", [128, 512], U16), ("eq", [128, 64], B16), ("tc0 tc1 tm0 tm1", [128, 32, 8], F), ("tmm", [128, 18, 8], B16),
+        ("kcol mx eqc eqs lm", [128, 8, 8], F), ("pt0 pt1 pt2 pl0 pl1 pl2", [128, 64], H16), ("osu", [128, 256], F)]:
     for _n in _names.split():
         SCRATCH[_n] = ("sbuf", _shape, _dt)
-for _n, _c in [("pk0", 512), ("pk1", 512), ("pda", 1024), ("pdb", 1024), ("pj", 512), ("pt", 512)]:
+for _n, _c in [("pa0", 1024), ("pa1", 1024), ("pk0", 512), ("pk1", 512), ("pc0", 512), ("pc1", 512)]:
     SCRATCH[_n] = ("psum", [128, _c], F)
-SEMAPHORES = ["nv", "ns", "nt", "ng", "sent", "arr0", "arr1", "arr2"] + ["d%d" % k for k in range(90)]
+SEMAPHORES = ["nv", "ns", "nt", "ng", "sent"] + ["al%d" % k for k in range(3)] + ["ap%d" % k for k in range(3)] + ["d%d" % k for k in range(70)]
 
 MASKS = [4, 1, 2]
 GR = 1.56
 CY = 0.83e-3
 PC = 0.42e-3
-PSUM = ("pk0", "pk1", "pda", "pdb", "pj", "pt")
-OPT = {"u": ["svss", "ssss", "svss"]}
-CODE = ("0806000U07010302040;090:0<0V0T10190B12131411180W16171:1;1<052227211=1?1V1>1@1A1B1C1N2823241H1D1E1I1F1G1K1M1J1L1O3<2;3:2A2<3=3>3?3F"
-        "2?1U2=3@253A2>262@3G2B292:3I383H1S3J0>0D0?0=0A0M0F0J0C0H0G3;2C2D2F2E2N2G2J2H2I2P2K2O2T3D393E3B3K3M3C0@0E0L1T3L1W1P2Q152U3Q3N0P0I3R"
-        "0N0R0O3O2L2M2R2S2V2W30313335323436374W3T3V463U3W4247434041484<494450511Q53523P3S54554:454;4=575856594>1R5:5;5=5>5<5?5@5A5H5B5G5C5I"
-        "5D5J5K5L5T4@4B4K4A4L4C4G4?4D4H4M4N4Q4E4F4I4J4U5F5E604R614O4P4S4T4V5O5V5U6266636:5W670K645Q5N5P65686=6;6<6>5R5S696D6@6A6?7U6B6G6E6F"
-        "6H6C7S6I6J6K6L7V7T7W806O6P0Q816N836S6Q82840S7476787:5M6R706T6U716V6W857572737787888689796M8:208;8=8<8>8?8@8L8B8A8G8C8H8D8I8J8K8U8W"
-        "8E8F7<7=7>7H7G7?7@7C7;7I7D7J7M7A917N7B7K7E7F7Q7L928M7O7P7R8N8V93978P948O8S8Q9;9095968R99:79>9<9=9?9E8T:9:89@:;9F9G9H9O9I:::=9:98:<"
-        "9C:?:>9J:A9R:@9A9P9Q9S:C:B:D9T:G:H:E:F9D9B9K9L9M9U9N:I:J:K:L9V:N:M:S;3:O:T:P:V:Q:U;0:W;1;4;6;5:R;7;8;;;9;<;:;=;H;>9W:4:1:0;2:2:5;K"
-        ";?;F;D;B;@;A;C;G;E:6:3;I;J;L;M;N;U;Q;S;R;T;V;P;O")
-ORDER = [(ord(CODE[i]) - 48) * 40 + ord(CODE[i + 1]) - 48 for i in range(0, len(CODE), 2)]
+WAKE = 0.1
+OPT = {"eng": 2, "dma": 1.8, "rem": 3.0, "bias": [0.3, 0.6, 1.0, 2.0], "passes": 4}
 
 
 def build(g, core, T, topo, rank):
     A, AF = AluOpType, ActivationFunctionType
     ops = []
-    tag = ["I"]
 
-    def add(eng, fn, r, w, t, kind="c", lat=0.0):
-        ops.append({"e": eng, "f": fn, "r": list(r), "w": list(w), "t": t, "k": kind, "lat": lat, "g": tag[0]})
+    def add(alt, r, w, kind="c", lat=0.0):
+        ops.append({"alt": alt, "r": list(r), "w": list(w), "k": kind, "lat": lat})
 
     def vt(n, c=1.0):
         return 0.05 + max(64, n * c) * CY
 
+    def stime(n, c=1.0):
+        return 0.065 + max(64, n * c) * CY
+
     def ts(out, in0, s1, s2, o0, o1, r, w, n, c=1.0):
         if o1 is None:
-            add("v", lambda: g.vector.tensor_scalar(out, in0, s1, None, o0), r, w, vt(n, c))
+            add({"v": (lambda: g.vector.tensor_scalar(out, in0, s1, None, o0), vt(n, c))}, r, w)
         else:
-            add("v", lambda: g.vector.tensor_scalar(out, in0, s1, s2, o0, o1), r, w, vt(n, c))
+            add({"v": (lambda: g.vector.tensor_scalar(out, in0, s1, s2, o0, o1), vt(n, c))}, r, w)
 
     def tt(out, in0, in1, o, r, w, n, c=2.0):
-        add("v", lambda: g.vector.tensor_tensor(out, in0, in1, o), r, w, vt(n, c))
+        add({"v": (lambda: g.vector.tensor_tensor(out, in0, in1, o), vt(n, c))}, r, w)
 
     def cp(out, in_, r, w, n, c=1.0):
-        add("v", lambda: g.vector.tensor_copy(out, in_), r, w, vt(n, c))
+        add({"v": (lambda: g.vector.tensor_copy(out, in_), vt(n, c))}, r, w)
 
     def ms(out, val, w, n, c=1.0):
-        add("v", lambda: g.vector.memset(out, val), [], w, vt(n, c))
+        add({"v": (lambda: g.vector.memset(out, val), vt(n, c))}, [], w)
 
-    def act(out, in_, fn, r, w, n, c=1.0, bias=0.0, scale=1.0):
-        add("s", lambda: g.scalar.activation(out, in_, fn, bias=bias, scale=scale), r, w, 0.065 + max(64, n * c) * CY)
+    def lin(out, in_, r, w, n, c=1.0, scale=1.0, bias=0.0, on="vs", cv=None):
+        alt = {}
+        if "s" in on:
+            fn = AF.Copy if isinstance(bias, float) else AF.Identity
+            alt["s"] = (lambda: g.scalar.activation(out, in_, fn, bias=bias, scale=scale), stime(n, c))
+        if "v" in on:
+            alt["v"] = (lambda: g.vector.tensor_scalar(out, in_, scale, bias, A.mult, A.add), vt(n, cv or c))
+        add(alt, r, w)
 
     def mms(lst, r, w, cyc):
         def fn():
             for a in lst:
                 ins = g.tensor.matmul(*a)
             return ins
-        add("p", fn, r, w, 0.05 + cyc * PC)
+        add({"p": (fn, 0.04 + cyc * PC)}, r, w)
 
-    def dma(q, out, in_, r, w, lat=2.0):
-        add(q, lambda: (g.sync if q == "y" else g.scalar).dma_start(out, in_), r, w, 0.06, "d", lat)
+    def dma(q, out, in_, r, w, lat=0.0):
+        add({q: (lambda: (g.sync if q == "y" else g.scalar).dma_start(out, in_), 0.06)}, r, w, "d", OPT["dma"] + lat)
 
     def iota(out, pat, base, cm, w, n, flt=True, r=()):
         if flt:
-            add("g", lambda: g.iota(out, pat, base, cm, allow_small_or_imprecise_dtypes=True), r, w, 0.13 + 2 * n * CY)
+            add({"g": (lambda: g.iota(out, pat, base, cm, allow_small_or_imprecise_dtypes=True), 0.13 + 2 * n * CY)}, r, w)
         else:
-            add("g", lambda: g.iota(out, pat, base, cm), r, w, 0.13 + 2 * n * CY)
+            add({"g": (lambda: g.iota(out, pat, base, cm), 0.13 + 2 * n * CY)}, r, w)
 
     def fill(out, val, w, n, r=()):
         iota(out, [[0, n]], val, 0, w, n, True, r)
 
     def pick(out, in_, pat, base, cm, r, w, n):
-        add("g", lambda: g.affine_select(out, in_, pat, A.is_equal, 0.0, base, cm), r, w, 0.17 + 2 * n * CY)
+        add({"g": (lambda: g.affine_select(out, in_, pat, A.is_equal, 0.0, base, cm), 0.17 + 2 * n * CY)}, r, w)
 
-    def send(t, src, dst, h, r):
+    def engines(a, b):
+        return topo.engines(a, b)[::OPT["eng"]]
+
+    def send(t, src, dst, sem, r, key):
         peer = T.cores[rank ^ MASKS[t]]
         rid, pid = topo.addr(peer, core)
-        m = topo.mask(core, peer)
-        add("g", lambda: g.remote_dma(dst[:, H(h)], src[:, H(h)], T.sem["arr%d" % t], T.sem.sent, pid, rid, m), r, [("snd", t, h)], 0.3, "r", 6.0)
-        ops[-1]["n"] = len(topo.engines(core, peer))
-        ops[-1]["nb"] = len(topo.engines(peer, core))
+        m = sum(1 << e for e in engines(core, peer))
+        add({"g": (lambda: g.remote_dma(dst, src, T.sem[sem], T.sem.sent, pid, rid, m), 2.4 if sem == "al0" else 0.4)}, r, [("snd", sem)], "r", OPT["rem"])
+        ops[-1]["n"] = len(engines(core, peer))
+        add({}, [("snd", sem)], [key], "a")
+        ops[-1]["sv"] = (sem, len(engines(peer, core)))
 
     def H(h):
         return slice(1024 * h, 1024 * h + 1024)
 
+    def Q(q):
+        return slice(512 * q, 512 * q + 512)
+
     def hk(name):
         return [(name, 0), (name, 1)]
 
+    def qk(name, h=None):
+        return [(name, q) for q in range(4) if h is None or q // 2 == h]
+
     col = T.col
-    C15, CN15, CZ, CW, CE2, CHL, CB0, CB1 = [col[:, k:k + 1] for k in range(8)]
-    X = [T.xa, T.xb, T.xc]
-    XP = [T.pa, T.pb, T.pc]
-    LU = [T.lu0, T.lu1, T.lu2]
-    PK = [T.pk0, T.pk1]
-    AB = [T.a0, T.a1]
-
-    dma("y", T.sui[:], T.su[:], [], ["sui"])
-    dma("s", T.xa[:, H(1)], T.x0[:, H(1)], [], [("x0", 1)], 2.8)
-    dma("y", T.xa[:, H(0)], T.x0[:, H(0)], [], [("x0", 0)], 2.8)
-    for h in range(2):
-        dma("y", T.xd[:, H(h)], T.x0[:, H(h)], [], [("xd", h)], 2.8)
-    dma("s", T.labi[:], T.lab[:], [], ["labi"])
-    iota(T.kc[:, 0:1], [[1, 1]], 0, 1, ["kc0"], 1, False)
-    iota(T.io1[:], [[1, 144]], 0, -1, ["io1"], 144)
-    ms(T.one[:], 1.0, ["one"], 128)
-    for k in range(4):
-        pick(T.prm[:, 128 * k:128 * k + 128], T.one[:], [[16, 8], [1000, 2], [2, 8]], k // 2 - 1000 * (k % 2), -1, ["one"], [("prm", k)], 128)
-    send(0, T.xa, T.pa, 0, [("x0", 0)])
-    send(0, T.xa, T.pa, 1, [("x0", 1)])
-    iota(T.vc[0:32, :], [[1, 32], [0, 32]], 0, 0, ["vc0"], 1024)
-    iota(T.vc[32:64, :], [[0, 32], [1, 32]], 0, 0, ["vc1"], 1024)
-    fill(T.sel[:], 0, ["sel"], 2048)
-    ms(T.big[:], -float(2 ** 25), ["big"], 128, 0.5)
-    pick(T.sel[:, 0:2048:16], T.big[:], [[-1, 16], [-16, 8]], 0, 1, ["big"], ["sel"], 128)
-    fill(T.vw[0:64, :], 0, ["vw"], 128)
-    fill(T.vw[0:1, 0:128:16], 32, ["vw0"], 8, ["vw"])
-    fill(T.vw[0:1, 8:128:16], -64, ["vw1"], 8, ["vw"])
-    fill(T.vw[32:33, 0:128:16], 1, ["vw2"], 8, ["vw"])
-    fill(T.vw[32:33, 8:128:16], -2, ["vw3"], 8, ["vw"])
-    fill(T.bc[:], 0, hk("bc"), 2048)
-    pick(T.selb[:], T.one[:, 0:16], [[8, 2], [16, 8]], 0, -1, ["one"], ["selb"], 16)
-    pick(T.idf[:], T.one[:], [[1, 128]], 0, -1, ["one"], ["idf"], 128)
-    pick(T.rd[:, 64:192], T.one[:], [[1, 128]], 0, -1, ["one"], ["rd1"], 128)
-    fill(T.neg[:], -1, ["neg"], 64)
-    pick(T.rd[0:64, 0:64], T.one[0:64, 0:64], [[1, 64]], 0, -1, ["one"], ["rd0"], 64)
-    pick(T.rd[64:128, 0:64], T.neg[64:128, :], [[1, 64]], 0, -1, ["neg"], ["rd2"], 64)
-    iota(T.io5[:], [[16, 64]], 0, 0, ["io5"], 64)
-    fill(T.lw[:], 0, ["lw0", "lw1", "lw2"], 1040)
-    fill(T.lg[0:8, 0:1040], 32, hk("lg"), 1040)
-    dma("y", T.lw[2:128:16, :], T.lg[0:8, 0:1040], hk("lg"), ["lw2"])
-    ms(T.jt[:], 0.0, ["jt0", "jt1"], 2048, 0.5)
-    ts(T.kc[:, 4:5], T.kc[:, 0:1], 15, None, A.bitwise_and, None, ["kc0"], ["kc4"], 1)
-    cp(C15, T.kc[:, 4:5], ["kc4"], ["c15"], 1)
-    ts(T.idb[:], T.io1[:, 0:128], 0.0, None, A.is_equal, None, ["io1", "jt0"], ["idb"], 128)
-    ts(T.idn[:], T.io1[:, 0:128], 0.0, -1.0, A.is_equal, A.mult, ["io1"], ["idn"], 128)
-    act(CN15, C15, AF.Copy, ["c15"], ["cn15"], 1, scale=-1.0)
-    act(CZ, C15, AF.Copy, ["c15"], ["cz"], 1, scale=-1.0, bias=15.0)
-    act(CW, C15, AF.Copy, ["c15"], ["cw"], 1, scale=-63.0, bias=64.0)
-    act(CB0, C15, AF.Copy, ["c15"], ["cb0"], 1, scale=-(2 ** 23 - 2048) / 8, bias=float(2 ** 23))
-    act(CB1, C15, AF.Copy, ["c15"], ["cb1"], 1, scale=-(2 ** 23 - 2047) / 8, bias=float(2 ** 23))
-    ts(T.rp[:], T.io1[:, 0:128], CN15, 2048.0, A.is_equal, A.mult, ["io1", "cn15"], ["rp"], 128)
-    act(T.rn[:], T.rp[:], AF.Copy, ["rp"], ["rn"], 128, scale=-1.0)
-    ts(T.zz[:], T.io1[:], CZ, CW, A.is_equal, A.mult, ["io1", "cz", "cw"], ["zz"], 144)
-
-    cp(T.suf[:], T.sui[:], ["sui"], ["suf"], 128)
-    for h in range(2):
-        mms([(T.pj[:, 64 * h:64 * h + 64], T.prm[:, 128 * (2 * h + b):128 * (2 * h + b) + 128], T.suf[:, b:128:2], b == 0, b == 1) for b in range(2)],
-            ["suf", ("prm", 2 * h), ("prm", 2 * h + 1)], ["pj"], 512)
+    C15, CN15, CA, CB = [col[:, k:k + 1] for k in range(4)]
+    CK = [col[:, 4:5], col[:, 5:6]]
+    X, LU, LP = [T.xa, T.xb, T.xc], [T.lu0, T.lu1, T.lu2], [T.lp0, T.lp1, T.lp2]
+    PA, PK, PCV = [T.pa0, T.pa1], [T.pk0, T.pk1], [T.pc0, T.pc1]
+    IDS, TC, TM = [T.ids0, T.ids1, T.ids2], [T.tc0, T.tc1], [T.tm0, T.tm1]
+    PT, PL = [T.pt0, T.pt1, T.pt2], [T.pl0, T.pl1, T.pl2]
     ti, tf = T.ti, T.tf
+
+    def pa(q):
+        return PA[q // 2][:, Q(q % 2)]
 
     def I(k, n=128):
         return ti[:, 128 * k:128 * k + n]
@@ -166,305 +128,371 @@ def build(g, core, T, topo, rank):
     def Fq(k, n=128):
         return tf[:, 128 * k:128 * k + n]
 
-    cp(T.lnat[:], T.pj[:, 0:128], ["pj"], ["lnat"], 128)
-    cp(I(0), T.pj[:, 0:128], ["pj"], ["i0"], 128)
-    act(T.nat[:], T.pj[:, 0:128], AF.Copy, ["pj"], ["nat"], 128)
-    ts(I(1), I(0), 1, None, A.bitwise_and, None, ["i0"], ["i1"], 128)
-    ts(I(2), I(0), 1, None, A.arith_shift_right, None, ["i0"], ["i2"], 128)
-    ts(I(4), I(0), 1, 63, A.arith_shift_right, A.bitwise_and, ["i0"], ["i4"], 128)
-    ts(Fq(0), I(1), 1024.0, None, A.mult, None, ["i1"], ["f0"], 128)
-    cp(T.hl[:, 1], I(4), ["i4"], ["hl1"], 128)
-    tt(I(3), Fq(0), I(2), A.add, ["f0", "i2"], ["i3"], 128)
-    ts(I(5), I(3), 6, None, A.arith_shift_right, None, ["i3"], ["i5"], 128)
-    cp(T.hl[:, 0], I(5), ["i5"], ["hl0"], 128)
+    dma("y", T.sui[:], T.su[:], [], ["sui"])
+    dma("s", T.xa[:, H(1)], T.x0[:, H(1)], [], [("x0", 1)], 1.0)
+    dma("y", T.xa[:, H(0)], T.x0[:, H(0)], [], [("x0", 0)], 1.0)
+    dma("y", T.labi[:], T.lab[:], [], ["labi"], 0.5)
+    cp(T.lraw[:], T.sui[:], ["sui"], ["lraw"], 128)
+    send(0, T.lraw[:], T.lp0[:], "al0", ["lraw"], ("lp", 0))
+    iota(T.kc[:, 0:1], [[1, 1]], 0, 1, ["kc0"], 1, False)
+    iota(T.io1[:], [[1, 128]], 0, -1, ["io1"], 128)
+    ms(T.one[:], 1.0, ["one"], 128)
+    for k in range(4):
+        pick(T.prm[:, 128 * k:128 * k + 128], T.one[:], [[16, 8], [1000, 2], [2, 8]], k // 2 - 1000 * (k % 2), -1, ["one"], [("prm", k)], 128)
+    ms(T.sel[:], 0.0, ["sel"], 2048, 0.5)
+    for h in range(2):
+        lin(T.jt[:, H(h)], T.sel[:, 64 * h:64 * h + 64, :], ["sel"], ["jt"], 1024, on="s")
+    cp(T.til[:], T.sel[:, 0:64, :], ["sel"], ["til0", "til8"], 1024, 0.5)
+    for h in range(2):
+        ms(TC[h][:, 0:18:2, :], 0.0, [("tc", h)], 72)
+        ms(TM[h][:, 0:18:2, :], 0.0, [("tm", h)], 72)
+    ms(T.tmm[:, 0:18:2, :], 0.0, ["tmm"], 72, 0.5)
+    lin(T.mc[:], T.sel[:, 0:4, :], ["sel"], ["mc"], 64)
+    lin(T.lw[:, 1024:1032], T.sel[:, 0, 0:8], ["sel"], ["lwx"], 8, bias=4096.0)
+    ts(T.kc[:, 4:5], T.kc[:, 0:1], 15, None, A.bitwise_and, None, ["kc0"], ["kc4"], 1)
+    cp(C15, T.kc[:, 4:5], ["kc4"], ["c15"], 1)
+    lin(CN15, C15, ["c15"], ["cn15"], 1, scale=-1.0)
+    ts(T.idb[:], T.io1[:], 0.0, None, A.is_equal, None, ["io1"], ["idb"], 128)
+    for t in range(3):
+        lin(IDS[t][:], T.idb[:], ["idb"], [("ids", t)], 128, scale=2.0 ** (-3 - t), cv=0.5)
+    lin(T.idf[:], T.idb[:], ["idb"], ["idf"], 128)
+    lin(T.idh[:], T.idb[:], ["idb"], ["idh"], 128, scale=-2048.0, on="v", cv=0.5)
+    lin(T.sel[:, 0:128:16, :], T.idb[:], ["idb"], ["sel"], 128, scale=2.0 ** 25, cv=0.5)
+    ts(T.rp[:], T.io1[:], CN15, -2048.0, A.is_equal, A.mult, ["io1", "cn15"], ["rp"], 128)
+    lin(T.rn[:], T.rp[:], ["rp"], ["rn"], 128, scale=-1.0, cv=0.5)
+    lin(T.gs[:, 0:8], T.rp[:, 0:128:16], ["rp"], ["gs0"], 8, scale=-1.0 / 2048)
+    lin(T.gs[:, 8:16], T.rp[:, 0:128:16], ["rp"], ["gs1"], 8, scale=1.0 / 2048)
+    for k, (row, wt) in enumerate([(1, 1.0), (0, -1.0), (8, 1.0)]):
+        ts(T.selb[:, 8 * k:8 * k + 8], T.io1[:, 0:128:16], -float(row), wt, A.is_equal, A.mult, ["io1"], [("selb", k)], 8)
+    selk = [("selb", k) for k in range(3)]
+    pick(T.st2[:], T.one[:], [[1, 2], [2, 64]], 0, -1, ["one"], ["st2"], 128)
+    lin(T.st2b[:], T.st2[:], ["st2"], ["st2b"], 128)
+    ts(CA, C15, 0.0, -float(2 ** 23), A.is_equal, A.mult, ["c15"], ["ca"], 1)
+    ts(CB, C15, 1.0, 4096.0, A.is_equal, A.mult, ["c15"], ["cb"], 1)
+    ts(CK[0], CA, CB, None, A.add, None, ["ca", "cb"], [("ck", 0)], 1)
+    ts(CK[1], C15, 8.0, CK[0], A.is_equal, A.add, ["c15", ("ck", 0)], [("ck", 1)], 1)
+    iota(T.vc[0:32, :], [[1, 32], [0, 32]], 0, 0, ["vc0"], 1024)
+    iota(T.vc[32:64, :], [[0, 32], [1, 32]], 0, 0, ["vc1"], 1024)
+    fill(T.vw[0:64, :], 0, ["vw"], 128)
+    for k, (p, c, val) in enumerate([(0, 0, -32), (0, 8, 64), (32, 0, -1), (32, 8, 2)]):
+        fill(T.vw[p:p + 1, c:128:16], val, [("vw", k)], 8, ["vw"])
+    for h in range(2):
+        fill(T.bc[:, H(h)], 4096, [("bc", h)], 1024)
 
-    def rows_of_su():
-        dma("y", T.jt[0:128:16, :], T.hl[:, 0], ["hl0"], ["jt0"])
-        dma("y", T.jt[1:128:16, :], T.hl[:, 1], ["hl1"], ["jt1"])
-
-    rows_of_su()
-    ts(I(6), I(3), 15, None, A.bitwise_and, None, ["i3"], ["i6"], 128)
-    ts(I(7), I(3), 4, None, A.arith_shift_right, None, ["i3"], ["i7"], 128)
-    ts(Fq(1), I(6), 128.0, None, A.mult, None, ["i6"], ["f1"], 128)
-    tt(T.sb[:, 1], Fq(1), I(7), A.add, ["f1", "i7"], ["sb1"], 128)
-    cp(T.sb[:, 0], I(3), ["i3"], ["sb0"], 128)
-    cp(T.sb[:, 2], I(2), ["i2"], ["sb2"], 128)
-    cp(T.lu0[:], T.sb[:], ["sb0", "sb1", "sb2"], ["lu0"], 384)
+    lin(T.suf[:], T.sui[:], ["sui"], ["suf"], 128, on="v")
+    for h in range(2):
+        mms([(T.pc0[:, 64 * h:64 * h + 64], T.prm[:, 128 * (2 * h + b):128 * (2 * h + b) + 128], T.suf[:, b:128:2], b == 0, b == 1) for b in range(2)],
+            ["suf", ("prm", 2 * h), ("prm", 2 * h + 1)], ["pc0"], 512)
+    lin(T.nat[:], T.pc0[:, 0:128], ["pc0"], ["nat"], 128)
+    for k, sh in enumerate([1, 5]):
+        lin(I(k), T.nat[:], ["nat"], [("i", k)], 128, scale=2.0 ** -sh, bias=2.0 ** (-sh - 1) - 0.5, on="v")
+        lin(Fq(k), T.nat[:], ["nat"], [("f", k)], 128, scale=2048.0 * 2.0 ** -sh)
+        lin(Fq(2 + k), I(k), [("i", k)], [("f", 2 + k)], 128, scale=-2047.0, on="v")
+        tt(T.sb[:, k], Fq(k), Fq(2 + k), A.add, [("f", k), ("f", 2 + k)], [("sb", k)], 128)
+        cp(T.lu0[:, 128 * k:128 * k + 128], T.sb[:, k], [("sb", k)], [("lu", 0, k)], 128)
+        tt(T.sd[:, k], T.sb[:, k, 1, :], T.sb[:, k, 0, :], A.subtract, [("sb", k)], [("sd", k)], 64)
+    for t in (1, 2):
+        send(t, T.lu0[:, 0:128], LP[t][:], "al%d" % t, [("lu", 0, 0)], ("lp", t))
     tt(T.eq[:], T.labi[:, 0:128:2], T.labi[:, 1:128:2], A.is_equal, ["labi"], ["eq"], 64)
-    ts(T.vcon[:], T.io5[:], C15, None, A.add, None, ["io5", "c15"], ["vcon"], 64)
-    ts(T.cv[:], T.vcon[:], 0.0, None, A.is_equal, None, ["vcon"], ["cv"], 64)
-    tt(T.sd[:], T.sb[:, :, 1, :], T.sb[:, :, 0, :], A.subtract, ["sb0", "sb1", "sb2"], ["sd"], 192)
-    tt(T.hd[:], T.hl[:, :, 1, :], T.hl[:, :, 0, :], A.subtract, ["hl0", "hl1"], ["hd"], 128)
     tt(T.nd[:], T.nat[:, 64:128], T.nat[:, 0:64], A.subtract, ["nat"], ["nd"], 64)
-    ts(CE2, C15, 2.0, 2.0, A.is_equal, A.mult, ["c15"], ["ce2"], 1)
-    ts(CHL, CW, -1.0, CE2, A.mult, A.add, ["cw", "ce2"], ["chl"], 1)
-    ts(T.selh[:], T.io1[:, 0:128:16], CN15, CHL, A.is_equal, A.mult, ["io1", "cn15", "chl"], ["selh"], 8)
 
-    ring = {"v": 0, "s": 0}
-    started = [False, False]
-
-    def own(x, t, h, a, n):
+    def half(x, t, h, a=0, n=1024):
         return x[:, 2 * a + h:2 * (a + n):2] if t == 0 else x[:, 1024 * h + a:1024 * h + a + n]
 
-    def reduce_into(b, w, src, r):
-        mms([(PK[b][:], w[:], src, not started[b], False)], r + ["rp", "rn"], ["pk%d" % b], 512)
-        started[b] = True
+    def partk(name, t, h, b):
+        return (name, b if t == 0 else 2 * h + b)
 
-    def gain_unit(t, s, b, eng):
-        tag[0] = "U%d%s%d" % (t, s, b)
-        x = X[t] if s == "o" else XP[t]
-        lst, lk = (T.lnat, "lnat") if t == 0 else (T.lu0, "lu0")
-        off = [lst[:, 64 * h + 32 * b:64 * h + 32 * b + 32] for h in range(2)]
-        xk = hk("x%d" % t) if s == "o" else [("xp", t)]
-        q = ring[eng]
-        ring[eng] = 1 - q
-        if eng == "v":
-            for n, (hi, ho) in enumerate([(0, 0), (0, 1), (1, 1), (1, 0)]):
-                m = T.mv[:, 2048 * q + 512 * n:2048 * q + 512 * n + 512]
-                tt(m, x[:, 0:2048].indirect(off[ho]), own(T.xd, t, hi, 512 * b, 512), A.max, xk + hk("xd") + [lk], [("mv", q, n)], 512, GR)
-                reduce_into(b, T.rp if hi == ho else T.rn, m, [("mv", q, n)])
-            return
-        for ho in range(2):
-            o = T.ob[:, 1024 * q + 512 * ho:1024 * q + 512 * ho + 512]
-            act(o, x[:, 0:2048].indirect(off[ho]), AF.Copy, xk + [lk], [("ob", q, ho)], 512, GR)
-        for ho in range(2):
-            o = T.ob[:, 1024 * q + 512 * ho:1024 * q + 512 * ho + 512]
-            pd, pn = (T.pda, "pda") if ho == 0 else (T.pdb, "pdb")
-            lst2 = []
-            for hi in range(2):
-                d = pd[:, 512 * hi:512 * hi + 512]
-                lst2 += [(d, T.idb[:], own(x, t, hi, 512 * b, 512), True, False), (d, T.idn[:], o, False, True)]
-            mms(lst2, xk + [("ob", q, ho), "idb", "idn"], [pn], 2048)
-            a0 = 2048 * q + 1024 * ho
-            act(T.ab[:, a0:a0 + 1024], pd[:], AF.Abs, [pn], [("ab", q, ho)], 1024, scale=0.5)
-            for hi in range(2):
-                reduce_into(b, T.rp if hi == ho else T.rn, T.ab[:, a0 + 512 * hi:a0 + 512 * hi + 512], [("ab", q, ho)])
-
-    def gains(t):
-        for n, (s, b) in enumerate([("o", 0), ("o", 1), ("p", 0), ("p", 1)]):
-            if n == 2:
-                add("a", None, [("snd", t, 0), ("snd", t, 1)], [("xp", t)], 0.0, "a")
-                ops[-1]["sem"] = "arr%d" % t
-            gain_unit(t, s, b, OPT["u"][t][n])
-        for b in range(2):
-            mms([(PK[b][:], T.vw[0:64, :], T.vc[0:64, 512 * b:512 * b + 512], False, False)],
-                ["vw", "vw0", "vw1", "vw2", "vw3", "vc0", "vc1"], ["pk%d" % b], 512)
-
-    def key(t):
-        tag[0] = "K%d" % t
-        for b in range(2):
-            if t == 0:
-                lst = [(PK[b][:, 64 * a:64 * a + 64], T.sel[:, 128 * (8 * b + a):128 * (8 * b + a) + 128], T.eq[:], False, a == 7) for a in range(8)]
-            else:
-                lst = [(PK[b][:, i:512:16], T.sel[:, 128 * i:128 * i + 128], T.eq[:, 32 * b:32 * b + 32], False, i == 15) for i in range(16)]
-            mms(lst, ["sel", "eq"], ["pk%d" % b], 64 * len(lst))
-            started[b] = False
-        act(T.kw[:, 0:512], T.pk0[:], AF.Identity, ["pk0", "cb0"], [("kw", 0)], 512, bias=CB0)
-        ts(T.kw[:, 512:1024], T.pk1[:], CB0, None, A.add, None, ["pk1", "cb0"], [("kw", 1)], 512)
-        act(T.kw[:, 1536:2048], T.pk1[:], AF.Identity, ["pk1", "cb1"], [("kw", 3)], 512, bias=CB1)
-        ts(T.kw[:, 1024:1536], T.pk0[:], CB1, None, A.add, None, ["pk0", "cb1"], [("kw", 2)], 512)
-        for h in range(2 if t == 2 else 0):
-            rows(T.kw[0:128:8, H(h)], [("kw", 2 * h), ("kw", 2 * h + 1)], h)
-
-    def rows(src, r, h):
-        dma("y", T.bc[0:128:8, H(h)], src, r, [("bc", h)])
+    def gather(out, win, off, r, w, scale=1.0, bias=0.0):
+        lin(out, win.indirect(off), r, w, 1024, GR, scale, bias)
 
     def jlist(k, h):
         return T.jl[:, 128 * (k - 1) + 64 * h:128 * (k - 1) + 64 * h + 64]
 
-    def jstep(t, k):
-        tag[0] = "J%d%d" % (t, k)
-        out, on = ([T.j0, T.j1][k % 2], "j%d" % (k % 2))
-        for h in range(2):
-            if k == 1:
-                act(out[:, H(h)], T.jt[:, 0:2048].indirect(LU[t][:, 128 + 64 * h:192 + 64 * h]), AF.Copy, ["jt0", "jt1", "lu%d" % t], [(on, h)], 1024, GR)
+    def columns(src, sk, h, lo, hi):
+        mms([(PCV[h][:, i:64 * (hi - lo):8], src[:, 1024 * h + i:1024 * h + 1024:8], T.selb[:, 8 * lo:8 * hi], True, True) for i in range(8)],
+            sk + selk, ["pc%d" % h], 2048)
+
+    def to_list(out, on, tile, tk, rhs, rk, cyc):
+        mms([(out, tile[:, 1 - b:17 - b, :], rhs[:, 64 * b:64 * b + 64], b == 0, b == 1) for b in range(2)], [tk, rk], [on], cyc)
+
+    def convert(src, sk, h, k, keep):
+        n = 2 if keep else 1
+        columns(src, sk, h, 0, n)
+        lin(TC[h][:, 1:16 * n:2, :], PCV[h][:, 0:64 * n], ["pc%d" % h], [("tc", h)], 64 * n)
+        to_list(PCV[h][:, 256:320], "pc%d" % h, TC[h], ("tc", h), T.st2, "st2", 512)
+        cp(jlist(k, h), PCV[h][:, 256:320], ["pc%d" % h], [("jl", k, h)], 64)
+
+    def to_rows(row_key):
+        for b in range(2):
+            mms([(PK[b][:, i:512:8], T.til[:, :, i], T.idh[:, 64 * b:64 * b + 64], False, i == 7) for i in range(8)],
+                ["til0", "til8", "idh"], ["pk%d" % b], 512)
+
+    TERMS = [(0, 0), (1, 0), (1, 1), (0, 1)]
+
+    def maxes(t, G, gn, M, mn):
+        for b in range(2):
+            for hi in range(2):
+                mms([(pa(2 + hi), T.idb[:], half(X[t], t, hi, 512 * b, 512), True, True)], [partk("x%d" % t, t, hi, b), "idb"], [("pa", 2 + hi)], 512)
+                for ho in range(2):
+                    n = TERMS.index((hi, ho))
+                    tt(M[:, Q(2 * n + b)], pa(2 + hi), half(G, t, ho, 512 * b, 512), A.max, [("pa", 2 + hi), partk(gn, t, ho, b)], [(mn, n, b)], 512, 1.0)
+
+    def at_successors(t, G, gn, lst, lk):
+        x, xk = X[t][:, 0:2048], qk("x%d" % t)
+        for b in range(2):
+            if t == 0:
+                gather(G[:, H(b)], x, lst[:, 64 * b:64 * b + 64], xk + [lk], [(gn, b)])
             else:
-                win = [T.j0, T.j1][(k - 1) % 2]
-                act(out[:, H(h)], win[:, 0:2048].indirect(jlist(k - 1, h)), AF.Copy, hk("j%d" % ((k - 1) % 2)) + [("jl", k - 1, h)], [(on, h)], 1024, GR)
-            mms([(T.pj[:, 64 * h:64 * h + 64], T.zz[:, 15 - i:143 - i], out[:, 1024 * h + i:1024 * h + 1024:16], i == 0, i == 15) for i in range(16)],
-                [(on, h), "zz"], ["pj"], 1024)
-            cp(jlist(k, h), T.pj[:, 64 * h:64 * h + 64], ["pj"], [("jl", k, h)], 64)
+                for q in (b, 2 + b):
+                    lin(G[:, Q(q)], x.indirect(lst[:, 32 * q:32 * q + 32]), xk + [lk], [(gn, q)], 512, GR)
+
+    def gains(t):
+        at_successors(t, T.g1, "g1", T.lraw if t == 0 else LU[t], "lraw" if t == 0 else ("lu", t, 0))
+        at_successors(t, T.gp, "gp", LP[t], ("lp", t))
+        if t == 0:
+            maxes(t, T.g1, "g1", T.mo, "mo")
+        maxes(t, T.gp, "gp", T.mp, "mp")
+        if t > 0:
+            maxes(t, T.g1, "g1", T.mo, "mo")
+        mms([(T.pk1[:, 0:64], T.idb[:], T.sel[:, 1:5, :], True, False)], ["idb", "sel"], ["pk1"], 64)
+        for n, (hi, ho) in enumerate(TERMS):
+            s = 0 if hi == ho else 1
+            mms([(T.pk1[:, i:64:8], T.mp[:, 1024 * n + i:1024 * n + 1024:8], T.gs[:, 8 * s:8 * s + 8], False, n == 3 and i == 7) for i in range(8)],
+                [("mp", n, 0), ("mp", n, 1), "gs0", "gs1"], ["pk1"], 512)
+        cp(PT[t][:], T.pk1[:, 0:64], ["pk1"], [("pt", t)], 64)
+        send(t, PT[t][:], PL[t][:], "ap%d" % t, [("pt", t)], ("pl", t))
+        for b in range(2):
+            mms([(PK[b][:], T.vw[0:64, :], T.vc[0:64, Q(b)], True, False)], ["vw", "vc0", "vc1"] + qk("vw"), ["pk%d" % b], 512)
+            if t == 0:
+                mms([(PK[b][:, 64 * a:64 * a + 64], T.sel[:, :, 8 * b + a], T.eq[:], False, False) for a in range(8)], ["sel", "eq"], ["pk%d" % b], 512)
+            for n, (hi, ho) in enumerate(TERMS):
+                mms([(PK[b][:], (T.rp if hi == ho else T.rn)[:], T.mo[:, 1024 * n + 512 * b:1024 * n + 512 * b + 512], False, False)],
+                    [("mo", n, b), "rp", "rn"], ["pk%d" % b], 512)
+        if t == 0:
+            cp(T.til[:, 0:128:16, :], PL[t][:], [("pl", t)], ["til0"], 64)
+        else:
+            tt(T.til[:, 0:128:16, :], PL[t][:], T.eqs[:], A.add, [("pl", t), "eqs"], ["til0"], 64)
+        to_rows("til0")
+        for h in range(2):
+            for b in range(2):
+                lin(T.kw[:, Q(2 * h + b)], PK[b][:], ["pk%d" % b, ("ck", h)], [("kw", 2 * h + b)], 512, bias=CK[h])
+
+    def two_steps(t):
+        dma("y", T.jt[1:128:16, :], T.sb[:, 0], [("sb", 0)], ["jt"])
+        for h in range(2):
+            gather(T.ib[:, H(h)], T.jt[:, 0:2048], LU[t][:, 128 + 64 * h:192 + 64 * h], ["jt", ("lu", t, 1)], [("ib", h)])
+            convert(T.ib, [("ib", h)], h, 1, False)
+        if t == 0:
+            for h in range(2):
+                gather(T.yl[:, H(h)], T.ib[:, 0:2048], jlist(1, h), hk("ib") + [("jl", 1, h)], [("yl", h)])
+                convert(T.yl, [("yl", h)], h, 2, False)
+
+    def rows(dst, dn, src, r, h):
+        dma("y", dst[0:128:8, H(h)], src[0:128:8, H(h)], r, [(dn, h)])
+
+    W = [None, T.w1, T.w2, T.w3, T.w4]
+    off = {}
 
     def astep(t, k):
-        tag[0] = "A%d%d" % (t, k)
-        out, on = (AB[k % 2], "a%d" % (k % 2))
-        win, wk = (AB[(k - 1) % 2], hk("a%d" % ((k - 1) % 2)))
+        K, sg = 3 + t, 2.0 ** (-3 - t)
+        beta = 128.5 + sg / 2
+        xn = "x%d" % (t + 1)
+        if k == 1:
+            off["w"] = 0.0 if t == 0 else 129.0
+        else:
+            win, wk = W[k - 1][:, 0:2048], qk("w%d" % (k - 1))
+        c = 2 * off["w"]
+        if k < 4:
+            off["w"] = -64.0 * 2 ** k if k < 3 else c
+            for h in range(2):
+                if k > 1:
+                    gather(T.gk[:, H(h)], win, jlist(k - 1, h), wk + [("jl", k - 1, h)], [("gk", h)])
+                for q in (2 * h, 2 * h + 1):
+                    a, bank = 512 * (q % 2), (q if k == 3 and t > 0 else q % 2)
+                    if k == 1:
+                        u, v, r = half(X[t], t, h, a, 512), half(T.g1, t, h, a, 512), [partk("x%d" % t, t, h, q % 2), partk("g1", t, h, q % 2)]
+                    else:
+                        u, v, r = W[k - 1][:, Q(q)], T.gk[:, Q(q)], [("w%d" % (k - 1), q), ("gk", h)]
+                    mms([(pa(bank), IDS[t][:], u, True, False), (pa(bank), IDS[t][:], v, False, True)], r + [("ids", t)], [("pa", bank)], 1024)
+                    if k < K:
+                        lin(W[k][:, Q(q)], pa(bank), [("pa", bank)], [("w%d" % k, q)], 512, scale=1 / sg, bias=off["w"] - c)
+                    else:
+                        lin(X[t + 1][:, Q(q)], pa(bank), [("pa", bank)], [(xn, q)], 512, bias=beta - sg * c)
+            return
         for h in range(2):
-            if k == 1:
-                off, lk = (T.lnat[:, 64 * h:64 * h + 64], "lnat") if t == 0 else (LU[t][:, 64 * h:64 * h + 64], "lu%d" % t)
-                tt(out[:, H(h)], X[t][:, 0:2048].indirect(off), own(T.xd, t, h, 0, 1024), A.add, hk("x%d" % t) + hk("xd") + [lk], [(on, h)], 1024, GR)
-            else:
-                tt(out[:, H(h)], win[:, 0:2048].indirect(jlist(k - 1, h)), T.ac[:, H(h)], A.add, wk + [("ac", h), ("jl", k - 1, h)], [(on, h)], 1024, GR)
-            if k < 3 + t:
-                pick(T.ac[:, H(h)], out[:, H(h)], [[0, 1024]], 0, 0, [(on, h)], [("ac", h)], 1024)
-
-    def quant(t):
-        tag[0] = "Q%d" % t
-        K = 3 + t
-        src = AB[K % 2]
-        bias = (129.0 if t == 0 else 0.0) - 0.5 + 2.0 ** (-K - 1)
-        dst = X[t + 1] if t < 2 else T.xq
-        for h in range(2):
-            act(dst[:, H(h)], src[:, H(h)], AF.Copy, [("a%d" % (K % 2), h)], [("x%d" % (t + 1), h)], 1024, bias=bias, scale=2.0 ** -K)
-            if t < 2:
-                send(t + 1, dst, XP[t + 1], h, [("x%d" % (t + 1), h)])
-                dma("y", T.xd[:, H(h)], dst[:, H(h)], [("x%d" % (t + 1), h)], [("xd", h)], 2.6)
-
-    def to_columns(src, r, nb):
-        mms([(T.pt[:, i:16 * nb:16], src[:, i:2048:16], T.selb[:, 0:nb], True, True) for i in range(16)], r + ["selb"], ["pt"], 4096)
+            gather(T.gf[:, H(h)], win, jlist(k - 1, h), wk + [("jl", k - 1, h)], [("gf", h)], sg if k == 4 else 1.0, beta - sg * c if k == K else 0.0)
+            for b in range(2):
+                q = 2 * h + b
+                if k < K:
+                    tt(W[k][:, Q(q)], pa(q), T.gf[:, Q(q)], A.add, [("pa", q), ("gf", h)], [("w%d" % k, q)], 512, 1.0)
+                    mms([(pa(q), T.idf[:], W[k][:, Q(q)], True, True)], [("w%d" % k, q), "idf"], [("pa", q)], 2048)
+                elif t < 2:
+                    tt(X[t + 1][:, Q(q)], pa(q), T.gf[:, Q(q)], A.add, [("pa", q), ("gf", h)], [(xn, q)], 512, 1.0)
+                else:
+                    tt(T.xq[:, 1024 * b + h:1024 * b + 1024:2], pa(q), T.gf[:, Q(q)], A.add, [("pa", q), ("gf", h)], [("xq", b, h)], 512, 1.0)
+        off["w"] = c
+        if k == 5:
+            for b in range(2):
+                lin(T.w1[:, H(b)], T.xq[:, H(b)], [("xq", b, 0), ("xq", b, 1)], qk("w1", b), 1024, bias=-129.0, cv=0.5)
+                dma("y", T.yx[:, H(b)], T.w1[:, H(b)], qk("w1", b), [("yx", b)], 1.0)
 
     def bstep(t, k):
-        tag[0] = "B%d%d" % (t, k)
         K = 3 + t
         out, on = ([T.b0, T.b1][k % 2], "b%d" % (k % 2))
-        win, wn = ([T.b0, T.b1][(k - 1) % 2], "b%d" % ((k - 1) % 2))
-        nb = 16 if t == 2 else 8
-        kk = [("kw", q) for q in range(4)]
+        win, wk = ([T.b0, T.b1][(k - 1) % 2], hk("b%d" % ((k - 1) % 2))) if k > 1 else (T.kw, qk("kw"))
+        sec, sn = (T.ib, "ib") if k == 1 and t > 0 else (T.bc, "bc")
+        if k == 1:
+            for h in range(2):
+                rows(sec, sn, T.kw, qk("kw", h), h)
+            columns(T.kw, qk("kw", 0), 0, 1, 2)
+            ts(T.kcol[:], T.pc0[:, 0:64], 0.5, None, A.max, None, ["pc0"], ["kcol"], 64)
         for h in range(2):
-            if k == 1 and t < 2:
-                tt(out[:, H(h)], T.kw[:, 0:1024].indirect(LU[t][:, 256 + 64 * h:320 + 64 * h]), T.kw[:, H(1)], A.max, kk + ["lu%d" % t], [(on, h)], 1024, GR)
-            elif k == 1:
-                tt(out[:, H(h)], T.kw[:, 0:2048].indirect(LU[t][:, 64 * h:64 * h + 64]), T.bc[:, H(h)], A.max, kk + [("bc", h), "lu%d" % t], [(on, h)], 1024, GR)
-            elif k < K:
-                tt(out[:, H(h)], win[:, 0:2048].indirect(jlist(k - 1, h)), T.bc[:, H(h)], A.max, hk(wn) + [("bc", h), ("jl", k - 1, h)], [(on, h)], 1024, GR)
-            else:
-                act(out[:, H(h)], win[:, 0:2048].indirect(jlist(k - 1, h)), AF.Copy, hk(wn) + [("jl", k - 1, h)], [(on, h)], 1024, GR)
-            if k < K - 1:
-                rows(out[0:128:8, H(h)], [(on, h)], h)
-        if k == K - 1:
-            to_columns(out, hk(on), nb)
-            act(T.tp[:, 0:16 * nb], T.pt[:, 0:16 * nb], AF.Copy, ["pt"], ["tp"], 16 * nb)
-        if k == K:
-            to_columns(out, hk(on), nb)
-            tt(T.tm[:, 0:16 * nb], T.pt[:, 0:16 * nb], T.tp[:, 0:16 * nb], A.max, ["pt", "tp"], ["tm"], 16 * nb, 1.0)
+            lst, lk = (LU[t][:, 64 * h:64 * h + 64], ("lu", t, 0)) if k == 1 else (jlist(k - 1, h), ("jl", k - 1, h))
+            if k == K and t < 2:
+                gather(out[:, H(h)], win[:, 0:2048], lst, wk + [lk], [(on, h)])
+                columns(out, [(on, h)], h, 1, 2)
+                tt(TM[h][:, 1:16:2, :], PCV[h][:, 0:64], TC[h][:, 17:32:2, :], A.max, ["pc%d" % h, ("tc", h)], [("tm", h)], 64, 1.0)
+                continue
+            tt(out[:, H(h)], win[:, 0:2048].indirect(lst), sec[:, H(h)], A.min, wk + [lk, (sn, h)], [(on, h)], 1024, GR)
+            if k == K:
+                columns(out, [(on, h)], h, 1, 3)
+                lin(TM[h][:, 1:32:2, :], PCV[h][:, 0:128], ["pc%d" % h], [("tm", h)], 128)
+                continue
+            if k < K - 1 or t == 2:
+                rows(T.bc, "bc", out, [(on, h)], h)
+            if t > 0 and k > 1:
+                convert(out, [(on, h)], h, k, k == K - 1 and t < 2)
+            elif k == K - 1:
+                columns(out, [(on, h)], h, 1, 2)
+                lin(TC[h][:, 17:32:2, :], PCV[h][:, 0:64], ["pc%d" % h], [("tc", h)], 64)
 
     def merge(t):
-        tag[0] = "M%d" % t
-        n = 128 if t < 2 else 192
-        mms([(T.pj[:, 0:n], T.tm[:, 0:128], T.rd[:, 0:n], True, True)], ["tm", "rd0", "rd1", "rd2"], ["pj"], 4 * n)
-        if t == 2:
-            mms([(T.pk1[:, 0:128], T.tm[:, 128:256], T.idf[:], True, True)], ["tm", "idf"], ["pk1"], 512)
-        ts(T.eq[:], T.pj[:, 0:64], 0.0, None, A.is_equal, None, ["pj"], ["eq"], 64)
-        tt(I(0, 64), T.pj[:, 64:128], T.cv[:], A.max, ["pj", "cv"], ["i0"], 64, 1.0)
-        ts(I(1, 64), I(0, 64), 1023, None, A.bitwise_and, None, ["i0"], ["i1"], 64)
-        tt(Fq(0, 64), I(1, 64), T.vcon[:], A.is_equal, ["i1", "vcon"], ["f0"], 64)
-        tt(T.mm[:], Fq(0, 64), T.eq[:], A.mult, ["f0", "eq"], ["mm"], 64)
+        B0, B1 = TM[0][:, 1:16:2, :], TM[1][:, 1:16:2, :]
+        tt(T.mx[:], B0, B1, A.max, hk("tm"), ["mx"], 64)
+        tt(T.tmm[:, 1:16:2, :], T.mx[:], T.kcol[:], A.is_equal, ["mx", "kcol"], ["tmm"], 64)
+        to_list(T.pc0[:, 0:64], "pc0", T.tmm, "tmm", T.st2b, "st2b", 128)
         if t < 2:
-            nr = 3 - t
-            for q in range(2):
-                tt(T.ht[:, q], T.hd[:, q], T.mm[:], A.mult, ["hd", "mm"], [("ht", q)], 64)
-            tt(T.hl[:, :, 0, :], T.hl[:, :, 0, :], T.ht[:], A.add, hk("ht"), ["hl0", "hl1"], 128)
-            tt(T.hl[:, :, 1, :], T.hl[:, :, 1, :], T.ht[:], A.subtract, hk("ht"), ["hl0", "hl1"], 128)
-            rows_of_su()
-            for q in range(nr):
-                tt(T.st[:, q], T.sd[:, q], T.mm[:], A.mult, ["sd", "mm"], [("st", q)], 64)
-            sk = [("st", q) for q in range(nr)]
-            tt(T.sb[:, 0:nr, 0, :], T.sb[:, 0:nr, 0, :], T.st[:, 0:nr], A.add, sk, ["sb0"], 64 * nr)
-            tt(T.sb[:, 0:nr, 1, :], T.sb[:, 0:nr, 1, :], T.st[:, 0:nr], A.subtract, sk, ["sb1"], 64 * nr)
-            cp(LU[t + 1][:, 0:128 * nr], T.sb[:, 0:nr], ["sb0", "sb1", "sb2"], ["lu%d" % (t + 1)], 128 * nr)
-        if t == 0:
-            act(T.mc[:], T.mm[:], AF.Copy, ["mm"], ["mc"], 64)
-        else:
-            tt(T.mc[:], T.mc[:], T.mm[:], A.max, ["mm"], ["mc"], 64)
-
-    def turn_out(ps, pn, src, r):
-        mms([(ps[0:64, h:256:2], src[:, 64 * h:64 * h + 64], T.idf[:], True, True) for h in range(2)], r + ["idf"], [pn], 1024)
-
-    def store8(y, src, r, name):
-        for q in range(8):
-            dma("y" if q % 2 == 0 else "s", y[q], src[0:64, 32 * q:32 * q + 32], r, [(name, q)])
+            for k in range(2):
+                tt(T.st[:, k], T.pc0[:, 0:64], T.sd[:, k], A.mult, ["pc0", ("sd", k)], [("st", k)], 64, 1.0)
+                tt(T.sb[:, k, 0, :], T.sb[:, k, 0, :], T.st[:, k], A.add, [("st", k)], [("sb", k)], 64)
+                tt(T.sb[:, k, 1, :], T.sb[:, k, 1, :], T.st[:, k], A.subtract, [("st", k), ("sb", k)], [("sc", k)], 64)
+                cp(LU[t + 1][:, 128 * k:128 * k + 128], T.sb[:, k], [("sb", k), ("sc", k)], [("lu", t + 1, k), ("sb", k)], 128)
+            tt(T.eqc[:], B0, B1, A.is_equal, hk("tm"), ["eqc"], 64)
+            lin(T.eqs[:], T.eqc[:], ["eqc"], ["eqs"], 64, scale=-16384.0)
+        tt(T.mc[:], T.pc0[:, 0:64], T.mc[:], A.add, ["pc0"], ["mc"], 64, 1.0)
 
     def finish():
-        tag[0] = "F"
-        cp(T.lv[:], T.pk1[:, 0:128], ["pk1"], ["lv"], 128)
-        tt(I(2, 64), T.lv[:, 0:64], T.lv[:, 64:128], A.max, ["lv"], ["i2"], 64)
-        ts(I(3, 64), I(2, 64), 6, None, A.arith_shift_right, None, ["i2"], ["i3"], 64)
-        ts(I(4, 64), I(2, 64), 63, None, A.bitwise_and, None, ["i2"], ["i4"], 64)
-        tt(T.lh[:, 0:64], I(3, 64), T.mm[:], A.mult, ["i3", "mm"], ["lh0"], 64)
-        tt(T.lh[:, 64:128], I(4, 64), T.mm[:], A.mult, ["i4", "mm"], ["lh1"], 64)
-        dma("y", T.lw[0:128:16, 0:1024], T.lh[:, 0:64], ["lh0"], ["lw0"])
-        dma("s", T.lw[1:128:16, 0:1024], T.lh[:, 64:128], ["lh1"], ["lw1"])
-        ts(I(5), T.pj[:, 64:192], 0.0, None, A.max, None, ["pj"], ["i5"], 128)
-        ts(I(6), I(5), 15, None, A.bitwise_and, None, ["i5"], ["i6"], 128)
-        ts(I(7), I(5), 4, 63, A.arith_shift_right, A.bitwise_and, ["i5"], ["i7"], 128)
-        ts(Fq(1), I(5), 0.0, 1024.0, A.is_equal, A.mult, ["i5"], ["f1"], 128)
-        ts(Fq(2), I(6), 64.0, None, A.mult, None, ["i6"], ["f2"], 128)
-        tt(Fq(3), Fq(1), I(7), A.add, ["f1", "i7"], ["f3"], 128)
-        tt(Fq(4), Fq(2), Fq(3), A.add, ["f2", "f3"], ["f4"], 128)
-        cp(T.ll[:], Fq(4), ["f4"], ["ll"], 128)
-        tt(Fq(5, 64), T.nd[:], T.mc[:], A.mult, ["nd", "mc"], ["f5"], 64)
-        tt(T.nat[:, 0:64], T.nat[:, 0:64], Fq(5, 64), A.add, ["f5"], ["nat"], 64)
-        tt(T.nat[:, 64:128], T.nat[:, 64:128], Fq(5, 64), A.subtract, ["f5"], ["nat1"], 64)
-        turn_out(T.pk0, "pk0", T.nat, ["nat", "nat1"])
-        act(T.osu[0:64, :], T.pk0[0:64, 0:256], AF.Copy, ["pk0"], ["osu"], 256)
-        store8(T.ysu, T.osu, ["osu"], "ysu")
-        turn_out(T.pk1, "pk1", T.lv, ["lv"])
-        act(T.ol0[0:64, :], T.pk1[0:64, 0:256], AF.Copy, ["pk1"], ["ol0"], 256, bias=2048.0, scale=-1.0)
-        lk = ["lw0", "lw1", "lw2", "ll"]
-        cp(T.lg[:, H(0)], T.lw[:, 0:1040].indirect(T.ll[:, 0:64]), lk, [("lg", 0)], 1024, GR)
-        act(T.lg[:, H(1)], T.lw[:, 0:1040].indirect(T.ll[:, 64:128]), AF.Copy, lk, [("lg", 1)], 1024, GR)
+        tt(T.lm[:], TM[0][:, 17:32:2, :], TM[1][:, 17:32:2, :], A.min, hk("tm"), ["lm"], 64)
+        lin(T.eqc[:], T.lm[:], ["lm"], ["eqc"], 64, bias=-2048.0)
+        tt(T.til[:, 8:128:16, :], T.eqc[:], T.tmm[:, 1:16:2, :], A.mult, ["eqc", "tmm"], ["til8"], 64)
+        for b in range(2):
+            mms([(PK[b][:], T.sel[:, 1:9, :], T.sel[:, 0:32, :], True, False)], ["sel"], ["pk%d" % b], 512)
+        to_rows("til8")
+        for b in range(2):
+            lin(T.lw[:, Q(b)], PK[b][:], ["pk%d" % b], [("lw", b)], 512, scale=-1.0 / 2048, bias=2048.0)
         for h in range(2):
-            mms([(T.pt[0:64, 2 * i + h:256:32], T.lg[:, 1024 * h + i:1024 * h + 1024:16], T.selh[:], True, True) for i in range(16)],
-                [("lg", h), "selh"], ["pt"], 1024)
-        tt(T.olb[0:64, :], T.pt[0:64, 0:256], T.ol0[0:64, :], A.min, ["pt", "ol0"], ["olb"], 256, 1.0)
-        store8(T.ylab, T.olb, ["olb"], "ylab")
-
-    def out_x():
-        tag[0] = "X"
-        for c in range(2):
+            to_list(T.pc1[:, 64 * h:64 * h + 64], "pc1", TM[h], ("tm", h), T.st2, "st2", 512)
+        ts(I(0), T.pc1[:, 0:128], -1024.0, None, A.max, None, ["pc1"], [("i", 0)], 128)
+        ts(I(1), I(0), 2047, None, A.bitwise_and, None, [("i", 0)], [("i", 1)], 128)
+        cp(T.ll[:], I(1), [("i", 1)], ["ll"], 128)
+        for b in range(2):
             for h in range(2):
-                act(T.xo[:, 1024 * c + h:1024 * c + 1024:2], T.xq[:, 1024 * h + 512 * c:1024 * h + 512 * c + 512], AF.Copy,
-                    [("x3", h)], [("xo", c, h)], 512, bias=-129.0)
-            dma("y", T.yx[:, H(c)], T.xo[:, H(c)], [("xo", c, 0), ("xo", c, 1)], [("yx", c)], 2.8)
+                tt(T.yl[:, 1024 * b + h:1024 * b + 1024:2], T.lw[:, 0:1032].indirect(T.ll[:, 64 * h + 32 * b:64 * h + 32 * b + 32]), T.b1[:, Q(2 * h + b)],
+                   A.min, hk("lw") + ["lwx", "ll", ("b1", h)] + hk("yl"), [("yo", b, h)], 512, GR)
+            dma("y", T.ylab[:, H(b)], T.yl[8:128:16, H(b)], [("yo", b, 0), ("yo", b, 1)], [("ylab", b)])
+        tt(Fq(0, 64), T.nd[:], T.mc[:], A.mult, ["nd", "mc"], [("f", 0)], 64)
+        tt(Fq(1, 64), T.nat[:, 0:64], Fq(0, 64), A.add, ["nat", ("f", 0)], [("f", 1)], 64)
+        tt(Fq(2, 64), T.nat[:, 64:128], Fq(0, 64), A.subtract, ["nat", ("f", 0)], [("f", 2)], 64)
+        mms([(T.pc0[0:64, h:256:2], Fq(1 + h, 64), T.idf[:], True, True) for h in range(2)], [("f", 1), ("f", 2), "idf"], ["pc0"], 1024)
+        lin(T.osu[0:64, :], T.pc0[0:64, 0:256], ["pc0"], ["osu"], 256)
+        for q in range(8):
+            dma("y" if q % 2 == 0 else "s", T.ysu[q], T.osu[0:64, 32 * q:32 * q + 32], ["osu"], [("ysu", q)])
 
-    gains(0)
     for t in range(3):
         K = 3 + t
-        key(t)
+        two_steps(t)
+        gains(t)
         astep(t, 1)
-        for k in range(1, K):
-            jstep(t, k)
-            astep(t, k + 1)
-        quant(t)
-        if t < 2:
-            gains(t + 1)
-        else:
-            out_x()
         for k in range(1, K + 1):
             bstep(t, k)
+            if k < K:
+                astep(t, k + 1)
         merge(t)
     finish()
     return ops
 
 
+def is_psum(k):
+    return (k[0] if isinstance(k, tuple) else k)[:2] in ("pa", "pk", "pc")
+
+
 def plan_deps(ops):
-    last_w, readers, bank = {}, {}, {}
+    last_w, readers = {}, {}
     for i, o in enumerate(ops):
-        d = set()
+        hard, soft = set(), set()
         for k in set(o["r"] + o["w"]):
-            if k in PSUM:
-                e, cur, before = bank.get(k, (None, [], []))
-                if e == o["e"] and e != "p":
-                    d.update(before)
-                    bank[k] = (e, cur + [i], before)
-                else:
-                    d.update(cur)
-                    bank[k] = (o["e"], [i], cur)
-                continue
             if k in last_w:
-                d.add(last_w[k])
+                hard.add(last_w[k])
             if k in o["w"]:
-                d.update(readers.get(k, []))
-        d.discard(i)
-        o["d"] = d
+                hard.update(readers.get(k, []))
+            elif is_psum(k) and readers.get(k):
+                soft.add(readers[k][-1])
+        o["d"], o["soft"] = hard | soft, soft - hard
         for k in o["r"]:
-            if k not in PSUM:
-                readers.setdefault(k, []).append(i)
+            readers.setdefault(k, []).append(i)
         for k in o["w"]:
-            if k not in PSUM:
-                last_w[k] = i
-                readers[k] = []
+            last_w[k] = i
+            readers[k] = []
     return ops
+
+
+def place(ops, order, before, bias):
+    busy = {e: [] for e in "vspgy"}
+    res = {}
+    for i in order:
+        o = ops[i]
+        pre, post = (0.0, o["lat"]) if before == "d" else (o["lat"], 0.0)
+        ready = max([res[j][0] + WAKE for j in o[before]] or [0.0]) + pre
+        best = (ready, ready, "a")
+        for m, (e, (fn, d)) in enumerate(sorted(o["alt"].items())):
+            s = ready
+            for a, b in busy[e]:
+                if s + d <= a:
+                    break
+                s = max(s, b)
+            if m == 0 or s + d + bias * d < best[0]:
+                best = (s + d, s, e)
+        res[i] = (best[0] + post, best[1], best[2])
+        if best[2] != "a":
+            busy[best[2]].append((best[1], best[0]))
+            busy[best[2]].sort()
+    return res
+
+
+def schedule(ops):
+    n = len(ops)
+    for o in ops:
+        o["u"] = []
+    for i, o in enumerate(ops):
+        for j in o["d"]:
+            ops[j]["u"].append(i)
+    rank = [0.0] * n
+    for i in range(n - 1, -1, -1):
+        o = ops[i]
+        rank[i] = min([a[1] for a in o["alt"].values()] or [0.0]) + o["lat"] + WAKE + max([rank[j] for j in o["u"]] or [0.0])
+    best = None
+    for bias in OPT["bias"]:
+        order = sorted(range(n), key=lambda j: (-rank[j], j))
+        for k in range(OPT["passes"]):
+            res = place(ops, order, "d", bias)
+            span = max(r[0] for r in res.values())
+            if best is None or span < best[0]:
+                best = (span, res)
+            back = place(ops, sorted(range(n), key=lambda j: (-res[j][0], -j)), "u", bias)
+            order = sorted(range(n), key=lambda j: (-back[j][0], j))
+    for i, o in enumerate(ops):
+        o["end"], o["start"], o["e"] = best[1][i]
+    return sorted(range(n), key=lambda j: (ops[j]["start"], j))
 
 
 def rank_program(g, core, T, topo):
@@ -472,7 +500,7 @@ def rank_program(g, core, T, topo):
     if rank is None:
         return
     ops = plan_deps(build(g, core, T, topo, rank))
-    order = ORDER
+    order = schedule(ops)
     Q = {"v": g.vector, "s": g.scalar, "p": g.tensor, "g": g, "y": g.sync}
     CS = {"v": "nv", "s": "ns", "p": "nt", "g": "ng"}
     pos = {i: n for n, i in enumerate(order)}
@@ -482,7 +510,7 @@ def rank_program(g, core, T, topo):
 
     def needs(i, j):
         a, b = ops[i], ops[j]
-        return not (b["k"] == "r" or (a["e"] == "p" and b["e"] == "p"))
+        return not (b["k"] == "r" or (a["e"] == b["e"] and (a["e"] == "p" or j in a["soft"])))
 
     want, seen = {}, {}
     for i in order:
@@ -516,8 +544,6 @@ def rank_program(g, core, T, topo):
         elif o["k"] == "d":
             o["sv"] = ("d%d" % nd, 16)
             nd += 1
-        elif o["k"] == "a":
-            o["sv"] = (o["sem"], sum(ops[j]["nb"] for j in o["d"]))
     sent = 0
     for i in order:
         o = ops[i]
@@ -526,7 +552,7 @@ def rank_program(g, core, T, topo):
         q = Q[o["e"]]
         for j in want[i]:
             q.wait_ge(T.sem[ops[j]["sv"][0]], ops[j]["sv"][1])
-        ins = o["f"]()
+        ins = o["alt"][o["e"]][0]()
         if o["k"] == "r":
             sent += o["n"]
         elif "sv" in o:

@@ -3,33 +3,40 @@ from concourse.mybir import AluOpType, ActivationFunctionType
 F, B16, I32, U16, H16 = "float32", "bfloat16", "int32", "uint16", "float16"
 SCRATCH = {}
 for _names, _shape, _dt in [
-        ("xa xb xc g1 gp gk w1 w2 xq", [128, 2048], B16), ("mo mp", [128, 4096], B16),
-        ("jt ib kw bc b0 b1 w3 w4 gf yl", [128, 2048], F), ("lw", [128, 1032], F),
-        ("sel", [128, 128, 16], B16), ("til", [128, 128, 8], H16), ("vc", [128, 1024], B16),
-        ("idb ids0 ids1 ids2 rp rn vw", [128, 128], B16), ("idh", [128, 128], H16), ("sui labi", [128, 128], I32),
-        ("suf one idf nat io1 st2", [128, 128], F), ("st2b", [128, 128], B16), ("kc", [128, 8], I32), ("col", [128, 16], F),
-        ("selb", [128, 24], F), ("gs", [128, 16], B16), ("prm", [128, 512], F),
-        ("ti", [128, 512], I32), ("tf", [128, 512], F), ("sb", [128, 2, 2, 64], F), ("sd st", [128, 2, 64], F),
-        ("nd mc", [128, 64], F), ("lraw lp0 lp1 lp2 ll", [128, 128], U16), ("lu0 lu1 lu2", [128, 256], U16),
-        ("jl", [128, 512], U16), ("eq", [128, 64], B16), ("tc0 tc1 tm0 tm1", [128, 32, 8], F), ("tmm", [128, 18, 8], B16),
-        ("kcol mx eqc eqs lm", [128, 8, 8], F), ("pt0 pt1 pt2 pl0 pl1 pl2", [128, 64], H16), ("osu", [128, 256], F)]:
+        ("xa xb xc g1 gp gk w1 w2 xq jt j0 j1", [128, 2048], B16), ("mo mp", [128, 4096], B16),
+        ("ib kw bc b0 b1 wa wb ac yl", [128, 2048], F),
+        ("sel", [128, 128, 16], B16), ("til", [128, 130, 8], H16), ("vc", [128, 1024], B16),
+        ("idb idn rp rn vw", [128, 128], B16), ("idh", [128, 128], H16), ("sui labi", [128, 128], I32),
+        ("suf one idf idm nat io1 own", [128, 128], F), ("st2", [128, 256], F), ("st2b", [128, 256], B16), ("kc", [128, 8], I32), ("col", [128, 16], F),
+        ("selb", [128, 24], F), ("tc0 tc1", [128, 18, 8], F), ("zb", [128, 144], B16), ("tp", [128, 2, 128], F), ("kcol", [128, 2, 64], F), ("hl", [128, 2, 128], B16), ("gs", [128, 16], B16), ("prm", [128, 512], F),
+        ("ti", [128, 512], I32), ("tf", [128, 512], F), ("sb sd st", [128, 2, 2, 64], F),
+        ("nd mc", [128, 64], F), ("lraw lp0 lp1 lp2 ll", [128, 128], U16), ("lu0 lu1 lu2", [128, 384], U16),
+        ("jl", [128, 512], U16), ("eq", [128, 64], B16), ("tm0 tm1", [128, 32, 8], F), ("tmm", [128, 18, 8], B16),
+        ("mx eqc eqs lm", [128, 8, 8], F), ("pt0 pt1 pt2 pl0 pl1 pl2", [128, 64], H16), ("osu", [128, 256], F)]:
     for _n in _names.split():
         SCRATCH[_n] = ("sbuf", _shape, _dt)
-for _n, _c in [("pa0", 1024), ("pa1", 1024), ("pk0", 512), ("pk1", 512), ("pc0", 512), ("pc1", 512)]:
-    SCRATCH[_n] = ("psum", [128, _c], F)
+for _k in range(8):
+    SCRATCH["ps%d" % _k] = ("psum", [128, 512], F)
 SEMAPHORES = ["nv", "ns", "nt", "ng", "sent"] + ["al%d" % k for k in range(3)] + ["ap%d" % k for k in range(3)] + ["d%d" % k for k in range(70)]
 
 MASKS = [4, 1, 2]
-GR = 1.56
+GR = 1.62
 CY = 0.83e-3
-PC = 0.42e-3
-WAKE = 0.1
-OPT = {"eng": 2, "dma": 1.8, "rem": 3.0, "bias": [0.3, 0.6, 1.0, 2.0], "passes": 4}
+PC = 0.45e-3
+WAKE = 0.06
+OPT = {"dma": 1.4, "rem": 2.3, "first": 2.4, "pool": 0.3, "gr": GR,
+       "bias": [2.0], "passes": 4, "rounds": 3, "steps": 1200, "back": 50, "near": 0.3, "seed": 1,
+       "bf": [[], [], []],
+       "relu": [["mp", "mo"], ["mp"], ["mp"]],
+       "pe": [2, 2, 3],
+       "ride": [False, True, True]}
+PLAN = {}
 
 
-def build(g, core, T, topo, rank):
+def build(g, core, T, topo, rank, banks):
     A, AF = AluOpType, ActivationFunctionType
     ops = []
+    RIDE, GR = OPT["ride"], OPT["gr"]
 
     def add(alt, r, w, kind="c", lat=0.0):
         ops.append({"alt": alt, "r": list(r), "w": list(w), "k": kind, "lat": lat})
@@ -64,6 +71,10 @@ def build(g, core, T, topo, rank):
             alt["v"] = (lambda: g.vector.tensor_scalar(out, in_, scale, bias, A.mult, A.add), vt(n, cv or c))
         add(alt, r, w)
 
+    def relu(out, in_, r, w, n):
+        add({"s": (lambda: g.scalar.activation(out, in_, AF.Relu), stime(n)),
+             "v": (lambda: g.vector.tensor_scalar(out, in_, 0.0, None, A.max), vt(n))}, r, w)
+
     def mms(lst, r, w, cyc):
         def fn():
             for a in lst:
@@ -86,14 +97,18 @@ def build(g, core, T, topo, rank):
     def pick(out, in_, pat, base, cm, r, w, n):
         add({"g": (lambda: g.affine_select(out, in_, pat, A.is_equal, 0.0, base, cm), 0.17 + 2 * n * CY)}, r, w)
 
+    def copy(out, in_, r, w, n):
+        lin(out, in_, r, w, n)
+        ops[-1]["alt"]["g"] = (lambda: g.affine_select(out, in_, [[0, n]], A.is_equal, 0.0, 0, 0), OPT["pool"] + 2 * n * CY)
+
     def engines(a, b):
-        return topo.engines(a, b)[::OPT["eng"]]
+        return topo.engines(a, b)
 
     def send(t, src, dst, sem, r, key):
         peer = T.cores[rank ^ MASKS[t]]
         rid, pid = topo.addr(peer, core)
         m = sum(1 << e for e in engines(core, peer))
-        add({"g": (lambda: g.remote_dma(dst, src, T.sem[sem], T.sem.sent, pid, rid, m), 2.4 if sem == "al0" else 0.4)}, r, [("snd", sem)], "r", OPT["rem"])
+        add({"g": (lambda: g.remote_dma(dst, src, T.sem[sem], T.sem.sent, pid, rid, m), OPT["first"] if sem == "al0" else 0.4)}, r, [("snd", sem)], "r", OPT["rem"])
         ops[-1]["n"] = len(engines(core, peer))
         add({}, [("snd", sem)], [key], "a")
         ops[-1]["sv"] = (sem, len(engines(peer, core)))
@@ -111,16 +126,18 @@ def build(g, core, T, topo, rank):
         return [(name, q) for q in range(4) if h is None or q // 2 == h]
 
     col = T.col
-    C15, CN15, CA, CB = [col[:, k:k + 1] for k in range(4)]
-    CK = [col[:, 4:5], col[:, 5:6]]
+    C15, CN15, CB, C2 = [col[:, k:k + 1] for k in range(4)]
+    CA, CK = [[col[:, k:k + 1], col[:, k + 1:k + 2]] for k in (4, 6)]
     X, LU, LP = [T.xa, T.xb, T.xc], [T.lu0, T.lu1, T.lu2], [T.lp0, T.lp1, T.lp2]
-    PA, PK, PCV = [T.pa0, T.pa1], [T.pk0, T.pk1], [T.pc0, T.pc1]
-    IDS, TC, TM = [T.ids0, T.ids1, T.ids2], [T.tc0, T.tc1], [T.tm0, T.tm1]
+    TC, TM, JR = [T.tc0, T.tc1], [T.tm0, T.tm1], [T.j0, T.j1]
     PT, PL = [T.pt0, T.pt1, T.pt2], [T.pl0, T.pl1, T.pl2]
     ti, tf = T.ti, T.tf
 
-    def pa(q):
-        return PA[q // 2][:, Q(q % 2)]
+    uses = [0]
+
+    def bank():
+        uses[0] += 1
+        return T["ps%d" % banks.get(uses[0], 0)], ("ps", uses[0])
 
     def I(k, n=128):
         return ti[:, 128 * k:128 * k + n]
@@ -141,36 +158,45 @@ def build(g, core, T, topo, rank):
         pick(T.prm[:, 128 * k:128 * k + 128], T.one[:], [[16, 8], [1000, 2], [2, 8]], k // 2 - 1000 * (k % 2), -1, ["one"], [("prm", k)], 128)
     ms(T.sel[:], 0.0, ["sel"], 2048, 0.5)
     for h in range(2):
-        lin(T.jt[:, H(h)], T.sel[:, 64 * h:64 * h + 64, :], ["sel"], ["jt"], 1024, on="s")
-    cp(T.til[:], T.sel[:, 0:64, :], ["sel"], ["til0", "til8"], 1024, 0.5)
+        lin(T.jt[:, H(h)], T.sel[:, 64 * h:64 * h + 64, :], ["sel"], [("jt", h)], 1024, cv=0.5)
+        ops[-1]["alt"]["g"] = (lambda h=h: g.iota(T.jt[:, H(h)], [[0, 1024]], 0, 0, allow_small_or_imprecise_dtypes=True), 0.2 + 2048 * CY)
+    cp(T.til[:], T.sel[:, 0:65, :], ["sel"], ["til0"] + hk("til"), 1040, 0.5)
     for h in range(2):
-        ms(TC[h][:, 0:18:2, :], 0.0, [("tc", h)], 72)
         ms(TM[h][:, 0:18:2, :], 0.0, [("tm", h)], 72)
+        ms(TC[h][:, 0:18:2, :], 0.0, [("tc", h)], 72)
     ms(T.tmm[:, 0:18:2, :], 0.0, ["tmm"], 72, 0.5)
     lin(T.mc[:], T.sel[:, 0:4, :], ["sel"], ["mc"], 64)
-    lin(T.lw[:, 1024:1032], T.sel[:, 0, 0:8], ["sel"], ["lwx"], 8, bias=4096.0)
     ts(T.kc[:, 4:5], T.kc[:, 0:1], 15, None, A.bitwise_and, None, ["kc0"], ["kc4"], 1)
     cp(C15, T.kc[:, 4:5], ["kc4"], ["c15"], 1)
     lin(CN15, C15, ["c15"], ["cn15"], 1, scale=-1.0)
     ts(T.idb[:], T.io1[:], 0.0, None, A.is_equal, None, ["io1"], ["idb"], 128)
-    for t in range(3):
-        lin(IDS[t][:], T.idb[:], ["idb"], [("ids", t)], 128, scale=2.0 ** (-3 - t), cv=0.5)
     lin(T.idf[:], T.idb[:], ["idb"], ["idf"], 128)
+    lin(T.idm[:], T.idb[:], ["idb"], ["idm"], 128, scale=-1.0)
+    lin(T.idn[:], T.idb[:], ["idb"], ["idn"], 128, scale=-1.0, cv=0.5)
     lin(T.idh[:], T.idb[:], ["idb"], ["idh"], 128, scale=-2048.0, on="v", cv=0.5)
     lin(T.sel[:, 0:128:16, :], T.idb[:], ["idb"], ["sel"], 128, scale=2.0 ** 25, cv=0.5)
     ts(T.rp[:], T.io1[:], CN15, -2048.0, A.is_equal, A.mult, ["io1", "cn15"], ["rp"], 128)
     lin(T.rn[:], T.rp[:], ["rp"], ["rn"], 128, scale=-1.0, cv=0.5)
     lin(T.gs[:, 0:8], T.rp[:, 0:128:16], ["rp"], ["gs0"], 8, scale=-1.0 / 2048)
     lin(T.gs[:, 8:16], T.rp[:, 0:128:16], ["rp"], ["gs1"], 8, scale=1.0 / 2048)
-    for k, (row, wt) in enumerate([(1, 1.0), (0, -1.0), (8, 1.0)]):
-        ts(T.selb[:, 8 * k:8 * k + 8], T.io1[:, 0:128:16], -float(row), wt, A.is_equal, A.mult, ["io1"], [("selb", k)], 8)
-    selk = [("selb", k) for k in range(3)]
-    pick(T.st2[:], T.one[:], [[1, 2], [2, 64]], 0, -1, ["one"], ["st2"], 128)
-    lin(T.st2b[:], T.st2[:], ["st2"], ["st2b"], 128)
-    ts(CA, C15, 0.0, -float(2 ** 23), A.is_equal, A.mult, ["c15"], ["ca"], 1)
-    ts(CB, C15, 1.0, 4096.0, A.is_equal, A.mult, ["c15"], ["cb"], 1)
-    ts(CK[0], CA, CB, None, A.add, None, ["ca", "cb"], [("ck", 0)], 1)
-    ts(CK[1], C15, 8.0, CK[0], A.is_equal, A.add, ["c15", ("ck", 0)], [("ck", 1)], 1)
+    i16 = T.io1[:, 0:128:16]
+    lin(T.zb[:], T.sel[:, 1:10, :], ["sel"], ["zb"], 144, cv=0.5)
+    ts(T.selb[:, 0:8], i16, -1.0, None, A.is_equal, None, ["io1"], [("selb", 0)], 8)
+    ts(T.selb[:, 8:16], i16, -2.0, None, A.is_equal, None, ["io1"], [("selb", 1)], 8)
+    tt(T.selb[:, 16:24], T.selb[:, 0:8], T.selb[:, 8:16], A.add, hk("selb"), [("selb", 2)], 8)
+    lin(T.zb[:, 15:143:16], T.selb[:, 16:24], [("selb", 2)], ["zb"], 8)
+    ts(T.selb[:, 0:8], i16, 0.0, -1.0, A.is_equal, A.mult, ["io1"], [("selb", 0)], 8)
+    ts(T.selb[:, 8:16], i16, -8.0, -1.0, A.is_equal, A.mult, ["io1"], [("selb", 1)], 8)
+    for b in range(2):
+        pick(T.st2[:, 128 * b:128 * b + 128], T.one[:], [[0, 2], [2, 64]], b, -1, ["one"], ["st2"], 128)
+    lin(T.st2b[:], T.st2[:], ["st2"], ["st2b"], 256)
+    ts(CB, C15, 8.0, 6144.0, A.is_lt, A.mult, ["c15"], ["cb"], 1)
+    for h in range(2):
+        ts(CA[h], C15, 0.0, -float(2 ** 23 + 4096 + 2 * h), A.is_equal, A.mult, ["c15"], [("ca", h)], 1)
+        ts(CK[h], CA[h], CB, h - 2048.0, A.add, A.add, ["cb", ("ca", h)], [("ck", h)], 1)
+    iota(T.own[:], [[1, 2], [32, 64]], 0, 0, ["own"], 128)
+    lin(C2, C15, ["c15"], ["c2"], 1, scale=2.0)
+    lin(T.own[:], T.own[:], ["c2"], ["own"], 128, bias=C2)
     iota(T.vc[0:32, :], [[1, 32], [0, 32]], 0, 0, ["vc0"], 1024)
     iota(T.vc[32:64, :], [[0, 32], [1, 32]], 0, 0, ["vc1"], 1024)
     fill(T.vw[0:64, :], 0, ["vw"], 128)
@@ -180,17 +206,22 @@ def build(g, core, T, topo, rank):
         fill(T.bc[:, H(h)], 4096, [("bc", h)], 1024)
 
     lin(T.suf[:], T.sui[:], ["sui"], ["suf"], 128, on="v")
+    p, pk = bank()
     for h in range(2):
-        mms([(T.pc0[:, 64 * h:64 * h + 64], T.prm[:, 128 * (2 * h + b):128 * (2 * h + b) + 128], T.suf[:, b:128:2], b == 0, b == 1) for b in range(2)],
-            ["suf", ("prm", 2 * h), ("prm", 2 * h + 1)], ["pc0"], 512)
-    lin(T.nat[:], T.pc0[:, 0:128], ["pc0"], ["nat"], 128)
+        mms([(p[:, 64 * h:64 * h + 64], T.prm[:, 128 * (2 * h + b):128 * (2 * h + b) + 128], T.suf[:, b:128:2], b == 0, b == 1) for b in range(2)],
+            ["suf", ("prm", 2 * h), ("prm", 2 * h + 1)], [pk], 512)
+    lin(T.nat[:], p[:, 0:128], [pk], ["nat"], 128)
     for k, sh in enumerate([1, 5]):
         lin(I(k), T.nat[:], ["nat"], [("i", k)], 128, scale=2.0 ** -sh, bias=2.0 ** (-sh - 1) - 0.5, on="v")
         lin(Fq(k), T.nat[:], ["nat"], [("f", k)], 128, scale=2048.0 * 2.0 ** -sh)
         lin(Fq(2 + k), I(k), [("i", k)], [("f", 2 + k)], 128, scale=-2047.0, on="v")
         tt(T.sb[:, k], Fq(k), Fq(2 + k), A.add, [("f", k), ("f", 2 + k)], [("sb", k)], 128)
         cp(T.lu0[:, 128 * k:128 * k + 128], T.sb[:, k], [("sb", k)], [("lu", 0, k)], 128)
-        tt(T.sd[:, k], T.sb[:, k, 1, :], T.sb[:, k, 0, :], A.subtract, [("sb", k)], [("sd", k)], 64)
+    if not RIDE[0]:
+        cp(T.lu0[:, 256:384], I(0), [("i", 0)], [("lu", 0, 2)], 128)
+    for k in range(2):
+        tt(T.sd[:, k, 0, :], T.sb[:, k, 1, :], T.sb[:, k, 0, :], A.subtract, [("sb", k)], [("sd", k, 0)], 64)
+        lin(T.sd[:, k, 1, :], T.sd[:, k, 0, :], [("sd", k, 0)], [("sd", k, 1)], 64, scale=-1.0)
     for t in (1, 2):
         send(t, T.lu0[:, 0:128], LP[t][:], "al%d" % t, [("lu", 0, 0)], ("lp", t))
     tt(T.eq[:], T.labi[:, 0:128:2], T.labi[:, 1:128:2], A.is_equal, ["labi"], ["eq"], 64)
@@ -209,33 +240,55 @@ def build(g, core, T, topo, rank):
         return T.jl[:, 128 * (k - 1) + 64 * h:128 * (k - 1) + 64 * h + 64]
 
     def columns(src, sk, h, lo, hi):
-        mms([(PCV[h][:, i:64 * (hi - lo):8], src[:, 1024 * h + i:1024 * h + 1024:8], T.selb[:, 8 * lo:8 * hi], True, True) for i in range(8)],
-            sk + selk, ["pc%d" % h], 2048)
+        p, pk = bank()
+        mms([(p[:, i:64 * (hi - lo):8], src[:, 1024 * h + i:1024 * h + 1024:8], T.selb[:, 8 * lo:8 * hi], True, True) for i in range(8)],
+            sk + qk("selb"), [pk], 2048)
+        return p[:, 0:64 * (hi - lo)], pk
 
-    def to_list(out, on, tile, tk, rhs, rk, cyc):
-        mms([(out, tile[:, 1 - b:17 - b, :], rhs[:, 64 * b:64 * b + 64], b == 0, b == 1) for b in range(2)], [tk, rk], [on], cyc)
+    def to_list(out, on, tile, tk, rhs, rk, n, cyc):
+        mms([(out, tile[:, 1 - b:17 - b, :], rhs[:, 128 * b:128 * b + n], b == 0, b == 1) for b in range(2)], [tk, rk], [on], cyc)
 
-    def convert(src, sk, h, k, keep):
-        n = 2 if keep else 1
-        columns(src, sk, h, 0, n)
-        lin(TC[h][:, 1:16 * n:2, :], PCV[h][:, 0:64 * n], ["pc%d" % h], [("tc", h)], 64 * n)
-        to_list(PCV[h][:, 256:320], "pc%d" % h, TC[h], ("tc", h), T.st2, "st2", 512)
-        cp(jlist(k, h), PCV[h][:, 256:320], ["pc%d" % h], [("jl", k, h)], 64)
+    later = []
 
-    def to_rows(row_key):
-        for b in range(2):
-            mms([(PK[b][:, i:512:8], T.til[:, :, i], T.idh[:, 64 * b:64 * b + 64], False, i == 7) for i in range(8)],
-                ["til0", "til8", "idh"], ["pk%d" % b], 512)
+    def convert(src, sk, h, k, short, keep=0, defer=False):
+        if short:
+            p, pk = bank()
+            mms([(p[:, 0:64], T.zb[:, 15 - i:143 - i], src[:, 1024 * h + i:1024 * h + 1024:16], i == 0, i == 15) for i in range(16)], sk + ["zb"], [pk], 1024)
+        else:
+            c, ck = columns(src, sk, h, 0 if keep else 2, 3)
+            lin(TC[h][:, 1:16:2, :], c[:, 128:192] if keep else c, [ck], [("tc", h)], 64)
+            if keep:
+                lin(T.tp[:, h, 0:64 * keep], c[:, 0:64 * keep], [ck], [("tp", h)], 64 * keep)
+            p, pk = bank()
+            to_list(p[:, 0:64], pk, TC[h], ("tc", h), T.st2, "st2", 64, 512)
+        later.append(lambda r: cp(jlist(k, h), p[:, 0:64], [pk] + r, [("jl", k, h)], 64))
+        if (short and not defer) or h == 0:
+            later.pop()([])
+
+    def to_rows(PK):
+        for b, (p, pk) in enumerate(PK):
+            mms([(p[:, i:512:8], T.til[:, 0:128, i], T.idh[:, 64 * b:64 * b + 64], False, i == 7) for i in range(8)], hk("til") + ["til0", "idh"], [pk], 512)
 
     TERMS = [(0, 0), (1, 0), (1, 1), (0, 1)]
 
     def maxes(t, G, gn, M, mn):
+        xn = "x%d" % t
         for b in range(2):
             for hi in range(2):
-                mms([(pa(2 + hi), T.idb[:], half(X[t], t, hi, 512 * b, 512), True, True)], [partk("x%d" % t, t, hi, b), "idb"], [("pa", 2 + hi)], 512)
+                x = half(X[t], t, hi, 512 * b, 512)
+                diff = OPT["relu"][t].count(mn) >= 2 - hi
+                if not diff:
+                    p, pk = bank()
+                    mms([(p[:], T.idb[:], x, True, True)], [partk(xn, t, hi, b), partk(gn, t, 0, b), "idb"], [pk], 512)
                 for ho in range(2):
-                    n = TERMS.index((hi, ho))
-                    tt(M[:, Q(2 * n + b)], pa(2 + hi), half(G, t, ho, 512 * b, 512), A.max, [("pa", 2 + hi), partk(gn, t, ho, b)], [(mn, n, b)], 512, 1.0)
+                    n, y = TERMS.index((hi, ho)), half(G, t, ho, 512 * b, 512)
+                    if diff:
+                        p, pk = bank()
+                        mms([(p[:], T.idn[:], x, True, False), (p[:], T.idb[:], y, False, True)],
+                            [partk(xn, t, hi, b), partk(gn, t, ho, b), "idb", "idn"], [pk], 1024)
+                        relu(M[:, Q(2 * n + b)], p[:], [pk], [(mn, n, b)], 512)
+                    else:
+                        tt(M[:, Q(2 * n + b)], p[:], y, A.max, [pk, partk(gn, t, ho, b)], [(mn, n, b)], 512, 1.0)
 
     def at_successors(t, G, gn, lst, lk):
         x, xk = X[t][:, 0:2048], qk("x%d" % t)
@@ -254,176 +307,211 @@ def build(g, core, T, topo, rank):
         maxes(t, T.gp, "gp", T.mp, "mp")
         if t > 0:
             maxes(t, T.g1, "g1", T.mo, "mo")
-        mms([(T.pk1[:, 0:64], T.idb[:], T.sel[:, 1:5, :], True, False)], ["idb", "sel"], ["pk1"], 64)
+        p, pk = bank()
         for n, (hi, ho) in enumerate(TERMS):
             s = 0 if hi == ho else 1
-            mms([(T.pk1[:, i:64:8], T.mp[:, 1024 * n + i:1024 * n + 1024:8], T.gs[:, 8 * s:8 * s + 8], False, n == 3 and i == 7) for i in range(8)],
-                [("mp", n, 0), ("mp", n, 1), "gs0", "gs1"], ["pk1"], 512)
-        cp(PT[t][:], T.pk1[:, 0:64], ["pk1"], [("pt", t)], 64)
+            mms([(p[:, 0:64], T.idb[:], T.sel[:, 1:5, :], True, False)][0:1 - min(n, 1)] +
+                [(p[:, i:64:8], T.mp[:, 1024 * n + i:1024 * n + 1024:8], T.gs[:, 8 * s:8 * s + 8], False, n == 3 and i == 7) for i in range(8)],
+                [("mp", n, 0), ("mp", n, 1), "gs0", "gs1", "idb", "sel"] + [pk][0:n % 3], [pk][0:1 - min(n % 3, 1)], 512)
+        cp(PT[t][:], p[:, 0:64], [pk], [("pt", t)], 64)
         send(t, PT[t][:], PL[t][:], "ap%d" % t, [("pt", t)], ("pl", t))
-        for b in range(2):
-            mms([(PK[b][:], T.vw[0:64, :], T.vc[0:64, Q(b)], True, False)], ["vw", "vc0", "vc1"] + qk("vw"), ["pk%d" % b], 512)
+        if t == 2:
+            fill(T.vw[0:1, 0:128:16], -64, [("vw", 0)], 8)
+            fill(T.vw[32:33, 0:128:16], -2, [("vw", 2)], 8)
+        PK = [bank(), bank()]
+        for b, (p, pk) in enumerate(PK):
+            for n in (0, 3, 1, 2):
+                mms([(p[:], (T.rp if n % 2 == 0 else T.rn)[:], T.mo[:, Q(2 * n + b)], n == 0, False)], [("mo", n, b), "rp", "rn"], [pk], 512)
+                if n == 0:
+                    mms([(p[:], T.vw[0:64, :], T.vc[0:64, Q(b)], False, False)], ["vw", "vc0", "vc1"] + qk("vw"), [pk], 512)
             if t == 0:
-                mms([(PK[b][:, 64 * a:64 * a + 64], T.sel[:, :, 8 * b + a], T.eq[:], False, False) for a in range(8)], ["sel", "eq"], ["pk%d" % b], 512)
-            for n, (hi, ho) in enumerate(TERMS):
-                mms([(PK[b][:], (T.rp if hi == ho else T.rn)[:], T.mo[:, 1024 * n + 512 * b:1024 * n + 512 * b + 512], False, False)],
-                    [("mo", n, b), "rp", "rn"], ["pk%d" % b], 512)
+                mms([(p[:, 64 * a:64 * a + 64], T.sel[:, :, 8 * b + a], T.eq[:], False, False) for a in range(8)], ["sel", "eq"], [pk], 512)
         if t == 0:
             cp(T.til[:, 0:128:16, :], PL[t][:], [("pl", t)], ["til0"], 64)
         else:
             tt(T.til[:, 0:128:16, :], PL[t][:], T.eqs[:], A.add, [("pl", t), "eqs"], ["til0"], 64)
-        to_rows("til0")
+        to_rows(PK)
         for h in range(2):
-            for b in range(2):
-                lin(T.kw[:, Q(2 * h + b)], PK[b][:], ["pk%d" % b, ("ck", h)], [("kw", 2 * h + b)], 512, bias=CK[h])
+            for b, (p, pk) in enumerate(PK):
+                j = h * (t // 2)
+                lin(T.kw[:, Q(2 * h + b)], p[:], [pk, ("ck", j)], [("kw", 2 * h + b)], 512, bias=CK[j])
 
-    def two_steps(t):
-        dma("y", T.jt[1:128:16, :], T.sb[:, 0], [("sb", 0)], ["jt"])
-        for h in range(2):
-            gather(T.ib[:, H(h)], T.jt[:, 0:2048], LU[t][:, 128 + 64 * h:192 + 64 * h], ["jt", ("lu", t, 1)], [("ib", h)])
-            convert(T.ib, [("ib", h)], h, 1, False)
-        if t == 0:
+    def doubling(t):
+        lin(T.hl[:, 0], T.sb[:, 0], [("sb", 0)], [("hl", 0)], 128)
+        tt(T.hl[:, 1], T.sb[:, 0], T.hl[:, 0], A.subtract, [("sb", 0), ("hl", 0)], [("hl", 1)], 128)
+        for r in range(2):
+            dma("y", T.jt[1 + r:128:16, :], T.hl[:, r], [("hl", r)] + hk("jt"), [("jr", r)])
+        for k in range(1, 2 if RIDE[t] else 3 + t):
+            out, on = (T.ib, "ib") if RIDE[t] else (JR[k % 2], "j%d" % (k % 2))
             for h in range(2):
-                gather(T.yl[:, H(h)], T.ib[:, 0:2048], jlist(1, h), hk("ib") + [("jl", 1, h)], [("yl", h)])
-                convert(T.yl, [("yl", h)], h, 2, False)
+                if k == 1:
+                    gather(out[:, H(h)], T.jt[:, 0:2048], LU[t][:, 128 + 64 * h:192 + 64 * h], hk("jr") + [("lu", t, 1)], [(on, h)])
+                else:
+                    gather(out[:, H(h)], JR[(k - 1) % 2][:, 0:2048], jlist(k - 1, h), hk("j%d" % ((k - 1) % 2)) + [("jl", k - 1, h)], [(on, h)])
+                convert(out, [(on, h)], h, k, not RIDE[t])
+                if later:
+                    later.pop()([])
 
     def rows(dst, dn, src, r, h):
         dma("y", dst[0:128:8, H(h)], src[0:128:8, H(h)], r, [(dn, h)])
 
-    W = [None, T.w1, T.w2, T.w3, T.w4]
-    off = {}
+    W, WF = [None, T.w1, T.w2], [T.wa, T.wb]
 
     def astep(t, k):
         K, sg = 3 + t, 2.0 ** (-3 - t)
         beta = 128.5 + sg / 2
-        xn = "x%d" % (t + 1)
-        if k == 1:
-            off["w"] = 0.0 if t == 0 else 129.0
-        else:
-            win, wk = W[k - 1][:, 0:2048], qk("w%d" % (k - 1))
-        c = 2 * off["w"]
-        if k < 4:
-            off["w"] = -64.0 * 2 ** k if k < 3 else c
+        xn, m = "x%d" % (t + 1), OPT["pe"][t]
+
+        def window(j):
+            return (W[j], "w%d" % j) if j < m else (WF[j % 2], "wf%d" % (j % 2))
+
+        out, on = window(k)
+        if k > 1:
+            win, wn = window(k - 1)
+        if k <= m:
+            c = (0.0 if t == 0 else 258.0) if k == 1 else -64.0 * 2 ** k
+            scale, bias = (1.0, -64.0 * 2 ** k - c) if k < m else (sg, beta * 2.0 ** (k - K) - sg * c)
             for h in range(2):
                 if k > 1:
-                    gather(T.gk[:, H(h)], win, jlist(k - 1, h), wk + [("jl", k - 1, h)], [("gk", h)])
-                for q in (2 * h, 2 * h + 1):
-                    a, bank = 512 * (q % 2), (q if k == 3 and t > 0 else q % 2)
+                    gather(T.gk[:, H(h)], win[:, 0:2048], jlist(k - 1, h), qk(wn) + [("jl", k - 1, h)], qk("gk", h))
+                for b in range(2):
+                    q = 2 * h + b
                     if k == 1:
-                        u, v, r = half(X[t], t, h, a, 512), half(T.g1, t, h, a, 512), [partk("x%d" % t, t, h, q % 2), partk("g1", t, h, q % 2)]
+                        u, v, r = half(X[t], t, h, 512 * b, 512), half(T.g1, t, h, 512 * b, 512), [partk("x%d" % t, t, h, b), partk("g1", t, h, b)]
                     else:
-                        u, v, r = W[k - 1][:, Q(q)], T.gk[:, Q(q)], [("w%d" % (k - 1), q), ("gk", h)]
-                    mms([(pa(bank), IDS[t][:], u, True, False), (pa(bank), IDS[t][:], v, False, True)], r + [("ids", t)], [("pa", bank)], 1024)
-                    if k < K:
-                        lin(W[k][:, Q(q)], pa(bank), [("pa", bank)], [("w%d" % k, q)], 512, scale=1 / sg, bias=off["w"] - c)
-                    else:
-                        lin(X[t + 1][:, Q(q)], pa(bank), [("pa", bank)], [(xn, q)], 512, bias=beta - sg * c)
-            return
-        for h in range(2):
-            gather(T.gf[:, H(h)], win, jlist(k - 1, h), wk + [("jl", k - 1, h)], [("gf", h)], sg if k == 4 else 1.0, beta - sg * c if k == K else 0.0)
-            for b in range(2):
-                q = 2 * h + b
-                if k < K:
-                    tt(W[k][:, Q(q)], pa(q), T.gf[:, Q(q)], A.add, [("pa", q), ("gf", h)], [("w%d" % k, q)], 512, 1.0)
-                    mms([(pa(q), T.idf[:], W[k][:, Q(q)], True, True)], [("w%d" % k, q), "idf"], [("pa", q)], 2048)
-                elif t < 2:
-                    tt(X[t + 1][:, Q(q)], pa(q), T.gf[:, Q(q)], A.add, [("pa", q), ("gf", h)], [(xn, q)], 512, 1.0)
+                        u, v, r = win[:, Q(q)], T.gk[:, Q(q)], [(wn, q), ("gk", q)]
+                    p, pk = bank()
+                    mms([(p[:], T.idb[:], u, True, False), (p[:], T.idb[:], v, False, True)], r + ["idb"], [pk], 1024)
+                    lin(out[:, Q(q)], p[:], [pk], [(on, q)], 512, scale=scale, bias=bias)
+        else:
+            for h in range(2):
+                r = qk(wn) + [("jl", k - 1, h)]
+                if k < K or t < 2:
+                    dst, dn = (out, on) if k < K else (X[t + 1], xn)
+                    tt(dst[:, H(h)], win[:, 0:2048].indirect(jlist(k - 1, h)), T.ac[:, H(h)], A.add, r + qk("ac", h), qk(dn, h), 1024, GR)
                 else:
-                    tt(T.xq[:, 1024 * b + h:1024 * b + 1024:2], pa(q), T.gf[:, Q(q)], A.add, [("pa", q), ("gf", h)], [("xq", b, h)], 512, 1.0)
-        off["w"] = c
+                    for b in range(2):
+                        tt(T.xq[:, 1024 * b + h:1024 * b + 1024:2], win[:, 0:2048].indirect(jlist(k - 1, h)[:, 32 * b:32 * b + 32]), T.ac[:, Q(2 * h + b)],
+                           A.add, r + [("ac", 2 * h + b)], [("xq", b, h)], 512, GR)
+        if m <= k < K:
+            for h in range(2):
+                copy(T.ac[:, H(h)], out[:, H(h)], qk(on, h), qk("ac", h), 1024)
         if k == 5:
             for b in range(2):
                 lin(T.w1[:, H(b)], T.xq[:, H(b)], [("xq", b, 0), ("xq", b, 1)], qk("w1", b), 1024, bias=-129.0, cv=0.5)
                 dma("y", T.yx[:, H(b)], T.w1[:, H(b)], qk("w1", b), [("yx", b)], 1.0)
 
     def bstep(t, k):
-        K = 3 + t
+        K, n = 3 + t, 1 + t // 2
         out, on = ([T.b0, T.b1][k % 2], "b%d" % (k % 2))
         win, wk = ([T.b0, T.b1][(k - 1) % 2], hk("b%d" % ((k - 1) % 2))) if k > 1 else (T.kw, qk("kw"))
-        sec, sn = (T.ib, "ib") if k == 1 and t > 0 else (T.bc, "bc")
+        sec, sn = (T.ib, "ib") if k == 1 else (T.bc, "bc")
         if k == 1:
-            for h in range(2):
+            for h in range(2 if RIDE[t] else 0):
                 rows(sec, sn, T.kw, qk("kw", h), h)
-            columns(T.kw, qk("kw", 0), 0, 1, 2)
-            ts(T.kcol[:], T.pc0[:, 0:64], 0.5, None, A.max, None, ["pc0"], ["kcol"], 64)
+            c, ck = columns(T.kw, qk("kw", 0), 0, 0, 1)
+            for h in range(n):
+                ts(T.kcol[:, h], c, float(h), 0.5, A.add, A.max, [ck], [("kcol", h)], 64)
         for h in range(2):
             lst, lk = (LU[t][:, 64 * h:64 * h + 64], ("lu", t, 0)) if k == 1 else (jlist(k - 1, h), ("jl", k - 1, h))
-            if k == K and t < 2:
-                gather(out[:, H(h)], win[:, 0:2048], lst, wk + [lk], [(on, h)])
-                columns(out, [(on, h)], h, 1, 2)
-                tt(TM[h][:, 1:16:2, :], PCV[h][:, 0:64], TC[h][:, 17:32:2, :], A.max, ["pc%d" % h, ("tc", h)], [("tm", h)], 64, 1.0)
-                continue
-            tt(out[:, H(h)], win[:, 0:2048].indirect(lst), sec[:, H(h)], A.min, wk + [lk, (sn, h)], [(on, h)], 1024, GR)
+            if len(later) == 1 and (h == 1 or k == K):
+                later.pop()([(on, 0)][0:h])
             if k == K:
-                columns(out, [(on, h)], h, 1, 3)
-                lin(TM[h][:, 1:32:2, :], PCV[h][:, 0:128], ["pc%d" % h], [("tm", h)], 128)
+                gather(out[:, H(h)], win[:, 0:2048], lst, wk + [lk], [(on, h)])
+                c, ck = columns(out, [(on, h)], h, 0, n)
+                tt(TM[h][:, 1:16 * n:2, :], c, T.tp[:, h, 0:64 * n], A.max, [ck, ("tp", h)], [("tm", h)], 64 * n, 1.0)
                 continue
-            if k < K - 1 or t == 2:
+            if k == 1 and not RIDE[t] and t == 0:
+                tt(out[:, H(h)], T.kw[:, H(0)].indirect(LU[t][:, 256 + 64 * h:320 + 64 * h]), T.kw[:, H(1)], A.min, wk + [("lu", t, 2)], [(on, h)], 1024, GR)
+            else:
+                tt(out[:, H(h)], win[:, 0:2048].indirect(lst), sec[:, H(h)], A.min, wk + [lk, (sn, h)], [(on, h)], 1024, GR)
+            if k < K - 1:
                 rows(T.bc, "bc", out, [(on, h)], h)
-            if t > 0 and k > 1:
-                convert(out, [(on, h)], h, k, k == K - 1 and t < 2)
-            elif k == K - 1:
-                columns(out, [(on, h)], h, 1, 2)
-                lin(TC[h][:, 17:32:2, :], PCV[h][:, 0:64], ["pc%d" % h], [("tc", h)], 64)
+            if RIDE[t] and k > 1:
+                if k in OPT["bf"][t]:
+                    lin(T.j0[:, H(h)], out[:, H(h)], [(on, h)], [("j0", h)], 1024)
+                    convert(T.j0, [("j0", h)], h, k, True, 0, True)
+                else:
+                    convert(out, [(on, h)], h, k, False, n if k == K - 1 else 0)
+            if k == K - 1 and (not RIDE[t] or k in OPT["bf"][t]):
+                c, ck = columns(out, [(on, h)], h, 0, n)
+                lin(T.tp[:, h, 0:64 * n], c, [ck], [("tp", h)], 64 * n)
 
     def merge(t):
         B0, B1 = TM[0][:, 1:16:2, :], TM[1][:, 1:16:2, :]
-        tt(T.mx[:], B0, B1, A.max, hk("tm"), ["mx"], 64)
-        tt(T.tmm[:, 1:16:2, :], T.mx[:], T.kcol[:], A.is_equal, ["mx", "kcol"], ["tmm"], 64)
-        to_list(T.pc0[:, 0:64], "pc0", T.tmm, "tmm", T.st2b, "st2b", 128)
+        if t < 2:
+            tt(T.mx[:], B0, B1, A.max, hk("tm"), ["mx"], 64)
+            tt(T.tmm[:, 1:16:2, :], T.mx[:], T.kcol[:, 0], A.is_equal, ["mx", ("kcol", 0)], ["tmm"], 64)
+        else:
+            tt(T.mx[:], B0, T.kcol[:, 0], A.is_equal, [("tm", 0), ("kcol", 0)], ["mx"], 64)
+            tt(T.eqs[:], B1, T.kcol[:, 1], A.is_equal, [("tm", 1), ("kcol", 1)], ["eqs"], 64)
+            tt(T.tmm[:, 1:16:2, :], T.mx[:], T.eqs[:], A.mult, ["mx", "eqs"], ["tmm"], 64)
+        p, pk = bank()
+        to_list(p[:, 0:128], pk, T.tmm, "tmm", T.st2b, "st2b", 128, 256)
         if t < 2:
             for k in range(2):
-                tt(T.st[:, k], T.pc0[:, 0:64], T.sd[:, k], A.mult, ["pc0", ("sd", k)], [("st", k)], 64, 1.0)
-                tt(T.sb[:, k, 0, :], T.sb[:, k, 0, :], T.st[:, k], A.add, [("st", k)], [("sb", k)], 64)
-                tt(T.sb[:, k, 1, :], T.sb[:, k, 1, :], T.st[:, k], A.subtract, [("st", k), ("sb", k)], [("sc", k)], 64)
-                cp(LU[t + 1][:, 128 * k:128 * k + 128], T.sb[:, k], [("sb", k), ("sc", k)], [("lu", t + 1, k), ("sb", k)], 128)
+                tt(T.st[:, k], p[:, 0:128], T.sd[:, k], A.mult, [pk, ("sd", k, 0), ("sd", k, 1)], [("st", k)], 128, 1.0)
+                tt(T.sb[:, k], T.sb[:, k], T.st[:, k], A.add, [("st", k)], [("sb", k)], 128)
+                cp(LU[t + 1][:, 128 * k:128 * k + 128], T.sb[:, k], [("sb", k)], [("lu", t + 1, k)], 128)
             tt(T.eqc[:], B0, B1, A.is_equal, hk("tm"), ["eqc"], 64)
             lin(T.eqs[:], T.eqc[:], ["eqc"], ["eqs"], 64, scale=-16384.0)
-        tt(T.mc[:], T.pc0[:, 0:64], T.mc[:], A.add, ["pc0"], ["mc"], 64, 1.0)
+            tt(T.mc[:], p[:, 0:64], T.mc[:], A.add, [pk], ["mc"], 64, 1.0)
+        if t == 1:
+            tt(Fq(0, 64), T.nd[:], T.mc[:], A.mult, ["nd", "mc"], [("f", 0)], 64)
+            tt(Fq(1, 64), T.nat[:, 0:64], Fq(0, 64), A.add, ["nat", ("f", 0)], [("f", 1)], 64)
+            tt(Fq(2, 64), T.nat[:, 64:128], Fq(0, 64), A.subtract, ["nat", ("f", 0)], [("f", 2)], 64)
+        if t == 2:
+            tt(Fq(3, 64), p[:, 0:64], T.nd[:], A.mult, [pk, "nd"], [("f", 3)], 64, 1.0)
 
     def finish():
-        tt(T.lm[:], TM[0][:, 17:32:2, :], TM[1][:, 17:32:2, :], A.min, hk("tm"), ["lm"], 64)
-        lin(T.eqc[:], T.lm[:], ["lm"], ["eqc"], 64, bias=-2048.0)
-        tt(T.til[:, 8:128:16, :], T.eqc[:], T.tmm[:, 1:16:2, :], A.mult, ["eqc", "tmm"], ["til8"], 64)
-        for b in range(2):
-            mms([(PK[b][:], T.sel[:, 1:9, :], T.sel[:, 0:32, :], True, False)], ["sel"], ["pk%d" % b], 512)
-        to_rows("til8")
-        for b in range(2):
-            lin(T.lw[:, Q(b)], PK[b][:], ["pk%d" % b], [("lw", b)], 512, scale=-1.0 / 2048, bias=2048.0)
+        L = [TM[h][:, 17:32:2, :] for h in range(2)]
+        tt(T.lm[:], L[0], L[1], A.max, hk("tm"), ["lm"], 64)
+        tt(T.eqc[:], T.lm[:], T.tmm[:, 1:16:2, :], A.mult, ["lm", "tmm"], ["eqc"], 64)
         for h in range(2):
-            to_list(T.pc1[:, 64 * h:64 * h + 64], "pc1", TM[h], ("tm", h), T.st2, "st2", 512)
-        ts(I(0), T.pc1[:, 0:128], -1024.0, None, A.max, None, ["pc1"], [("i", 0)], 128)
+            tt(T.til[:, 8 + h:128:16, :], L[h], T.eqc[:], A.max, [("tm", h), "eqc"], [("til", h)], 64)
+        for q in range(4):
+            p, pk = bank()
+            mms([(p[:, 2 * i + h:512:16], T.til[:, h:128 + h, i], T.idh[:, 32 * q:32 * q + 32], True, True) for i in range(8) for h in range(2)],
+                hk("til") + ["til0", "idh"], [pk], 1024)
+            lin(T.kw[:, Q(q)], p[:], [pk], [("kw", q)], 512, scale=1.0 / 2048, bias=2048.0)
+        p, pk = bank()
+        for h in range(2):
+            to_list(p[:, 64 * h:64 * h + 64], pk, TM[h], ("tm", h), T.st2, "st2", 64, 512)
+        tt(I(0), p[:, 0:128], T.own[:], A.max, [pk, "own"], [("i", 0)], 128, 1.0)
         ts(I(1), I(0), 2047, None, A.bitwise_and, None, [("i", 0)], [("i", 1)], 128)
         cp(T.ll[:], I(1), [("i", 1)], ["ll"], 128)
         for b in range(2):
             for h in range(2):
-                tt(T.yl[:, 1024 * b + h:1024 * b + 1024:2], T.lw[:, 0:1032].indirect(T.ll[:, 64 * h + 32 * b:64 * h + 32 * b + 32]), T.b1[:, Q(2 * h + b)],
-                   A.min, hk("lw") + ["lwx", "ll", ("b1", h)] + hk("yl"), [("yo", b, h)], 512, GR)
+                lin(T.yl[:, 1024 * b + h:1024 * b + 1024:2], T.kw[:, 0:2048].indirect(T.ll[:, 64 * h + 32 * b:64 * h + 32 * b + 32]),
+                    qk("kw") + ["ll"], [("yo", b, h)], 512, GR)
             dma("y", T.ylab[:, H(b)], T.yl[8:128:16, H(b)], [("yo", b, 0), ("yo", b, 1)], [("ylab", b)])
-        tt(Fq(0, 64), T.nd[:], T.mc[:], A.mult, ["nd", "mc"], [("f", 0)], 64)
-        tt(Fq(1, 64), T.nat[:, 0:64], Fq(0, 64), A.add, ["nat", ("f", 0)], [("f", 1)], 64)
-        tt(Fq(2, 64), T.nat[:, 64:128], Fq(0, 64), A.subtract, ["nat", ("f", 0)], [("f", 2)], 64)
-        mms([(T.pc0[0:64, h:256:2], Fq(1 + h, 64), T.idf[:], True, True) for h in range(2)], [("f", 1), ("f", 2), "idf"], ["pc0"], 1024)
-        lin(T.osu[0:64, :], T.pc0[0:64, 0:256], ["pc0"], ["osu"], 256)
+        p, pk = bank()
+        mms([(p[0:64, h:256:2], Fq([1 + h, 3][j], 64), (T.idm if j * h else T.idf)[:], j == 0, j == 1) for h in range(2) for j in range(2)],
+            [("f", 1), ("f", 2), ("f", 3), "idf", "idm"], [pk], 2048)
+        lin(T.osu[0:64, :], p[0:64, 0:256], [pk], ["osu"], 256)
         for q in range(8):
-            dma("y" if q % 2 == 0 else "s", T.ysu[q], T.osu[0:64, 32 * q:32 * q + 32], ["osu"], [("ysu", q)])
+            dma("y", T.ysu[q], T.osu[0:64, 32 * q:32 * q + 32], ["osu"], [("ysu", q)], 1.0)
 
     for t in range(3):
         K = 3 + t
-        two_steps(t)
+        doubling(t)
         gains(t)
-        astep(t, 1)
-        for k in range(1, K + 1):
-            bstep(t, k)
-            if k < K:
-                astep(t, k + 1)
+        if RIDE[t]:
+            for k in range(1, K + 1):
+                bstep(t, k)
+                astep(t, k)
+        else:
+            for k in range(1, K + 1):
+                astep(t, k)
+            for k in range(1, K + 1):
+                bstep(t, k)
         merge(t)
     finish()
     return ops
 
 
 def is_psum(k):
-    return (k[0] if isinstance(k, tuple) else k)[:2] in ("pa", "pk", "pc")
+    return k[0] == "ps"
 
 
 def plan_deps(ops):
@@ -435,7 +523,7 @@ def plan_deps(ops):
                 hard.add(last_w[k])
             if k in o["w"]:
                 hard.update(readers.get(k, []))
-            elif is_psum(k) and readers.get(k):
+            elif is_psum(k) and readers.get(k) and "p" not in o["alt"]:
                 soft.add(readers[k][-1])
         o["d"], o["soft"] = hard | soft, soft - hard
         for k in o["r"]:
@@ -446,7 +534,7 @@ def plan_deps(ops):
     return ops
 
 
-def place(ops, order, before, bias):
+def place(ops, order, before, bias, keep=None):
     busy = {e: [] for e in "vspgy"}
     res = {}
     for i in order:
@@ -454,7 +542,7 @@ def place(ops, order, before, bias):
         pre, post = (0.0, o["lat"]) if before == "d" else (o["lat"], 0.0)
         ready = max([res[j][0] + WAKE for j in o[before]] or [0.0]) + pre
         best = (ready, ready, "a")
-        for m, (e, (fn, d)) in enumerate(sorted(o["alt"].items())):
+        for m, (e, (fn, d)) in enumerate(sorted(a for a in o["alt"].items() if keep is None or a[0] == keep[i][2])):
             s = ready
             for a, b in busy[e]:
                 if s + d <= a:
@@ -469,38 +557,190 @@ def place(ops, order, before, bias):
     return res
 
 
-def schedule(ops):
-    n = len(ops)
+def link(ops, extra):
+    for i, j in extra:
+        ops[i]["d"].add(j)
+        ops[i]["soft"].discard(j)
     for o in ops:
         o["u"] = []
     for i, o in enumerate(ops):
         for j in o["d"]:
             ops[j]["u"].append(i)
-    rank = [0.0] * n
-    for i in range(n - 1, -1, -1):
-        o = ops[i]
-        rank[i] = min([a[1] for a in o["alt"].values()] or [0.0]) + o["lat"] + WAKE + max([rank[j] for j in o["u"]] or [0.0])
-    best = None
+
+
+def passes(ops, order):
+    n, best = len(ops), None
     for bias in OPT["bias"]:
-        order = sorted(range(n), key=lambda j: (-rank[j], j))
+        now = order
         for k in range(OPT["passes"]):
-            res = place(ops, order, "d", bias)
+            res = place(ops, now, "d", bias)
             span = max(r[0] for r in res.values())
             if best is None or span < best[0]:
                 best = (span, res)
-            back = place(ops, sorted(range(n), key=lambda j: (-res[j][0], -j)), "u", bias)
-            order = sorted(range(n), key=lambda j: (-back[j][0], j))
+            back = place(ops, sorted(range(n), key=lambda j: (-res[j][0], -res[j][1], -j)), "u", bias)
+            now = sorted(range(n), key=lambda j: (-back[j][0], -back[j][1], j))
+    return best[1]
+
+
+def improve(ops, res, steps):
+    n = len(ops)
+    pre, suc, lag = [list(o["d"]) for o in ops], [o["u"] for o in ops], [o["lat"] + WAKE for o in ops]
+    eng, dur, seq = [0] * n, [0.0] * n, {}
+
+    def take(plan):
+        for i in range(n):
+            eng[i] = plan[i][2]
+            dur[i] = ops[i]["alt"][eng[i]][1] if ops[i]["alt"] else 0.0
+        for e in "vspgy":
+            seq[e] = sorted((i for i in range(n) if eng[i] == e), key=lambda i: (plan[i][1], i))
+
+    def times():
+        mp, mn, hd, r, tl, q = [-1] * n, [-1] * n, [0.0] * n, [0.0] * n, [0.0] * n, [0.0] * n
+        for l in seq.values():
+            for a, b in zip(l, l[1:]):
+                mn[a], mp[b] = b, a
+        left = [len(pre[i]) + (mp[i] >= 0) for i in range(n)]
+        order = [i for i in range(n) if left[i] == 0]
+        for i in order:
+            r[i] = hd[i] if mp[i] < 0 else max(hd[i], r[mp[i]] + dur[mp[i]])
+            e = r[i] + dur[i] + lag[i]
+            for s in suc[i]:
+                if e > hd[s]:
+                    hd[s] = e
+            for s in suc[i] + [mn[i]][0:mn[i] >= 0]:
+                left[s] -= 1
+                if left[s] == 0:
+                    order.append(s)
+        for i in reversed(order):
+            tl[i] = max([lag[i] + q[s] for s in suc[i]] or [lag[i] - WAKE])
+            q[i] = dur[i] + (tl[i] if mn[i] < 0 else max(tl[i], q[mn[i]]))
+        return r, q, hd, tl, mp, mn
+
+    def through(seg, a, b, u, d):
+        t, heads, best = (r[a] + dur[a] if a >= 0 else 0.0), [], 0.0
+        for x in seg:
+            heads.append(max(t, hd[x]))
+            t = heads[-1] + (d if x == u else dur[x])
+        t = q[b] if b >= 0 else 0.0
+        for x, h in zip(reversed(seg), reversed(heads)):
+            t = (d if x == u else dur[x]) + max(t, tl[x])
+            best = max(best, h + t)
+        return best
+
+    take(res)
+    seed, banned, best, since = OPT["seed"], {}, None, 0
+    for it in range(steps):
+        r, q, hd, tl, mp, mn = times()
+        span = max(r[i] + q[i] for i in range(n))
+        if best is None or span < best[0] - 1e-9:
+            best, since = (span, {i: (r[i] + dur[i] + lag[i] - WAKE, r[i], eng[i]) for i in range(n)}), it
+        if it - since > OPT["back"]:
+            since = it
+            take(best[1])
+            continue
+        on = set(i for i in range(n) if r[i] + q[i] > span - 1e-6 and eng[i] != "a")
+        moves = []
+        for u in on:
+            l = seq[eng[u]]
+            j = k = l.index(u)
+            while j + 1 < len(l) and j - k < 6 and l[j + 1] in on and r[l[j + 1]] < r[l[j]] + dur[l[j]] + 1e-6:
+                j += 1
+                if any(q[s] > q[l[j]] or s == l[j] for s in suc[u]):
+                    break
+                moves.append((through(l[k + 1:j + 1] + [u], mp[u], mn[l[j]], u, dur[u]), u, eng[u], j))
+            j = k
+            while j > 0 and k - j < 6 and l[j - 1] in on and r[l[j]] < r[l[j - 1]] + dur[l[j - 1]] + 1e-6:
+                j -= 1
+                if any(r[p] >= r[l[j]] + dur[l[j]] or p == l[j] for p in pre[u]):
+                    break
+                moves.append((through([u] + l[j:k], mp[l[j]], mn[u], u, dur[u]), u, eng[u], j))
+            for e in ops[u]["alt"]:
+                m = seq[e]
+                for j in range(len(m) + 1 if e != eng[u] else 0):
+                    a, b = (m[j - 1] if j > 0 else -1), (m[j] if j < len(m) else -1)
+                    if b >= 0 and r[b] + dur[b] <= hd[u]:
+                        continue
+                    if a >= 0 and q[a] <= tl[u] + dur[a]:
+                        break
+                    moves.append((through([u], a, b, u, ops[u]["alt"][e][1]), u, e, j))
+        if not moves:
+            break
+        seed = (seed * 1103515245 + 12345) % 2147483648
+        ok = [m for m in moves if banned.get(m[1], -1) < it or m[0] < best[0] - 1e-6] or moves
+        low = min(ok)[0] + OPT["near"]
+        ok = sorted(m for m in ok if m[0] <= low)
+        est, u, e, j = ok[(seed >> 8) % len(ok)]
+        banned[u] = it + 15 + seed % 15
+        seq[eng[u]].remove(u)
+        seq[e].insert(j, u)
+        eng[u], dur[u] = e, ops[u]["alt"][e][1]
+    return best[1]
+
+
+def give_banks(ops, res):
+    uses = {}
     for i, o in enumerate(ops):
-        o["end"], o["start"], o["e"] = best[1][i]
-    return sorted(range(n), key=lambda j: (ops[j]["start"], j))
+        for k in o["r"] + o["w"]:
+            if is_psum(k):
+                uses.setdefault(k[1], []).append(i)
+    free, last, banks, extra = [0.0] * 8, [[] for b in range(8)], {}, []
+    for u in sorted(uses, key=lambda u: (res[uses[u][0]][1], u)):
+        start = res[uses[u][0]][1]
+        b = min(range(8), key=lambda b: (max(free[b], start - 1.0), -min(free[b ^ 1], start), b))
+        extra += [(uses[u][0], j) for j in last[b]]
+        banks[u], last[b], free[b] = b, uses[u], max(res[i][0] for i in uses[u])
+    return banks, extra
+
+
+def schedule(g, core, T, topo, rank):
+    if repr(OPT) not in PLAN:
+        ops = plan_deps(build(g, core, T, topo, rank, {}))
+        link(ops, [])
+        n = len(ops)
+        path = [0.0] * n
+        for i in range(n - 1, -1, -1):
+            o = ops[i]
+            path[i] = min([a[1] for a in o["alt"].values()] or [0.0]) + o["lat"] + WAKE + max([path[j] for j in o["u"]] or [0.0])
+        res = passes(ops, sorted(range(n), key=lambda j: (-path[j], j)))
+        best = None
+        for k in range(OPT["rounds"]):
+            banks, extra = give_banks(ops, res)
+            ops = plan_deps(ops)
+            link(ops, extra)
+            res = passes(ops, topological(ops, res)) if k == 0 else place(ops, topological(ops, res), "d", 0.0, res)
+            res = improve(ops, res, OPT["steps"])
+            span = max(r[0] for r in res.values())
+            if best is None or span < best[0]:
+                best = (span, banks, extra, res)
+        PLAN[repr(OPT)] = best[1:]
+    banks, extra, res = PLAN[repr(OPT)]
+    ops = plan_deps(build(g, core, T, topo, rank, banks))
+    link(ops, extra)
+    for i, o in enumerate(ops):
+        o["end"], o["start"], o["e"] = res[i]
+    return ops, sorted(range(len(ops)), key=lambda j: (ops[j]["start"], j))
+
+
+def topological(ops, res):
+    done, order = set(), []
+
+    def visit(i):
+        if i not in done:
+            done.add(i)
+            for j in sorted(ops[i]["d"], key=lambda j: res[j][1]):
+                visit(j)
+            order.append(i)
+
+    for i in sorted(range(len(ops)), key=lambda j: (res[j][1], j)):
+        visit(i)
+    return order
 
 
 def rank_program(g, core, T, topo):
     rank = T.rank_of(core)
     if rank is None:
         return
-    ops = plan_deps(build(g, core, T, topo, rank))
-    order = schedule(ops)
+    ops, order = schedule(g, core, T, topo, rank)
     Q = {"v": g.vector, "s": g.scalar, "p": g.tensor, "g": g, "y": g.sync}
     CS = {"v": "nv", "s": "ns", "p": "nt", "g": "ng"}
     pos = {i: n for n, i in enumerate(order)}

from concourse.mybir import AluOpType, ActivationFunctionType

F, B16, I32, U16, H16 = "float32", "bfloat16", "int32", "uint16", "float16"
SCRATCH = {}
for _names, _shape, _dt in [
        ("xa xb xc g1 gp gk w1 w2 xq jt j0 j1", [128, 2048], B16), ("mo mp", [128, 4096], B16),
        ("ib kw bc b0 b1 wa wb ac yl", [128, 2048], F),
        ("sel", [128, 128, 16], B16), ("til", [128, 130, 8], H16), ("vc", [128, 1024], B16),
        ("idb idn rp rn vw", [128, 128], B16), ("idh", [128, 128], H16), ("sui labi", [128, 128], I32),
        ("suf one idf idm nat io1 own", [128, 128], F), ("st2", [128, 256], F), ("st2b", [128, 256], B16), ("kc", [128, 8], I32), ("col", [128, 16], F),
        ("selb", [128, 24], F), ("tc0 tc1", [128, 18, 8], F), ("zb", [128, 144], B16), ("tp", [128, 2, 128], F), ("kcol", [128, 2, 64], F), ("hl", [128, 2, 128], B16), ("gs", [128, 16], B16), ("prm", [128, 512], F),
        ("ti", [128, 512], I32), ("tf", [128, 512], F), ("sb sd st", [128, 2, 2, 64], F),
        ("nd mc", [128, 64], F), ("lraw lp0 lp1 lp2 ll", [128, 128], U16), ("lu0 lu1 lu2", [128, 384], U16),
        ("jl", [128, 512], U16), ("eq", [128, 64], B16), ("tm0 tm1", [128, 32, 8], F), ("tmm", [128, 18, 8], B16),
        ("mx eqc eqs lm", [128, 8, 8], F), ("pt0 pt1 pt2 pl0 pl1 pl2", [128, 64], H16), ("osu", [128, 256], F)]:
    for _n in _names.split():
        SCRATCH[_n] = ("sbuf", _shape, _dt)
for _k in range(8):
    SCRATCH["ps%d" % _k] = ("psum", [128, 512], F)
SEMAPHORES = ["nv", "ns", "nt", "ng", "sent"] + ["al%d" % k for k in range(3)] + ["ap%d" % k for k in range(3)] + ["d%d" % k for k in range(70)]

MASKS = [4, 1, 2]
GR = 1.62
CY = 0.83e-3
PC = 0.45e-3
WAKE = 0.06
OPT = {"dma": 1.4, "rem": 2.3, "first": 2.4, "pool": 0.3, "gr": GR,
       "bias": [2.0], "passes": 4, "rounds": 3, "steps": 1200, "back": 50, "near": 0.3, "seed": 1,
       "bf": [[], [], []],
       "relu": [["mp", "mo"], ["mp"], ["mp"]],
       "pe": [2, 2, 3],
       "ride": [False, True, True]}
PLAN = {}


def build(g, core, T, topo, rank, banks):
    A, AF = AluOpType, ActivationFunctionType
    ops = []
    RIDE, GR = OPT["ride"], OPT["gr"]

    def add(alt, r, w, kind="c", lat=0.0):
        ops.append({"alt": alt, "r": list(r), "w": list(w), "k": kind, "lat": lat})

    def vt(n, c=1.0):
        return 0.05 + max(64, n * c) * CY

    def stime(n, c=1.0):
        return 0.065 + max(64, n * c) * CY

    def ts(out, in0, s1, s2, o0, o1, r, w, n, c=1.0):
        if o1 is None:
            add({"v": (lambda: g.vector.tensor_scalar(out, in0, s1, None, o0), vt(n, c))}, r, w)
        else:
            add({"v": (lambda: g.vector.tensor_scalar(out, in0, s1, s2, o0, o1), vt(n, c))}, r, w)

    def tt(out, in0, in1, o, r, w, n, c=2.0):
        add({"v": (lambda: g.vector.tensor_tensor(out, in0, in1, o), vt(n, c))}, r, w)

    def cp(out, in_, r, w, n, c=1.0):
        add({"v": (lambda: g.vector.tensor_copy(out, in_), vt(n, c))}, r, w)

    def ms(out, val, w, n, c=1.0):
        add({"v": (lambda: g.vector.memset(out, val), vt(n, c))}, [], w)

    def lin(out, in_, r, w, n, c=1.0, scale=1.0, bias=0.0, on="vs", cv=None):
        alt = {}
        if "s" in on:
            fn = AF.Copy if isinstance(bias, float) else AF.Identity
            alt["s"] = (lambda: g.scalar.activation(out, in_, fn, bias=bias, scale=scale), stime(n, c))
        if "v" in on:
            alt["v"] = (lambda: g.vector.tensor_scalar(out, in_, scale, bias, A.mult, A.add), vt(n, cv or c))
        add(alt, r, w)

    def relu(out, in_, r, w, n):
        add({"s": (lambda: g.scalar.activation(out, in_, AF.Relu), stime(n)),
             "v": (lambda: g.vector.tensor_scalar(out, in_, 0.0, None, A.max), vt(n))}, r, w)

    def mms(lst, r, w, cyc):
        def fn():
            for a in lst:
                ins = g.tensor.matmul(*a)
            return ins
        add({"p": (fn, 0.04 + cyc * PC)}, r, w)

    def dma(q, out, in_, r, w, lat=0.0):
        add({q: (lambda: (g.sync if q == "y" else g.scalar).dma_start(out, in_), 0.06)}, r, w, "d", OPT["dma"] + lat)

    def iota(out, pat, base, cm, w, n, flt=True, r=()):
        if flt:
            add({"g": (lambda: g.iota(out, pat, base, cm, allow_small_or_imprecise_dtypes=True), 0.13 + 2 * n * CY)}, r, w)
        else:
            add({"g": (lambda: g.iota(out, pat, base, cm), 0.13 + 2 * n * CY)}, r, w)

    def fill(out, val, w, n, r=()):
        iota(out, [[0, n]], val, 0, w, n, True, r)

    def pick(out, in_, pat, base, cm, r, w, n):
        add({"g": (lambda: g.affine_select(out, in_, pat, A.is_equal, 0.0, base, cm), 0.17 + 2 * n * CY)}, r, w)

    def copy(out, in_, r, w, n):
        lin(out, in_, r, w, n)
        ops[-1]["alt"]["g"] = (lambda: g.affine_select(out, in_, [[0, n]], A.is_equal, 0.0, 0, 0), OPT["pool"] + 2 * n * CY)

    def engines(a, b):
        return topo.engines(a, b)

    def send(t, src, dst, sem, r, key):
        peer = T.cores[rank ^ MASKS[t]]
        rid, pid = topo.addr(peer, core)
        m = sum(1 << e for e in engines(core, peer))
        add({"g": (lambda: g.remote_dma(dst, src, T.sem[sem], T.sem.sent, pid, rid, m), OPT["first"] if sem == "al0" else 0.4)}, r, [("snd", sem)], "r", OPT["rem"])
        ops[-1]["n"] = len(engines(core, peer))
        add({}, [("snd", sem)], [key], "a")
        ops[-1]["sv"] = (sem, len(engines(peer, core)))

    def H(h):
        return slice(1024 * h, 1024 * h + 1024)

    def Q(q):
        return slice(512 * q, 512 * q + 512)

    def hk(name):
        return [(name, 0), (name, 1)]

    def qk(name, h=None):
        return [(name, q) for q in range(4) if h is None or q // 2 == h]

    col = T.col
    C15, CN15, CB, C2 = [col[:, k:k + 1] for k in range(4)]
    CA, CK = [[col[:, k:k + 1], col[:, k + 1:k + 2]] for k in (4, 6)]
    X, LU, LP = [T.xa, T.xb, T.xc], [T.lu0, T.lu1, T.lu2], [T.lp0, T.lp1, T.lp2]
    TC, TM, JR = [T.tc0, T.tc1], [T.tm0, T.tm1], [T.j0, T.j1]
    PT, PL = [T.pt0, T.pt1, T.pt2], [T.pl0, T.pl1, T.pl2]
    ti, tf = T.ti, T.tf

    uses = [0]

    def bank():
        uses[0] += 1
        return T["ps%d" % banks.get(uses[0], 0)], ("ps", uses[0])

    def I(k, n=128):
        return ti[:, 128 * k:128 * k + n]

    def Fq(k, n=128):
        return tf[:, 128 * k:128 * k + n]

    dma("y", T.sui[:], T.su[:], [], ["sui"])
    dma("s", T.xa[:, H(1)], T.x0[:, H(1)], [], [("x0", 1)], 1.0)
    dma("y", T.xa[:, H(0)], T.x0[:, H(0)], [], [("x0", 0)], 1.0)
    dma("y", T.labi[:], T.lab[:], [], ["labi"], 0.5)
    cp(T.lraw[:], T.sui[:], ["sui"], ["lraw"], 128)
    send(0, T.lraw[:], T.lp0[:], "al0", ["lraw"], ("lp", 0))
    iota(T.kc[:, 0:1], [[1, 1]], 0, 1, ["kc0"], 1, False)
    iota(T.io1[:], [[1, 128]], 0, -1, ["io1"], 128)
    ms(T.one[:], 1.0, ["one"], 128)
    for k in range(4):
        pick(T.prm[:, 128 * k:128 * k + 128], T.one[:], [[16, 8], [1000, 2], [2, 8]], k // 2 - 1000 * (k % 2), -1, ["one"], [("prm", k)], 128)
    ms(T.sel[:], 0.0, ["sel"], 2048, 0.5)
    for h in range(2):
        lin(T.jt[:, H(h)], T.sel[:, 64 * h:64 * h + 64, :], ["sel"], [("jt", h)], 1024, cv=0.5)
        ops[-1]["alt"]["g"] = (lambda h=h: g.iota(T.jt[:, H(h)], [[0, 1024]], 0, 0, allow_small_or_imprecise_dtypes=True), 0.2 + 2048 * CY)
    cp(T.til[:], T.sel[:, 0:65, :], ["sel"], ["til0"] + hk("til"), 1040, 0.5)
    for h in range(2):
        ms(TM[h][:, 0:18:2, :], 0.0, [("tm", h)], 72)
        ms(TC[h][:, 0:18:2, :], 0.0, [("tc", h)], 72)
    ms(T.tmm[:, 0:18:2, :], 0.0, ["tmm"], 72, 0.5)
    lin(T.mc[:], T.sel[:, 0:4, :], ["sel"], ["mc"], 64)
    ts(T.kc[:, 4:5], T.kc[:, 0:1], 15, None, A.bitwise_and, None, ["kc0"], ["kc4"], 1)
    cp(C15, T.kc[:, 4:5], ["kc4"], ["c15"], 1)
    lin(CN15, C15, ["c15"], ["cn15"], 1, scale=-1.0)
    ts(T.idb[:], T.io1[:], 0.0, None, A.is_equal, None, ["io1"], ["idb"], 128)
    lin(T.idf[:], T.idb[:], ["idb"], ["idf"], 128)
    lin(T.idm[:], T.idb[:], ["idb"], ["idm"], 128, scale=-1.0)
    lin(T.idn[:], T.idb[:], ["idb"], ["idn"], 128, scale=-1.0, cv=0.5)
    lin(T.idh[:], T.idb[:], ["idb"], ["idh"], 128, scale=-2048.0, on="v", cv=0.5)
    lin(T.sel[:, 0:128:16, :], T.idb[:], ["idb"], ["sel"], 128, scale=2.0 ** 25, cv=0.5)
    ts(T.rp[:], T.io1[:], CN15, -2048.0, A.is_equal, A.mult, ["io1", "cn15"], ["rp"], 128)
    lin(T.rn[:], T.rp[:], ["rp"], ["rn"], 128, scale=-1.0, cv=0.5)
    lin(T.gs[:, 0:8], T.rp[:, 0:128:16], ["rp"], ["gs0"], 8, scale=-1.0 / 2048)
    lin(T.gs[:, 8:16], T.rp[:, 0:128:16], ["rp"], ["gs1"], 8, scale=1.0 / 2048)
    i16 = T.io1[:, 0:128:16]
    lin(T.zb[:], T.sel[:, 1:10, :], ["sel"], ["zb"], 144, cv=0.5)
    ts(T.selb[:, 0:8], i16, -1.0, None, A.is_equal, None, ["io1"], [("selb", 0)], 8)
    ts(T.selb[:, 8:16], i16, -2.0, None, A.is_equal, None, ["io1"], [("selb", 1)], 8)
    tt(T.selb[:, 16:24], T.selb[:, 0:8], T.selb[:, 8:16], A.add, hk("selb"), [("selb", 2)], 8)
    lin(T.zb[:, 15:143:16], T.selb[:, 16:24], [("selb", 2)], ["zb"], 8)
    ts(T.selb[:, 0:8], i16, 0.0, -1.0, A.is_equal, A.mult, ["io1"], [("selb", 0)], 8)
    ts(T.selb[:, 8:16], i16, -8.0, -1.0, A.is_equal, A.mult, ["io1"], [("selb", 1)], 8)
    for b in range(2):
        pick(T.st2[:, 128 * b:128 * b + 128], T.one[:], [[0, 2], [2, 64]], b, -1, ["one"], ["st2"], 128)
    lin(T.st2b[:], T.st2[:], ["st2"], ["st2b"], 256)
    ts(CB, C15, 8.0, 6144.0, A.is_lt, A.mult, ["c15"], ["cb"], 1)
    for h in range(2):
        ts(CA[h], C15, 0.0, -float(2 ** 23 + 4096 + 2 * h), A.is_equal, A.mult, ["c15"], [("ca", h)], 1)
        ts(CK[h], CA[h], CB, h - 2048.0, A.add, A.add, ["cb", ("ca", h)], [("ck", h)], 1)
    iota(T.own[:], [[1, 2], [32, 64]], 0, 0, ["own"], 128)
    lin(C2, C15, ["c15"], ["c2"], 1, scale=2.0)
    lin(T.own[:], T.own[:], ["c2"], ["own"], 128, bias=C2)
    iota(T.vc[0:32, :], [[1, 32], [0, 32]], 0, 0, ["vc0"], 1024)
    iota(T.vc[32:64, :], [[0, 32], [1, 32]], 0, 0, ["vc1"], 1024)
    fill(T.vw[0:64, :], 0, ["vw"], 128)
    for k, (p, c, val) in enumerate([(0, 0, -32), (0, 8, 64), (32, 0, -1), (32, 8, 2)]):
        fill(T.vw[p:p + 1, c:128:16], val, [("vw", k)], 8, ["vw"])
    for h in range(2):
        fill(T.bc[:, H(h)], 4096, [("bc", h)], 1024)

    lin(T.suf[:], T.sui[:], ["sui"], ["suf"], 128, on="v")
    p, pk = bank()
    for h in range(2):
        mms([(p[:, 64 * h:64 * h + 64], T.prm[:, 128 * (2 * h + b):128 * (2 * h + b) + 128], T.suf[:, b:128:2], b == 0, b == 1) for b in range(2)],
            ["suf", ("prm", 2 * h), ("prm", 2 * h + 1)], [pk], 512)
    lin(T.nat[:], p[:, 0:128], [pk], ["nat"], 128)
    for k, sh in enumerate([1, 5]):
        lin(I(k), T.nat[:], ["nat"], [("i", k)], 128, scale=2.0 ** -sh, bias=2.0 ** (-sh - 1) - 0.5, on="v")
        lin(Fq(k), T.nat[:], ["nat"], [("f", k)], 128, scale=2048.0 * 2.0 ** -sh)
        lin(Fq(2 + k), I(k), [("i", k)], [("f", 2 + k)], 128, scale=-2047.0, on="v")
        tt(T.sb[:, k], Fq(k), Fq(2 + k), A.add, [("f", k), ("f", 2 + k)], [("sb", k)], 128)
        cp(T.lu0[:, 128 * k:128 * k + 128], T.sb[:, k], [("sb", k)], [("lu", 0, k)], 128)
    if not RIDE[0]:
        cp(T.lu0[:, 256:384], I(0), [("i", 0)], [("lu", 0, 2)], 128)
    for k in range(2):
        tt(T.sd[:, k, 0, :], T.sb[:, k, 1, :], T.sb[:, k, 0, :], A.subtract, [("sb", k)], [("sd", k, 0)], 64)
        lin(T.sd[:, k, 1, :], T.sd[:, k, 0, :], [("sd", k, 0)], [("sd", k, 1)], 64, scale=-1.0)
    for t in (1, 2):
        send(t, T.lu0[:, 0:128], LP[t][:], "al%d" % t, [("lu", 0, 0)], ("lp", t))
    tt(T.eq[:], T.labi[:, 0:128:2], T.labi[:, 1:128:2], A.is_equal, ["labi"], ["eq"], 64)
    tt(T.nd[:], T.nat[:, 64:128], T.nat[:, 0:64], A.subtract, ["nat"], ["nd"], 64)

    def half(x, t, h, a=0, n=1024):
        return x[:, 2 * a + h:2 * (a + n):2] if t == 0 else x[:, 1024 * h + a:1024 * h + a + n]

    def partk(name, t, h, b):
        return (name, b if t == 0 else 2 * h + b)

    def gather(out, win, off, r, w, scale=1.0, bias=0.0):
        lin(out, win.indirect(off), r, w, 1024, GR, scale, bias)

    def jlist(k, h):
        return T.jl[:, 128 * (k - 1) + 64 * h:128 * (k - 1) + 64 * h + 64]

    def columns(src, sk, h, lo, hi):
        p, pk = bank()
        mms([(p[:, i:64 * (hi - lo):8], src[:, 1024 * h + i:1024 * h + 1024:8], T.selb[:, 8 * lo:8 * hi], True, True) for i in range(8)],
            sk + qk("selb"), [pk], 2048)
        return p[:, 0:64 * (hi - lo)], pk

    def to_list(out, on, tile, tk, rhs, rk, n, cyc):
        mms([(out, tile[:, 1 - b:17 - b, :], rhs[:, 128 * b:128 * b + n], b == 0, b == 1) for b in range(2)], [tk, rk], [on], cyc)

    later = []

    def convert(src, sk, h, k, short, keep=0, defer=False):
        if short:
            p, pk = bank()
            mms([(p[:, 0:64], T.zb[:, 15 - i:143 - i], src[:, 1024 * h + i:1024 * h + 1024:16], i == 0, i == 15) for i in range(16)], sk + ["zb"], [pk], 1024)
        else:
            c, ck = columns(src, sk, h, 0 if keep else 2, 3)
            lin(TC[h][:, 1:16:2, :], c[:, 128:192] if keep else c, [ck], [("tc", h)], 64)
            if keep:
                lin(T.tp[:, h, 0:64 * keep], c[:, 0:64 * keep], [ck], [("tp", h)], 64 * keep)
            p, pk = bank()
            to_list(p[:, 0:64], pk, TC[h], ("tc", h), T.st2, "st2", 64, 512)
        later.append(lambda r: cp(jlist(k, h), p[:, 0:64], [pk] + r, [("jl", k, h)], 64))
        if (short and not defer) or h == 0:
            later.pop()([])

    def to_rows(PK):
        for b, (p, pk) in enumerate(PK):
            mms([(p[:, i:512:8], T.til[:, 0:128, i], T.idh[:, 64 * b:64 * b + 64], False, i == 7) for i in range(8)], hk("til") + ["til0", "idh"], [pk], 512)

    TERMS = [(0, 0), (1, 0), (1, 1), (0, 1)]

    def maxes(t, G, gn, M, mn):
        xn = "x%d" % t
        for b in range(2):
            for hi in range(2):
                x = half(X[t], t, hi, 512 * b, 512)
                diff = OPT["relu"][t].count(mn) >= 2 - hi
                if not diff:
                    p, pk = bank()
                    mms([(p[:], T.idb[:], x, True, True)], [partk(xn, t, hi, b), partk(gn, t, 0, b), "idb"], [pk], 512)
                for ho in range(2):
                    n, y = TERMS.index((hi, ho)), half(G, t, ho, 512 * b, 512)
                    if diff:
                        p, pk = bank()
                        mms([(p[:], T.idn[:], x, True, False), (p[:], T.idb[:], y, False, True)],
                            [partk(xn, t, hi, b), partk(gn, t, ho, b), "idb", "idn"], [pk], 1024)
                        relu(M[:, Q(2 * n + b)], p[:], [pk], [(mn, n, b)], 512)
                    else:
                        tt(M[:, Q(2 * n + b)], p[:], y, A.max, [pk, partk(gn, t, ho, b)], [(mn, n, b)], 512, 1.0)

    def at_successors(t, G, gn, lst, lk):
        x, xk = X[t][:, 0:2048], qk("x%d" % t)
        for b in range(2):
            if t == 0:
                gather(G[:, H(b)], x, lst[:, 64 * b:64 * b + 64], xk + [lk], [(gn, b)])
            else:
                for q in (b, 2 + b):
                    lin(G[:, Q(q)], x.indirect(lst[:, 32 * q:32 * q + 32]), xk + [lk], [(gn, q)], 512, GR)

    def gains(t):
        at_successors(t, T.g1, "g1", T.lraw if t == 0 else LU[t], "lraw" if t == 0 else ("lu", t, 0))
        at_successors(t, T.gp, "gp", LP[t], ("lp", t))
        if t == 0:
            maxes(t, T.g1, "g1", T.mo, "mo")
        maxes(t, T.gp, "gp", T.mp, "mp")
        if t > 0:
            maxes(t, T.g1, "g1", T.mo, "mo")
        p, pk = bank()
        for n, (hi, ho) in enumerate(TERMS):
            s = 0 if hi == ho else 1
            mms([(p[:, 0:64], T.idb[:], T.sel[:, 1:5, :], True, False)][0:1 - min(n, 1)] +
                [(p[:, i:64:8], T.mp[:, 1024 * n + i:1024 * n + 1024:8], T.gs[:, 8 * s:8 * s + 8], False, n == 3 and i == 7) for i in range(8)],
                [("mp", n, 0), ("mp", n, 1), "gs0", "gs1", "idb", "sel"] + [pk][0:n % 3], [pk][0:1 - min(n % 3, 1)], 512)
        cp(PT[t][:], p[:, 0:64], [pk], [("pt", t)], 64)
        send(t, PT[t][:], PL[t][:], "ap%d" % t, [("pt", t)], ("pl", t))
        if t == 2:
            fill(T.vw[0:1, 0:128:16], -64, [("vw", 0)], 8)
            fill(T.vw[32:33, 0:128:16], -2, [("vw", 2)], 8)
        PK = [bank(), bank()]
        for b, (p, pk) in enumerate(PK):
            for n in (0, 3, 1, 2):
                mms([(p[:], (T.rp if n % 2 == 0 else T.rn)[:], T.mo[:, Q(2 * n + b)], n == 0, False)], [("mo", n, b), "rp", "rn"], [pk], 512)
                if n == 0:
                    mms([(p[:], T.vw[0:64, :], T.vc[0:64, Q(b)], False, False)], ["vw", "vc0", "vc1"] + qk("vw"), [pk], 512)
            if t == 0:
                mms([(p[:, 64 * a:64 * a + 64], T.sel[:, :, 8 * b + a], T.eq[:], False, False) for a in range(8)], ["sel", "eq"], [pk], 512)
        if t == 0:
            cp(T.til[:, 0:128:16, :], PL[t][:], [("pl", t)], ["til0"], 64)
        else:
            tt(T.til[:, 0:128:16, :], PL[t][:], T.eqs[:], A.add, [("pl", t), "eqs"], ["til0"], 64)
        to_rows(PK)
        for h in range(2):
            for b, (p, pk) in enumerate(PK):
                j = h * (t // 2)
                lin(T.kw[:, Q(2 * h + b)], p[:], [pk, ("ck", j)], [("kw", 2 * h + b)], 512, bias=CK[j])

    def doubling(t):
        lin(T.hl[:, 0], T.sb[:, 0], [("sb", 0)], [("hl", 0)], 128)
        tt(T.hl[:, 1], T.sb[:, 0], T.hl[:, 0], A.subtract, [("sb", 0), ("hl", 0)], [("hl", 1)], 128)
        for r in range(2):
            dma("y", T.jt[1 + r:128:16, :], T.hl[:, r], [("hl", r)] + hk("jt"), [("jr", r)])
        for k in range(1, 2 if RIDE[t] else 3 + t):
            out, on = (T.ib, "ib") if RIDE[t] else (JR[k % 2], "j%d" % (k % 2))
            for h in range(2):
                if k == 1:
                    gather(out[:, H(h)], T.jt[:, 0:2048], LU[t][:, 128 + 64 * h:192 + 64 * h], hk("jr") + [("lu", t, 1)], [(on, h)])
                else:
                    gather(out[:, H(h)], JR[(k - 1) % 2][:, 0:2048], jlist(k - 1, h), hk("j%d" % ((k - 1) % 2)) + [("jl", k - 1, h)], [(on, h)])
                convert(out, [(on, h)], h, k, not RIDE[t])
                if later:
                    later.pop()([])

    def rows(dst, dn, src, r, h):
        dma("y", dst[0:128:8, H(h)], src[0:128:8, H(h)], r, [(dn, h)])

    W, WF = [None, T.w1, T.w2], [T.wa, T.wb]

    def astep(t, k):
        K, sg = 3 + t, 2.0 ** (-3 - t)
        beta = 128.5 + sg / 2
        xn, m = "x%d" % (t + 1), OPT["pe"][t]

        def window(j):
            return (W[j], "w%d" % j) if j < m else (WF[j % 2], "wf%d" % (j % 2))

        out, on = window(k)
        if k > 1:
            win, wn = window(k - 1)
        if k <= m:
            c = (0.0 if t == 0 else 258.0) if k == 1 else -64.0 * 2 ** k
            scale, bias = (1.0, -64.0 * 2 ** k - c) if k < m else (sg, beta * 2.0 ** (k - K) - sg * c)
            for h in range(2):
                if k > 1:
                    gather(T.gk[:, H(h)], win[:, 0:2048], jlist(k - 1, h), qk(wn) + [("jl", k - 1, h)], qk("gk", h))
                for b in range(2):
                    q = 2 * h + b
                    if k == 1:
                        u, v, r = half(X[t], t, h, 512 * b, 512), half(T.g1, t, h, 512 * b, 512), [partk("x%d" % t, t, h, b), partk("g1", t, h, b)]
                    else:
                        u, v, r = win[:, Q(q)], T.gk[:, Q(q)], [(wn, q), ("gk", q)]
                    p, pk = bank()
                    mms([(p[:], T.idb[:], u, True, False), (p[:], T.idb[:], v, False, True)], r + ["idb"], [pk], 1024)
                    lin(out[:, Q(q)], p[:], [pk], [(on, q)], 512, scale=scale, bias=bias)
        else:
            for h in range(2):
                r = qk(wn) + [("jl", k - 1, h)]
                if k < K or t < 2:
                    dst, dn = (out, on) if k < K else (X[t + 1], xn)
                    tt(dst[:, H(h)], win[:, 0:2048].indirect(jlist(k - 1, h)), T.ac[:, H(h)], A.add, r + qk("ac", h), qk(dn, h), 1024, GR)
                else:
                    for b in range(2):
                        tt(T.xq[:, 1024 * b + h:1024 * b + 1024:2], win[:, 0:2048].indirect(jlist(k - 1, h)[:, 32 * b:32 * b + 32]), T.ac[:, Q(2 * h + b)],
                           A.add, r + [("ac", 2 * h + b)], [("xq", b, h)], 512, GR)
        if m <= k < K:
            for h in range(2):
                copy(T.ac[:, H(h)], out[:, H(h)], qk(on, h), qk("ac", h), 1024)
        if k == 5:
            for b in range(2):
                lin(T.w1[:, H(b)], T.xq[:, H(b)], [("xq", b, 0), ("xq", b, 1)], qk("w1", b), 1024, bias=-129.0, cv=0.5)
                dma("y", T.yx[:, H(b)], T.w1[:, H(b)], qk("w1", b), [("yx", b)], 1.0)

    def bstep(t, k):
        K, n = 3 + t, 1 + t // 2
        out, on = ([T.b0, T.b1][k % 2], "b%d" % (k % 2))
        win, wk = ([T.b0, T.b1][(k - 1) % 2], hk("b%d" % ((k - 1) % 2))) if k > 1 else (T.kw, qk("kw"))
        sec, sn = (T.ib, "ib") if k == 1 else (T.bc, "bc")
        if k == 1:
            for h in range(2 if RIDE[t] else 0):
                rows(sec, sn, T.kw, qk("kw", h), h)
            c, ck = columns(T.kw, qk("kw", 0), 0, 0, 1)
            for h in range(n):
                ts(T.kcol[:, h], c, float(h), 0.5, A.add, A.max, [ck], [("kcol", h)], 64)
        for h in range(2):
            lst, lk = (LU[t][:, 64 * h:64 * h + 64], ("lu", t, 0)) if k == 1 else (jlist(k - 1, h), ("jl", k - 1, h))
            if len(later) == 1 and (h == 1 or k == K):
                later.pop()([(on, 0)][0:h])
            if k == K:
                gather(out[:, H(h)], win[:, 0:2048], lst, wk + [lk], [(on, h)])
                c, ck = columns(out, [(on, h)], h, 0, n)
                tt(TM[h][:, 1:16 * n:2, :], c, T.tp[:, h, 0:64 * n], A.max, [ck, ("tp", h)], [("tm", h)], 64 * n, 1.0)
                continue
            if k == 1 and not RIDE[t] and t == 0:
                tt(out[:, H(h)], T.kw[:, H(0)].indirect(LU[t][:, 256 + 64 * h:320 + 64 * h]), T.kw[:, H(1)], A.min, wk + [("lu", t, 2)], [(on, h)], 1024, GR)
            else:
                tt(out[:, H(h)], win[:, 0:2048].indirect(lst), sec[:, H(h)], A.min, wk + [lk, (sn, h)], [(on, h)], 1024, GR)
            if k < K - 1:
                rows(T.bc, "bc", out, [(on, h)], h)
            if RIDE[t] and k > 1:
                if k in OPT["bf"][t]:
                    lin(T.j0[:, H(h)], out[:, H(h)], [(on, h)], [("j0", h)], 1024)
                    convert(T.j0, [("j0", h)], h, k, True, 0, True)
                else:
                    convert(out, [(on, h)], h, k, False, n if k == K - 1 else 0)
            if k == K - 1 and (not RIDE[t] or k in OPT["bf"][t]):
                c, ck = columns(out, [(on, h)], h, 0, n)
                lin(T.tp[:, h, 0:64 * n], c, [ck], [("tp", h)], 64 * n)

    def merge(t):
        B0, B1 = TM[0][:, 1:16:2, :], TM[1][:, 1:16:2, :]
        if t < 2:
            tt(T.mx[:], B0, B1, A.max, hk("tm"), ["mx"], 64)
            tt(T.tmm[:, 1:16:2, :], T.mx[:], T.kcol[:, 0], A.is_equal, ["mx", ("kcol", 0)], ["tmm"], 64)
        else:
            tt(T.mx[:], B0, T.kcol[:, 0], A.is_equal, [("tm", 0), ("kcol", 0)], ["mx"], 64)
            tt(T.eqs[:], B1, T.kcol[:, 1], A.is_equal, [("tm", 1), ("kcol", 1)], ["eqs"], 64)
            tt(T.tmm[:, 1:16:2, :], T.mx[:], T.eqs[:], A.mult, ["mx", "eqs"], ["tmm"], 64)
        p, pk = bank()
        to_list(p[:, 0:128], pk, T.tmm, "tmm", T.st2b, "st2b", 128, 256)
        if t < 2:
            for k in range(2):
                tt(T.st[:, k], p[:, 0:128], T.sd[:, k], A.mult, [pk, ("sd", k, 0), ("sd", k, 1)], [("st", k)], 128, 1.0)
                tt(T.sb[:, k], T.sb[:, k], T.st[:, k], A.add, [("st", k)], [("sb", k)], 128)
                cp(LU[t + 1][:, 128 * k:128 * k + 128], T.sb[:, k], [("sb", k)], [("lu", t + 1, k)], 128)
            tt(T.eqc[:], B0, B1, A.is_equal, hk("tm"), ["eqc"], 64)
            lin(T.eqs[:], T.eqc[:], ["eqc"], ["eqs"], 64, scale=-16384.0)
            tt(T.mc[:], p[:, 0:64], T.mc[:], A.add, [pk], ["mc"], 64, 1.0)
        if t == 1:
            tt(Fq(0, 64), T.nd[:], T.mc[:], A.mult, ["nd", "mc"], [("f", 0)], 64)
            tt(Fq(1, 64), T.nat[:, 0:64], Fq(0, 64), A.add, ["nat", ("f", 0)], [("f", 1)], 64)
            tt(Fq(2, 64), T.nat[:, 64:128], Fq(0, 64), A.subtract, ["nat", ("f", 0)], [("f", 2)], 64)
        if t == 2:
            tt(Fq(3, 64), p[:, 0:64], T.nd[:], A.mult, [pk, "nd"], [("f", 3)], 64, 1.0)

    def finish():
        L = [TM[h][:, 17:32:2, :] for h in range(2)]
        tt(T.lm[:], L[0], L[1], A.max, hk("tm"), ["lm"], 64)
        tt(T.eqc[:], T.lm[:], T.tmm[:, 1:16:2, :], A.mult, ["lm", "tmm"], ["eqc"], 64)
        for h in range(2):
            tt(T.til[:, 8 + h:128:16, :], L[h], T.eqc[:], A.max, [("tm", h), "eqc"], [("til", h)], 64)
        for q in range(4):
            p, pk = bank()
            mms([(p[:, 2 * i + h:512:16], T.til[:, h:128 + h, i], T.idh[:, 32 * q:32 * q + 32], True, True) for i in range(8) for h in range(2)],
                hk("til") + ["til0", "idh"], [pk], 1024)
            lin(T.kw[:, Q(q)], p[:], [pk], [("kw", q)], 512, scale=1.0 / 2048, bias=2048.0)
        p, pk = bank()
        for h in range(2):
            to_list(p[:, 64 * h:64 * h + 64], pk, TM[h], ("tm", h), T.st2, "st2", 64, 512)
        tt(I(0), p[:, 0:128], T.own[:], A.max, [pk, "own"], [("i", 0)], 128, 1.0)
        ts(I(1), I(0), 2047, None, A.bitwise_and, None, [("i", 0)], [("i", 1)], 128)
        cp(T.ll[:], I(1), [("i", 1)], ["ll"], 128)
        for b in range(2):
            for h in range(2):
                lin(T.yl[:, 1024 * b + h:1024 * b + 1024:2], T.kw[:, 0:2048].indirect(T.ll[:, 64 * h + 32 * b:64 * h + 32 * b + 32]),
                    qk("kw") + ["ll"], [("yo", b, h)], 512, GR)
            dma("y", T.ylab[:, H(b)], T.yl[8:128:16, H(b)], [("yo", b, 0), ("yo", b, 1)], [("ylab", b)])
        p, pk = bank()
        mms([(p[0:64, h:256:2], Fq([1 + h, 3][j], 64), (T.idm if j * h else T.idf)[:], j == 0, j == 1) for h in range(2) for j in range(2)],
            [("f", 1), ("f", 2), ("f", 3), "idf", "idm"], [pk], 2048)
        lin(T.osu[0:64, :], p[0:64, 0:256], [pk], ["osu"], 256)
        for q in range(8):
            dma("y", T.ysu[q], T.osu[0:64, 32 * q:32 * q + 32], ["osu"], [("ysu", q)], 1.0)

    for t in range(3):
        K = 3 + t
        doubling(t)
        gains(t)
        if RIDE[t]:
            for k in range(1, K + 1):
                bstep(t, k)
                astep(t, k)
        else:
            for k in range(1, K + 1):
                astep(t, k)
            for k in range(1, K + 1):
                bstep(t, k)
        merge(t)
    finish()
    return ops


def is_psum(k):
    return k[0] == "ps"


def plan_deps(ops):
    last_w, readers = {}, {}
    for i, o in enumerate(ops):
        hard, soft = set(), set()
        for k in set(o["r"] + o["w"]):
            if k in last_w:
                hard.add(last_w[k])
            if k in o["w"]:
                hard.update(readers.get(k, []))
            elif is_psum(k) and readers.get(k) and "p" not in o["alt"]:
                soft.add(readers[k][-1])
        o["d"], o["soft"] = hard | soft, soft - hard
        for k in o["r"]:
            readers.setdefault(k, []).append(i)
        for k in o["w"]:
            last_w[k] = i
            readers[k] = []
    return ops


def place(ops, order, before, bias, keep=None):
    busy = {e: [] for e in "vspgy"}
    res = {}
    for i in order:
        o = ops[i]
        pre, post = (0.0, o["lat"]) if before == "d" else (o["lat"], 0.0)
        ready = max([res[j][0] + WAKE for j in o[before]] or [0.0]) + pre
        best = (ready, ready, "a")
        for m, (e, (fn, d)) in enumerate(sorted(a for a in o["alt"].items() if keep is None or a[0] == keep[i][2])):
            s = ready
            for a, b in busy[e]:
                if s + d <= a:
                    break
                s = max(s, b)
            if m == 0 or s + d + bias * d < best[0]:
                best = (s + d, s, e)
        res[i] = (best[0] + post, best[1], best[2])
        if best[2] != "a":
            busy[best[2]].append((best[1], best[0]))
            busy[best[2]].sort()
    return res


def link(ops, extra):
    for i, j in extra:
        ops[i]["d"].add(j)
        ops[i]["soft"].discard(j)
    for o in ops:
        o["u"] = []
    for i, o in enumerate(ops):
        for j in o["d"]:
            ops[j]["u"].append(i)


def passes(ops, order):
    n, best = len(ops), None
    for bias in OPT["bias"]:
        now = order
        for k in range(OPT["passes"]):
            res = place(ops, now, "d", bias)
            span = max(r[0] for r in res.values())
            if best is None or span < best[0]:
                best = (span, res)
            back = place(ops, sorted(range(n), key=lambda j: (-res[j][0], -res[j][1], -j)), "u", bias)
            now = sorted(range(n), key=lambda j: (-back[j][0], -back[j][1], j))
    return best[1]


def improve(ops, res, steps):
    n = len(ops)
    pre, suc, lag = [list(o["d"]) for o in ops], [o["u"] for o in ops], [o["lat"] + WAKE for o in ops]
    eng, dur, seq = [0] * n, [0.0] * n, {}

    def take(plan):
        for i in range(n):
            eng[i] = plan[i][2]
            dur[i] = ops[i]["alt"][eng[i]][1] if ops[i]["alt"] else 0.0
        for e in "vspgy":
            seq[e] = sorted((i for i in range(n) if eng[i] == e), key=lambda i: (plan[i][1], i))

    def times():
        mp, mn, hd, r, tl, q = [-1] * n, [-1] * n, [0.0] * n, [0.0] * n, [0.0] * n, [0.0] * n
        for l in seq.values():
            for a, b in zip(l, l[1:]):
                mn[a], mp[b] = b, a
        left = [len(pre[i]) + (mp[i] >= 0) for i in range(n)]
        order = [i for i in range(n) if left[i] == 0]
        for i in order:
            r[i] = hd[i] if mp[i] < 0 else max(hd[i], r[mp[i]] + dur[mp[i]])
            e = r[i] + dur[i] + lag[i]
            for s in suc[i]:
                if e > hd[s]:
                    hd[s] = e
            for s in suc[i] + [mn[i]][0:mn[i] >= 0]:
                left[s] -= 1
                if left[s] == 0:
                    order.append(s)
        for i in reversed(order):
            tl[i] = max([lag[i] + q[s] for s in suc[i]] or [lag[i] - WAKE])
            q[i] = dur[i] + (tl[i] if mn[i] < 0 else max(tl[i], q[mn[i]]))
        return r, q, hd, tl, mp, mn

    def through(seg, a, b, u, d):
        t, heads, best = (r[a] + dur[a] if a >= 0 else 0.0), [], 0.0
        for x in seg:
            heads.append(max(t, hd[x]))
            t = heads[-1] + (d if x == u else dur[x])
        t = q[b] if b >= 0 else 0.0
        for x, h in zip(reversed(seg), reversed(heads)):
            t = (d if x == u else dur[x]) + max(t, tl[x])
            best = max(best, h + t)
        return best

    take(res)
    seed, banned, best, since = OPT["seed"], {}, None, 0
    for it in range(steps):
        r, q, hd, tl, mp, mn = times()
        span = max(r[i] + q[i] for i in range(n))
        if best is None or span < best[0] - 1e-9:
            best, since = (span, {i: (r[i] + dur[i] + lag[i] - WAKE, r[i], eng[i]) for i in range(n)}), it
        if it - since > OPT["back"]:
            since = it
            take(best[1])
            continue
        on = set(i for i in range(n) if r[i] + q[i] > span - 1e-6 and eng[i] != "a")
        moves = []
        for u in on:
            l = seq[eng[u]]
            j = k = l.index(u)
            while j + 1 < len(l) and j - k < 6 and l[j + 1] in on and r[l[j + 1]] < r[l[j]] + dur[l[j]] + 1e-6:
                j += 1
                if any(q[s] > q[l[j]] or s == l[j] for s in suc[u]):
                    break
                moves.append((through(l[k + 1:j + 1] + [u], mp[u], mn[l[j]], u, dur[u]), u, eng[u], j))
            j = k
            while j > 0 and k - j < 6 and l[j - 1] in on and r[l[j]] < r[l[j - 1]] + dur[l[j - 1]] + 1e-6:
                j -= 1
                if any(r[p] >= r[l[j]] + dur[l[j]] or p == l[j] for p in pre[u]):
                    break
                moves.append((through([u] + l[j:k], mp[l[j]], mn[u], u, dur[u]), u, eng[u], j))
            for e in ops[u]["alt"]:
                m = seq[e]
                for j in range(len(m) + 1 if e != eng[u] else 0):
                    a, b = (m[j - 1] if j > 0 else -1), (m[j] if j < len(m) else -1)
                    if b >= 0 and r[b] + dur[b] <= hd[u]:
                        continue
                    if a >= 0 and q[a] <= tl[u] + dur[a]:
                        break
                    moves.append((through([u], a, b, u, ops[u]["alt"][e][1]), u, e, j))
        if not moves:
            break
        seed = (seed * 1103515245 + 12345) % 2147483648
        ok = [m for m in moves if banned.get(m[1], -1) < it or m[0] < best[0] - 1e-6] or moves
        low = min(ok)[0] + OPT["near"]
        ok = sorted(m for m in ok if m[0] <= low)
        est, u, e, j = ok[(seed >> 8) % len(ok)]
        banned[u] = it + 15 + seed % 15
        seq[eng[u]].remove(u)
        seq[e].insert(j, u)
        eng[u], dur[u] = e, ops[u]["alt"][e][1]
    return best[1]


def give_banks(ops, res):
    uses = {}
    for i, o in enumerate(ops):
        for k in o["r"] + o["w"]:
            if is_psum(k):
                uses.setdefault(k[1], []).append(i)
    free, last, banks, extra = [0.0] * 8, [[] for b in range(8)], {}, []
    for u in sorted(uses, key=lambda u: (res[uses[u][0]][1], u)):
        start = res[uses[u][0]][1]
        b = min(range(8), key=lambda b: (max(free[b], start - 1.0), -min(free[b ^ 1], start), b))
        extra += [(uses[u][0], j) for j in last[b]]
        banks[u], last[b], free[b] = b, uses[u], max(res[i][0] for i in uses[u])
    return banks, extra


def schedule(g, core, T, topo, rank):
    if repr(OPT) not in PLAN:
        ops = plan_deps(build(g, core, T, topo, rank, {}))
        link(ops, [])
        n = len(ops)
        path = [0.0] * n
        for i in range(n - 1, -1, -1):
            o = ops[i]
            path[i] = min([a[1] for a in o["alt"].values()] or [0.0]) + o["lat"] + WAKE + max([path[j] for j in o["u"]] or [0.0])
        res = passes(ops, sorted(range(n), key=lambda j: (-path[j], j)))
        best = None
        for k in range(OPT["rounds"]):
            banks, extra = give_banks(ops, res)
            ops = plan_deps(ops)
            link(ops, extra)
            res = passes(ops, topological(ops, res)) if k == 0 else place(ops, topological(ops, res), "d", 0.0, res)
            res = improve(ops, res, OPT["steps"])
            span = max(r[0] for r in res.values())
            if best is None or span < best[0]:
                best = (span, banks, extra, res)
        PLAN[repr(OPT)] = best[1:]
    banks, extra, res = PLAN[repr(OPT)]
    ops = plan_deps(build(g, core, T, topo, rank, banks))
    link(ops, extra)
    for i, o in enumerate(ops):
        o["end"], o["start"], o["e"] = res[i]
    return ops, sorted(range(len(ops)), key=lambda j: (ops[j]["start"], j))


def topological(ops, res):
    done, order = set(), []

    def visit(i):
        if i not in done:
            done.add(i)
            for j in sorted(ops[i]["d"], key=lambda j: res[j][1]):
                visit(j)
            order.append(i)

    for i in sorted(range(len(ops)), key=lambda j: (res[j][1], j)):
        visit(i)
    return order


def rank_program(g, core, T, topo):
    rank = T.rank_of(core)
    if rank is None:
        return
    ops, order = schedule(g, core, T, topo, rank)
    Q = {"v": g.vector, "s": g.scalar, "p": g.tensor, "g": g, "y": g.sync}
    CS = {"v": "nv", "s": "ns", "p": "nt", "g": "ng"}
    pos = {i: n for n, i in enumerate(order)}
    pool = [i for i in order if ops[i]["e"] == "g" and ops[i]["k"] == "c"]
    for a, b in zip(pool, pool[1:]):
        ops[b]["d"].add(a)

    def needs(i, j):
        a, b = ops[i], ops[j]
        return not (b["k"] == "r" or (a["e"] == b["e"] and (a["e"] == "p" or j in a["soft"])))

    want, seen = {}, {}
    for i in order:
        o = ops[i]
        if o["k"] == "a":
            continue
        best, w = {}, []
        for j in sorted(o["d"]):
            if not needs(i, j):
                continue
            b = ops[j]
            if b["k"] == "c":
                if b["e"] not in best or pos[j] > pos[best[b["e"]]]:
                    best[b["e"]] = j
            elif (o["e"], j) not in seen:
                seen[(o["e"], j)] = True
                w.append(j)
        for e, j in best.items():
            if pos[j] > seen.get((o["e"], e), -1):
                seen[(o["e"], e)] = pos[j]
                w.append(j)
        want[i] = w
    waited = set(j for w in want.values() for j in w)
    count = {e: 0 for e in CS}
    nd = 0
    for i in order:
        o = ops[i]
        if o["k"] == "c" and i in waited:
            count[o["e"]] += 1
            o["sv"] = (CS[o["e"]], count[o["e"]])
        elif o["k"] == "d":
            o["sv"] = ("d%d" % nd, 16)
            nd += 1
    sent = 0
    for i in order:
        o = ops[i]
        if o["k"] == "a":
            continue
        q = Q[o["e"]]
        for j in want[i]:
            q.wait_ge(T.sem[ops[j]["sv"][0]], ops[j]["sv"][1])
        ins = o["alt"][o["e"]][0]()
        if o["k"] == "r":
            sent += o["n"]
        elif "sv" in o:
            ins.then_inc(T.sem[o["sv"][0]], 16 if o["k"] == "d" else 1)
    g.wait_ge(T.sem.sent, sent)
    for i in order:
        if ops[i]["k"] == "d" and i not in waited:
            g.sync.wait_ge(T.sem[ops[i]["sv"][0]], 16)
